import numpy as np
import ml_dtypes


def mxq(x, axis, fmt="e4m3"):
    dtype, down = {"e4m3": (ml_dtypes.float8_e4m3fn, 7), "e5m2": (ml_dtypes.float8_e5m2, 14)}[fmt]
    v = np.moveaxis(np.asarray(x, np.float32).astype(ml_dtypes.bfloat16).astype(np.float64), axis, -1)
    blocks = v.reshape(v.shape[:-1] + (-1, 32))
    amax = np.abs(blocks).max(-1, keepdims=True)
    byte = np.maximum(np.where(amax > 0, np.frexp(amax)[1] - 1 + 127, 0) - down, 1)
    scale = np.exp2(byte - 127.0)
    codes = (blocks / scale).astype(np.float32).astype(dtype).astype(np.float64)
    return np.moveaxis((codes * scale).reshape(v.shape), -1, axis)


WIDE = False


def mx_kscale(k):
    if not WIDE:
        return np.ones(k)
    levels = np.array([10, -10, 5, -5, 0])
    if k % 512:
        return np.exp2(np.random.permutation(np.resize(levels, k // 32))).repeat(32)
    a = np.empty((k // 512, 16))
    for p in range(k // 512):
        a[p, :8] = np.random.permutation(np.resize(levels, 8))
        for g in range(8):
            far = levels[np.abs(levels - a[p, g]) >= 10]
            a[p, g + 8] = far[np.random.randint(len(far))]
    return np.exp2(a.ravel()).repeat(32)


def f64(x):
    return np.asarray(x).astype(np.float64)


def striped(idx):
    return np.tile(idx.reshape(-1, 16).T, (8, 1)).astype(np.uint16)


def unstriped(offs):
    return offs[:16].T.reshape(-1).astype(np.int64)


def pack_weight(w):
    k, n = w.shape
    w = f64(np.asarray(w, np.float32).astype(ml_dtypes.bfloat16)).reshape(k // 32, 32, n)
    amax = np.abs(w).max(1)
    byte = np.clip(np.where(amax > 0, np.frexp(amax)[1] - 1 + 127 - 7, 1), 1, 254)
    scaled = (w * np.exp2(127.0 - byte)[:, None, :]).reshape(k, n).astype(np.float32)
    words = np.ascontiguousarray(scaled.reshape(k // 512, 128, 4, n).transpose(0, 1, 3, 2)).astype(ml_dtypes.float8_e4m3fn).view(np.uint8)
    return words, np.ascontiguousarray(byte.astype(np.uint8).reshape(k // 512, 16, n))


def unpack_weight(words, scales):
    g, p, n, _ = words.shape
    vals = np.ascontiguousarray(words).view(ml_dtypes.float8_e4m3fn).astype(np.float64) * np.repeat(np.exp2(scales.astype(np.float64) - 127.0), 8, axis=1)[..., None]
    return vals.transpose(0, 1, 3, 2).reshape(g * 512, n)


def planes(y):
    n, m = y.shape
    v = y.astype(np.float32).astype(ml_dtypes.bfloat16).astype(np.float64).reshape(n // 32, 32, m)
    top = np.abs(v).max(1)
    byte = np.clip(np.where(top > 0, np.frexp(top)[1] - 1 + 127 - 7, 1), 1, 254)
    codes = (v * np.exp2(127.0 - byte)[:, None, :]).reshape(n, m).astype(np.float32).astype(ml_dtypes.float8_e4m3fn).view(np.uint8)
    words = codes.reshape(n // 512, 128, 4, m).transpose(0, 1, 3, 2)
    return np.ascontiguousarray(words), np.ascontiguousarray(byte.astype(np.uint8).reshape(n // 512, 16, m))


def relu(v):
    return np.maximum(v, 0.0)


K, T, S, V, H, N = 512, 2048, 512, 256, 512, 512


def setup_inputs():
    n = np.random.standard_normal
    s = mx_kscale(K)[:, None]
    u = mx_kscale(H)
    near = np.random.permutation(S)
    packed_xT = pack_weight(n((K, T)) * s)
    packed_w2 = pack_weight(n((H, N)) / np.sqrt(H) / u[:, None])
    packed_w3 = pack_weight(n((H, N)) / np.sqrt(H) / u[:, None])
    return {
        "x_words": packed_xT[0],
        "x_scales": packed_xT[1],
        "w1": (n((K, H)) / np.sqrt(K) / s * u).astype(np.float32),
        "w2_words": packed_w2[0],
        "w2_scales": packed_w2[1],
        "w3_words": packed_w3[0],
        "w3_scales": packed_w3[1],
        "offs": striped(np.random.permutation(T)[:S]),
        "pos1": striped(near[:V]),
        "pos2": striped(near[V:]),
        "pos3": striped(np.random.permutation(S)[:V]),
    }


def reference(x_words, x_scales, w1, w2_words, w2_scales, w3_words, w3_scales, offs, pos1, pos2, pos3):
    xq = unpack_weight(x_words, x_scales)[:, unstriped(offs)]
    h = relu(mxq(f64(w1), 0, "e4m3").T @ xq)
    hq = mxq(h, 0, "e4m3")
    y = unpack_weight(w3_words, w3_scales).T @ hq
    e = np.exp(unpack_weight(w2_words, w2_scales).T @ hq)
    e0 = e[:, unstriped(pos1)]
    e1 = e[:, unstriped(pos2)]
    e2 = e[:, unstriped(pos3)]
    num = y[:, unstriped(pos1)] * e0 + y[:, unstriped(pos2)] * e1 + y[:, unstriped(pos3)] * e2
    den = e0 + e1 + e2
    out_0 = num / den
    return (out_0,) + planes(out_0)

@@ -1,0 +1,219 @@
+from contextlib import ExitStack
+
+import concourse.mybir as mybir
+
+K, T, S, V, H, N = 512, 2048, 512, 256, 512, 512
+FLOPS = 2 * S * (K * H + 2 * H * N)
+
+F32 = mybir.dt.float32
+BF16 = mybir.dt.bfloat16
+I32 = mybir.dt.int32
+U32 = mybir.dt.uint32
+U16 = mybir.dt.uint16
+U8 = mybir.dt.uint8
+FP8X4 = mybir.dt.float8_e4m3fn_x4
+ACT = mybir.ActivationFunctionType
+ALU = mybir.AluOpType
+
+P = 128
+PACK = 4
+QUAD = 32
+LANES = 16
+
+
+def load_scale_rows(queues, tile, scales):
+    for q, queue in enumerate(queues):
+        row = QUAD * q
+        queue.dma_start(out=tile[row : row + PACK, :].bitcast(I32), in_=scales[0, PACK * q : PACK * (q + 1), :].bitcast(I32))
+
+
+def words_of(packed):
+    return packed[0].rearrange("p c r -> p (c r)").bitcast(I32)
+
+
+def tile_picked_zrandla_relu_po_kernel(
+    tc, x_words, x_scales, w1, w2_words, w2_scales, w3_words, w3_scales, offs, pos1, pos2, pos3, out_0, out_1, out_2
+):
+    nc = tc.nc
+    with ExitStack() as ctx:
+        lists = ctx.enter_context(tc.tile_pool(name="lists", bufs=1))
+        keep = ctx.enter_context(tc.tile_pool(name="keep", bufs=1))
+        psum = ctx.enter_context(tc.psum_pool(name="psum", bufs=1))
+
+        picks = lists.tile([P, S // LANES], U16, name="picks")
+        near = [lists.tile([P, V // LANES], U16, name=f"near{d}") for d in range(3)]
+
+        x_scale_table = keep.tile([P, T], U8, name="x_scale_table", align_bytes=64)
+        w2_scale_rows = keep.tile([P, N], U8, name="w2_scale_rows", align_bytes=64)
+        w3_scale_rows = keep.tile([P, N], U8, name="w3_scale_rows", align_bytes=64)
+        nc.vector.memset(x_scale_table[:].bitcast(I32), 0)
+
+        half_cols = H // 2
+        w1_rows = [keep.tile([P, PACK, half_cols], F32, name=f"w1_rows{a}", tag=f"stage{a}", align_bytes=64) for a in range(2)]
+        x_table = keep.tile([P, T], I32, name="x_table", tag="table", align_bytes=64)
+        nc.sync.dma_start(picks[:], offs)
+        nc.sync.dma_start(out=x_table[:], in_=words_of(x_words))
+        load_scale_rows([nc.scalar] * 4, x_scale_table, x_scales)
+        w1_view = w1.rearrange("(p j) c -> p j c", j=PACK)
+        for a in range(2):
+            nc.sync.dma_start(out=w1_rows[a][:], in_=w1_view[:, :, a * half_cols : (a + 1) * half_cols])
+        for tile, source in zip(near, (pos1, pos2, pos3)):
+            nc.sync.dma_start(tile[:], source)
+        nc.gpsimd.memset(w2_scale_rows[:].bitcast(I32), 0)
+        load_scale_rows([nc.gpsimd] * 4, w2_scale_rows, w2_scales)
+        nc.gpsimd.memset(w3_scale_rows[:].bitcast(I32), 0)
+
+        x_code = keep.tile([P, S], U32, name="x_code", align_bytes=64)
+        nc.vector.tensor_copy(x_code[:], x_table[:].bitcast(U32).indirect(picks[:]))
+        w2_rows = keep.tile([P, N], I32, name="w2_rows", tag="table", align_bytes=64)
+        nc.sync.dma_start(out=w2_rows[:], in_=words_of(w2_words))
+        load_scale_rows([nc.sync] * 4, w3_scale_rows, w3_scales)
+        x_scale = keep.tile([P, S], U8, name="x_scale", align_bytes=64)
+
+        def pick_scales(a):
+            half = S // 2
+            nc.vector.tensor_copy(
+                x_scale[:, a * half : (a + 1) * half],
+                x_scale_table[:].indirect(picks[:, a * half // LANES : (a + 1) * half // LANES]),
+            )
+
+        w1_code = keep.tile([P, H], U32, name="w1_code", align_bytes=64)
+        w1_scale = keep.tile([P, H], U8, name="w1_scale", align_bytes=64)
+        half_m = P // 2
+        for a, split in enumerate((32, 24)):
+            w1_bf = keep.tile([P, PACK, half_m, PACK], BF16, name=f"w1_bf{a}", align_bytes=64)
+            w1_src = w1_rows[a][:].rearrange("p j (m t) -> p m j t", t=PACK)
+            w1_dst = w1_bf[:].rearrange("p t m j -> p m j t")
+            nc.vector.tensor_copy(out=w1_dst[:, :split], in_=w1_src[:, :split])
+            nc.scalar.copy(out=w1_dst[:, split:], in_=w1_src[:, split:])
+            for t in range(PACK):
+                cols = slice(t * P + a * half_m, t * P + (a + 1) * half_m)
+                nc.vector.quantize_mx(
+                    out=w1_code[:, cols].bitcast(FP8X4), scales=w1_scale[:, cols], in_=w1_bf[:, t].rearrange("p m j -> p (m j)")
+                )
+            pick_scales(a)
+        w3_rows = keep.tile([P, N], I32, name="w3_rows", tag="stage0", align_bytes=64)
+        nc.sync.dma_start(out=w3_rows[:], in_=words_of(w3_words))
+
+        h_code = keep.tile([P, S], U32, name="h_code", align_bytes=64)
+        h_scale = keep.tile([P, S], U8, name="h_scale", align_bytes=64)
+        w2_code = keep.tile([P, N], I32, name="w2_code", align_bytes=64)
+        w3_code = keep.tile([P, N], I32, name="w3_code", align_bytes=64)
+        w2_scale = keep.tile([P, N], U8, name="w2_scale", align_bytes=64)
+        w3_scale = keep.tile([P, N], U8, name="w3_scale", align_bytes=64)
+        deals = [(w2_scale, w2_scale_rows), (w2_code, w2_rows), (w3_code, w3_rows), (w3_scale, w3_scale_rows)]
+        for q in range(4):
+            cols = slice(q * P, (q + 1) * P)
+            h_sum = psum.tile([P, PACK, P], F32, name=f"h_sum{q}", tag=f"bank{q}")
+            for t in range(PACK):
+                w_cols = slice(t * P, (t + 1) * P)
+                nc.tensor.matmul_mx(
+                    out=h_sum[:, t, :],
+                    lhsT=w1_code[:, w_cols].bitcast(FP8X4),
+                    lhsT_scale=w1_scale[:, w_cols],
+                    rhs=x_code[:, cols].bitcast(FP8X4),
+                    rhs_scale=x_scale[:, cols],
+                    start=True,
+                    stop=True,
+                )
+            h_bf = keep.tile([P, P, PACK], BF16, name=f"h_bf{q}", align_bytes=64)
+            nc.scalar.activation(out=h_bf[:], in_=h_sum[:].rearrange("p t n -> p n t"), func=ACT.Relu)
+            if q < len(deals):
+                dealt, rows = deals[q]
+                nc.vector.tensor_copy(
+                    out=dealt[:].rearrange("p (t m) -> p t m", t=PACK), in_=rows[:].rearrange("p (m t) -> p t m", t=PACK)
+                )
+            nc.vector.quantize_mx(out=h_code[:, cols].bitcast(FP8X4), scales=h_scale[:, cols], in_=h_bf[:].rearrange("p n t -> p (n t)"))
+
+        score = []
+        weighted = []
+        feature = []
+        for t in range(PACK):
+            w_cols = slice(t * P, (t + 1) * P)
+
+            def product(total, code, scale, cols):
+                nc.tensor.matmul_mx(
+                    out=total,
+                    lhsT=code[:, w_cols].bitcast(FP8X4),
+                    lhsT_scale=scale[:, w_cols],
+                    rhs=h_code[:, cols].bitcast(FP8X4),
+                    rhs_scale=h_scale[:, cols],
+                    start=True,
+                    stop=True,
+                )
+
+            e = keep.tile([P, S], F32, name=f"score{t}", align_bytes=64)
+            if t == 0:
+                s_head = psum.tile([P, S], F32, name="s_head", tag="bank7")
+                product(s_head[:, 0:256], w2_code, w2_scale, slice(0, 256))
+                product(s_head[:, 256:384], w2_code, w2_scale, slice(256, 384))
+                nc.scalar.activation(out=e[:, 0:384], in_=s_head[:, 0:384], func=ACT.Exp)
+                s_sum = psum.tile([P, S], F32, name=f"s_sum{t}", tag=f"bank{t}")
+                product(s_sum[:, 0:128], w2_code, w2_scale, slice(384, 512))
+                nc.scalar.activation(out=e[:, 384:512], in_=s_sum[:, 0:128], func=ACT.Exp)
+            else:
+                s_sum = psum.tile([P, S], F32, name=f"s_sum{t}", tag=f"bank{t}")
+                product(s_sum[:], w2_code, w2_scale, slice(0, S))
+                nc.scalar.activation(out=e[:], in_=s_sum[:], func=ACT.Exp)
+            y_sum = psum.tile([P, S], F32, name=f"y_sum{t}", tag=f"bank{PACK + t}")
+            product(y_sum[:], w3_code, w3_scale, slice(0, S))
+            score.append(e)
+            feature.append(y_sum)
+            weighted.append(keep.tile([P, S], F32, name=f"weighted{t}", align_bytes=64))
+
+        result = keep.tile([P, PACK, V], F32, name="result", align_bytes=64)
+        result_bf = keep.tile([P, V, PACK], BF16, name="result_bf", align_bytes=64)
+        out_rows = out_0.rearrange("(p t) v -> p t v", t=PACK)
+
+        def gather_steps(window, label):
+            sums = [keep.tile([P, V], F32, name=f"{label}_{d}", align_bytes=64) for d in range(3)]
+            steps = [lambda: nc.vector.tensor_copy(sums[0][:], window[:].indirect(near[0][:]))]
+            for d in (1, 2):
+                steps.append(lambda d=d: nc.vector.tensor_tensor(sums[d][:], window[:].indirect(near[d][:]), sums[d - 1][:], ALU.add))
+            return steps, sums[2]
+
+        def weigh(t):
+            nc.vector.tensor_tensor(weighted[t][:], feature[t][:], score[t][:], ALU.mult)
+
+        def invert(t, den):
+            root = keep.tile([P, V], F32, name=f"root{t}", align_bytes=64)
+            inv = keep.tile([P, V], F32, name=f"inv{t}", align_bytes=64)
+            nc.scalar.activation(out=root[:], in_=den[:], func=ACT.Abs_reciprocal_sqrt)
+            nc.scalar.activation(out=inv[:], in_=root[:], func=ACT.Square)
+            return inv
+
+        den_steps, den = gather_steps(score[0], "den0")
+        den_steps[0]()
+        weigh(0)
+        den_steps[1]()
+        weigh(1)
+        den_steps[2]()
+        inv = invert(0, den)
+        for t in range(PACK):
+            num_steps, num = gather_steps(weighted[t], f"num{t}")
+            if t + 1 < PACK:
+                den_steps, den = gather_steps(score[t + 1], f"den{t + 1}")
+                for d in range(3):
+                    num_steps[d]()
+                    den_steps[d]()
+                if t + 2 < PACK:
+                    weigh(t + 2)
+                next_inv = invert(t + 1, den)
+            else:
+                for d in range(3):
+                    num_steps[d]()
+            nc.vector.tensor_tensor(result[:, t, :], num[:], inv[:], ALU.mult)
+            nc.sync.dma_start(out=out_rows[:, t, :], in_=result[:, t, :])
+            inv = next_inv
+            if t == 1:
+                nc.scalar.copy(out=result_bf[:, :, 0:2], in_=result[:, 0:2, :].rearrange("p t v -> p v t"))
+        nc.vector.tensor_copy(out=result_bf[:, :, 2:4], in_=result[:, 2:4, :].rearrange("p t v -> p v t"))
+        out_code = keep.tile([P, V], U32, name="out_code", align_bytes=64)
+        out_scale = keep.tile([P, V], U8, name="out_scale", align_bytes=64)
+        nc.vector.quantize_mx(out=out_code[:].bitcast(FP8X4), scales=out_scale[:], in_=result_bf[:].rearrange("p v t -> p (v t)"))
+        nc.sync.dma_start(out=words_of(out_1), in_=out_code[:].bitcast(I32))
+        for q in range(P // QUAD):
+            queue = nc.sync if q % 2 else nc.scalar
+            queue.dma_start(
+                out=out_2[0, PACK * q : PACK * (q + 1), :].bitcast(I32), in_=out_scale[QUAD * q : QUAD * q + PACK, :].bitcast(I32)
+            )

@@ -1,6 +1,7 @@
 from contextlib import ExitStack
 
 import concourse.mybir as mybir
+from concourse.masks import make_identity
 
 K, T, S, V, H, N = 512, 2048, 512, 256, 512, 512
 FLOPS = 2 * S * (K * H + 2 * H * N)
@@ -43,65 +44,64 @@ def tile_picked_zrandla_relu_po_kernel(
         picks = lists.tile([P, S // LANES], U16, name="picks")
         near = [lists.tile([P, V // LANES], U16, name=f"near{d}") for d in range(3)]
 
-        x_scale_table = keep.tile([P, T], U8, name="x_scale_table", align_bytes=64)
+        x_scale_table = keep.tile([P, T], U8, name="x_scale_table", tag="slot_a", align_bytes=64)
         w2_scale_rows = keep.tile([P, N], U8, name="w2_scale_rows", align_bytes=64)
         w3_scale_rows = keep.tile([P, N], U8, name="w3_scale_rows", align_bytes=64)
         nc.vector.memset(x_scale_table[:].bitcast(I32), 0)
 
-        half_cols = H // 2
-        w1_rows = [keep.tile([P, PACK, half_cols], F32, name=f"w1_rows{a}", tag=f"stage{a}", align_bytes=64) for a in range(2)]
-        x_table = keep.tile([P, T], I32, name="x_table", tag="table", align_bytes=64)
+        w1_rows = keep.tile([P, PACK, H], F32, name="w1_rows", tag="slot_w1", align_bytes=64)
+        x_table = keep.tile([P, T], I32, name="x_table", tag="slot_x", align_bytes=64)
+        x_scale_rows = keep.tile([P, T], U8, name="x_scale_rows", tag="slot_b", align_bytes=64)
         nc.sync.dma_start(picks[:], offs)
+        load_scale_rows([nc.scalar, nc.scalar, nc.sync, nc.sync], x_scale_rows, x_scales)
+        nc.sync.dma_start(out=w1_rows[:], in_=w1.rearrange("(p j) c -> p j c", j=PACK))
         nc.sync.dma_start(out=x_table[:], in_=words_of(x_words))
-        load_scale_rows([nc.scalar] * 4, x_scale_table, x_scales)
-        w1_view = w1.rearrange("(p j) c -> p j c", j=PACK)
-        for a in range(2):
-            nc.sync.dma_start(out=w1_rows[a][:], in_=w1_view[:, :, a * half_cols : (a + 1) * half_cols])
         for tile, source in zip(near, (pos1, pos2, pos3)):
             nc.sync.dma_start(tile[:], source)
         nc.gpsimd.memset(w2_scale_rows[:].bitcast(I32), 0)
         load_scale_rows([nc.gpsimd] * 4, w2_scale_rows, w2_scales)
         nc.gpsimd.memset(w3_scale_rows[:].bitcast(I32), 0)
 
-        x_code = keep.tile([P, S], U32, name="x_code", align_bytes=64)
-        nc.vector.tensor_copy(x_code[:], x_table[:].bitcast(U32).indirect(picks[:]))
-        w2_rows = keep.tile([P, N], I32, name="w2_rows", tag="table", align_bytes=64)
-        nc.sync.dma_start(out=w2_rows[:], in_=words_of(w2_words))
-        load_scale_rows([nc.sync] * 4, w3_scale_rows, w3_scales)
+        identity = keep.tile([P, P], F32, name="identity", align_bytes=64)
+        make_identity(nc, identity[:])
+        for q in range(P // QUAD):
+            rows = slice(QUAD * q, QUAD * q + PACK)
+            nc.vector.tensor_copy(out=x_scale_table[rows, :].bitcast(I32), in_=x_scale_rows[rows, :].bitcast(I32))
         x_scale = keep.tile([P, S], U8, name="x_scale", align_bytes=64)
-
-        def pick_scales(a):
-            half = S // 2
-            nc.vector.tensor_copy(
-                x_scale[:, a * half : (a + 1) * half],
-                x_scale_table[:].indirect(picks[:, a * half // LANES : (a + 1) * half // LANES]),
-            )
+        nc.vector.tensor_copy(x_scale[:], x_scale_table[:].indirect(picks[:]))
+        w2_rows = keep.tile([P, N], I32, name="w2_rows", tag="slot_b", align_bytes=64)
+        nc.sync.dma_start(out=w2_rows[:], in_=words_of(w2_words))
 
         w1_code = keep.tile([P, H], U32, name="w1_code", align_bytes=64)
         w1_scale = keep.tile([P, H], U8, name="w1_scale", align_bytes=64)
-        half_m = P // 2
-        for a, split in enumerate((32, 24)):
-            w1_bf = keep.tile([P, PACK, half_m, PACK], BF16, name=f"w1_bf{a}", align_bytes=64)
-            w1_src = w1_rows[a][:].rearrange("p j (m t) -> p m j t", t=PACK)
-            w1_dst = w1_bf[:].rearrange("p t m j -> p m j t")
-            nc.vector.tensor_copy(out=w1_dst[:, :split], in_=w1_src[:, :split])
-            nc.scalar.copy(out=w1_dst[:, split:], in_=w1_src[:, split:])
-            for t in range(PACK):
-                cols = slice(t * P + a * half_m, t * P + (a + 1) * half_m)
-                nc.vector.quantize_mx(
-                    out=w1_code[:, cols].bitcast(FP8X4), scales=w1_scale[:, cols], in_=w1_bf[:, t].rearrange("p m j -> p (m j)")
-                )
-            pick_scales(a)
-        w3_rows = keep.tile([P, N], I32, name="w3_rows", tag="stage0", align_bytes=64)
+        w1_src = w1_rows[:].rearrange("p j (m t) -> p m j t", t=PACK)
+        for a, (copy, tag) in enumerate(((nc.scalar.copy, "slot_c"), (nc.vector.tensor_copy, "slot_a"))):
+            w1_bf = keep.tile([P, 2, P, PACK], BF16, name=f"w1_bf{a}", tag=tag, align_bytes=64)
+            copy(out=w1_bf[:].rearrange("p t m j -> p m j t"), in_=w1_src[:, :, :, 2 * a : 2 * a + 2])
+            cols = slice(2 * a * P, 2 * (a + 1) * P)
+            nc.vector.quantize_mx(
+                out=w1_code[:, cols].bitcast(FP8X4), scales=w1_scale[:, cols], in_=w1_bf[:].rearrange("p t m j -> p (t m j)")
+            )
+        w3_rows = keep.tile([P, N], I32, name="w3_rows", tag="slot_w1", align_bytes=64)
         nc.sync.dma_start(out=w3_rows[:], in_=words_of(w3_words))
+        load_scale_rows([nc.sync] * 4, w3_scale_rows, w3_scales)
+
+        half = S // 2
+        x_code = []
+        for a, tag in enumerate(("slot_a", "slot_c")):
+            picked = keep.tile([P, half], U32, name=f"x_code{a}", tag=tag, align_bytes=64)
+            nc.vector.tensor_copy(picked[:], x_table[:].bitcast(U32).indirect(picks[:, a * half // LANES : (a + 1) * half // LANES]))
+            x_code.append(picked)
+
+        def deal(rows, dtype, name, tag):
+            dealt = keep.tile([P, N], dtype, name=name, tag=tag, align_bytes=64)
+            nc.vector.tensor_copy(out=dealt[:].rearrange("p (t m) -> p t m", t=PACK), in_=rows[:].rearrange("p (m t) -> p t m", t=PACK))
+            return dealt
+
+        w2_code = deal(w2_rows, I32, "w2_code", "slot_x")
 
         h_code = keep.tile([P, S], U32, name="h_code", align_bytes=64)
         h_scale = keep.tile([P, S], U8, name="h_scale", align_bytes=64)
-        w2_code = keep.tile([P, N], I32, name="w2_code", align_bytes=64)
-        w3_code = keep.tile([P, N], I32, name="w3_code", align_bytes=64)
-        w2_scale = keep.tile([P, N], U8, name="w2_scale", align_bytes=64)
-        w3_scale = keep.tile([P, N], U8, name="w3_scale", align_bytes=64)
-        deals = [(w2_scale, w2_scale_rows), (w2_code, w2_rows), (w3_code, w3_rows), (w3_scale, w3_scale_rows)]
         for q in range(4):
             cols = slice(q * P, (q + 1) * P)
             h_sum = psum.tile([P, PACK, P], F32, name=f"h_sum{q}", tag=f"bank{q}")
@@ -111,22 +111,22 @@ def tile_picked_zrandla_relu_po_kernel(
                     out=h_sum[:, t, :],
                     lhsT=w1_code[:, w_cols].bitcast(FP8X4),
                     lhsT_scale=w1_scale[:, w_cols],
-                    rhs=x_code[:, cols].bitcast(FP8X4),
+                    rhs=x_code[q // 2][:, (q % 2) * P : (q % 2 + 1) * P].bitcast(FP8X4),
                     rhs_scale=x_scale[:, cols],
                     start=True,
                     stop=True,
                 )
-            h_bf = keep.tile([P, P, PACK], BF16, name=f"h_bf{q}", align_bytes=64)
+            h_bf = keep.tile([P, P, PACK], BF16, name=f"h_bf{q}", tag=f"slot_h{q}", align_bytes=64)
             nc.scalar.activation(out=h_bf[:], in_=h_sum[:].rearrange("p t n -> p n t"), func=ACT.Relu)
-            if q < len(deals):
-                dealt, rows = deals[q]
-                nc.vector.tensor_copy(
-                    out=dealt[:].rearrange("p (t m) -> p t m", t=PACK), in_=rows[:].rearrange("p (m t) -> p t m", t=PACK)
-                )
             nc.vector.quantize_mx(out=h_code[:, cols].bitcast(FP8X4), scales=h_scale[:, cols], in_=h_bf[:].rearrange("p n t -> p (n t)"))
+            if q == 0:
+                w2_scale = deal(w2_scale_rows, U8, "w2_scale", "slot_h0")
+            if q == 2:
+                w3_code = deal(w3_rows, I32, "w3_code", "slot_h2")
+            if q == 3:
+                w3_scale = deal(w3_scale_rows, U8, "w3_scale", "slot_h3")
 
         score = []
-        weighted = []
         feature = []
         for t in range(PACK):
             w_cols = slice(t * P, (t + 1) * P)
@@ -158,59 +158,107 @@ def tile_picked_zrandla_relu_po_kernel(
             y_sum = psum.tile([P, S], F32, name=f"y_sum{t}", tag=f"bank{PACK + t}")
             product(y_sum[:], w3_code, w3_scale, slice(0, S))
             score.append(e)
-            feature.append(y_sum)
-            weighted.append(keep.tile([P, S], F32, name=f"weighted{t}", align_bytes=64))
+            if t < PACK - 1:
+                y = keep.tile([P, S], F32, name=f"feature{t}", align_bytes=64)
+                nc.scalar.copy(out=y[:], in_=y_sum[:])
+                feature.append(y)
 
         result = keep.tile([P, PACK, V], F32, name="result", align_bytes=64)
         result_bf = keep.tile([P, V, PACK], BF16, name="result_bf", align_bytes=64)
         out_rows = out_0.rearrange("(p t) v -> p t v", t=PACK)
 
-        def gather_steps(window, label):
-            sums = [keep.tile([P, V], F32, name=f"{label}_{d}", align_bytes=64) for d in range(3)]
-            steps = [lambda: nc.vector.tensor_copy(sums[0][:], window[:].indirect(near[0][:]))]
-            for d in (1, 2):
-                steps.append(lambda d=d: nc.vector.tensor_tensor(sums[d][:], window[:].indirect(near[d][:]), sums[d - 1][:], ALU.add))
-            return steps, sums[2]
+        halves = V // P
 
-        def weigh(t):
-            nc.vector.tensor_tensor(weighted[t][:], feature[t][:], score[t][:], ALU.mult)
+        def turned_sum(terms, name, bank):
+            total = psum.tile([P, halves, P], F32, name=name, tag=bank)
+            for a in range(halves):
+                for d in range(3):
+                    nc.tensor.matmul(
+                        total[:, a, :], lhsT=terms[d][:, a * P : (a + 1) * P], rhs=identity[:],
+                        is_transpose=True, start=(d == 0), stop=(d == 2),
+                    )
+            return total
 
-        def invert(t, den):
-            root = keep.tile([P, V], F32, name=f"root{t}", align_bytes=64)
-            inv = keep.tile([P, V], F32, name=f"inv{t}", align_bytes=64)
+        def near_tiles(name, first_tag):
+            tags = [first_tag or f"{name}_0", f"{name}_1", f"{name}_2"]
+            return [keep.tile([P, V], F32, name=f"{name}_{d}", tag=tags[d], align_bytes=64) for d in range(3)]
+
+        def fetch_scores(t, first_tag=None):
+            e_near = near_tiles(f"e_near{t}", first_tag)
+            for d in range(3):
+                nc.vector.tensor_copy(e_near[d][:], score[t][:].indirect(near[d][:]))
+            den = turned_sum(e_near, f"den{t}", f"bank{5 + t % 2}")
+            root = keep.tile([P, halves, P], F32, name=f"root{t}", align_bytes=64)
+            inv = keep.tile([P, halves, P], F32, name=f"inv{t}", tag=f"inv{t}", align_bytes=64)
             nc.scalar.activation(out=root[:], in_=den[:], func=ACT.Abs_reciprocal_sqrt)
             nc.scalar.activation(out=inv[:], in_=root[:], func=ACT.Square)
-            return inv
+            return e_near, inv
 
-        den_steps, den = gather_steps(score[0], "den0")
-        den_steps[0]()
-        weigh(0)
-        den_steps[1]()
-        weigh(1)
-        den_steps[2]()
-        inv = invert(0, den)
-        for t in range(PACK):
-            num_steps, num = gather_steps(weighted[t], f"num{t}")
-            if t + 1 < PACK:
-                den_steps, den = gather_steps(score[t + 1], f"den{t + 1}")
-                for d in range(3):
-                    num_steps[d]()
-                    den_steps[d]()
-                if t + 2 < PACK:
-                    weigh(t + 2)
-                next_inv = invert(t + 1, den)
-            else:
-                for d in range(3):
-                    num_steps[d]()
-            nc.vector.tensor_tensor(result[:, t, :], num[:], inv[:], ALU.mult)
+        def fetch_features(t, e_near, first_tag=None):
+            ey_near = near_tiles(f"ey_near{t}", first_tag)
+            for d in range(3):
+                nc.vector.tensor_tensor(ey_near[d][:], feature[t][:].indirect(near[d][:]), e_near[d][:], ALU.mult)
+            return turned_sum(ey_near, f"num{t}", f"bank{2 + t % 2}")
+
+        def finish(t, num, inv):
+            turned = keep.tile([P, halves, P], F32, name=f"turned{t}", align_bytes=64)
+            nc.vector.tensor_tensor(turned[:], num[:], inv[:], ALU.mult)
+            back = psum.tile([P, halves, P], F32, name=f"back{t}", tag=f"bank{(1, 0, 4)[t]}")
+            for a in range(halves):
+                nc.tensor.transpose(back[:, a, :], turned[:, a, :], identity[:])
+            nc.scalar.copy(out=result[:, t, :], in_=back[:].rearrange("p a v -> p (a v)"))
             nc.sync.dma_start(out=out_rows[:, t, :], in_=result[:, t, :])
-            inv = next_inv
             if t == 1:
                 nc.scalar.copy(out=result_bf[:, :, 0:2], in_=result[:, 0:2, :].rearrange("p t v -> p v t"))
-        nc.vector.tensor_copy(out=result_bf[:, :, 2:4], in_=result[:, 2:4, :].rearrange("p t v -> p v t"))
+
+        e0, inv0 = fetch_scores(0)
+        num0 = fetch_features(0, e0)
+        e1, inv1 = fetch_scores(1)
+        num1 = fetch_features(1, e1)
+        e2, inv2 = fetch_scores(2)
+
+        last = PACK - 1
+        weighted = keep.tile([P, S], F32, name="weighted", align_bytes=64)
+
+        def gather_sum(window, d, before, name, tag):
+            total = keep.tile([P, V], F32, name=name, tag=tag, align_bytes=64)
+            if before is None:
+                nc.vector.tensor_copy(total[:], window[:].indirect(near[d][:]))
+            else:
+                nc.vector.tensor_tensor(total[:], window[:].indirect(near[d][:]), before[:], ALU.add)
+            return total
+
+        den = gather_sum(score[last], 0, None, "den_a", "den_a")
+        nc.vector.tensor_tensor(weighted[:], y_sum[:], score[last][:], ALU.mult)
+        den = gather_sum(score[last], 1, den, "den_b", "den_b")
+        finish(0, num0, inv0)
+        den = gather_sum(score[last], 2, den, "den_c", "inv0")
+        root = keep.tile([P, V], F32, name="root3", align_bytes=64)
+        inv = keep.tile([P, V], F32, name="inv3", align_bytes=64)
+        nc.scalar.activation(out=root[:], in_=den[:], func=ACT.Abs_reciprocal_sqrt)
+        nc.scalar.activation(out=inv[:], in_=root[:], func=ACT.Square)
+        num2 = fetch_features(2, e2)
+        finish(1, num1, inv1)
+        num = gather_sum(weighted, 0, None, "num_a", "inv1")
+        finish(2, num2, inv2)
+        num = gather_sum(weighted, 1, num, "num_b", "inv2")
+
         out_code = keep.tile([P, V], U32, name="out_code", align_bytes=64)
         out_scale = keep.tile([P, V], U8, name="out_scale", align_bytes=64)
-        nc.vector.quantize_mx(out=out_code[:].bitcast(FP8X4), scales=out_scale[:], in_=result_bf[:].rearrange("p v t -> p (v t)"))
+        total = keep.tile([P, V], F32, name="num_c", align_bytes=64)
+        parts = [slice(a * P, (a + 1) * P) for a in range(halves)]
+        for a, cols in enumerate(parts):
+            offsets = near[2][:, a * P // LANES : (a + 1) * P // LANES]
+            nc.vector.tensor_tensor(total[:, cols], weighted[:].indirect(offsets), num[:, cols], ALU.add)
+        for cols in parts:
+            nc.vector.tensor_tensor(result[:, last, cols], total[:, cols], inv[:, cols], ALU.mult)
+        nc.sync.dma_start(out=out_rows[:, last, :], in_=result[:, last, :])
+        for cols in parts:
+            nc.vector.tensor_copy(out=result_bf[:, cols, 2:4], in_=result[:, 2:4, cols].rearrange("p t v -> p v t"))
+        for cols in parts:
+            nc.vector.quantize_mx(
+                out=out_code[:, cols].bitcast(FP8X4), scales=out_scale[:, cols], in_=result_bf[:, cols, :].rearrange("p v t -> p (v t)")
+            )
         nc.sync.dma_start(out=words_of(out_1), in_=out_code[:].bitcast(I32))
         for q in range(P // QUAD):
             queue = nc.sync if q % 2 else nc.scalar

@@ -87,15 +87,16 @@ def tile_picked_zrandla_relu_po_kernel(
         load_scale_rows([nc.sync] * 4, w3_scale_rows, w3_scales)
 
         half = S // 2
-        x_code = []
-        for a, tag in enumerate(("slot_a", "slot_c")):
-            picked = keep.tile([P, half], U32, name=f"x_code{a}", tag=tag, align_bytes=64)
-            nc.vector.tensor_copy(picked[:], x_table[:].bitcast(U32).indirect(picks[:, a * half // LANES : (a + 1) * half // LANES]))
-            x_code.append(picked)
+        x_code = keep.tile([P, S], U32, name="x_code", tag="slot_c", align_bytes=64)
+        for a in range(2):
+            nc.vector.tensor_copy(
+                x_code[:, a * half : (a + 1) * half],
+                x_table[:].bitcast(U32).indirect(picks[:, a * half // LANES : (a + 1) * half // LANES]),
+            )
 
         def deal(rows, dtype, name, tag):
             dealt = keep.tile([P, N], dtype, name=name, tag=tag, align_bytes=64)
-            nc.vector.tensor_copy(out=dealt[:].rearrange("p (t m) -> p t m", t=PACK), in_=rows[:].rearrange("p (m t) -> p t m", t=PACK))
+            nc.vector.tensor_copy(out=dealt[:].rearrange("p (t m) -> p m t", t=PACK), in_=rows[:].rearrange("p (m t) -> p m t", t=PACK))
             return dealt
 
         w2_code = deal(w2_rows, I32, "w2_code", "slot_x")
@@ -111,7 +112,7 @@ def tile_picked_zrandla_relu_po_kernel(
                     out=h_sum[:, t, :],
                     lhsT=w1_code[:, w_cols].bitcast(FP8X4),
                     lhsT_scale=w1_scale[:, w_cols],
-                    rhs=x_code[q // 2][:, (q % 2) * P : (q % 2 + 1) * P].bitcast(FP8X4),
+                    rhs=x_code[:, cols].bitcast(FP8X4),
                     rhs_scale=x_scale[:, cols],
                     start=True,
                     stop=True,
@@ -121,8 +122,8 @@ def tile_picked_zrandla_relu_po_kernel(
             nc.vector.quantize_mx(out=h_code[:, cols].bitcast(FP8X4), scales=h_scale[:, cols], in_=h_bf[:].rearrange("p n t -> p (n t)"))
             if q == 0:
                 w2_scale = deal(w2_scale_rows, U8, "w2_scale", "slot_h0")
-            if q == 2:
-                w3_code = deal(w3_rows, I32, "w3_code", "slot_h2")
+            if q == 1:
+                w3_code = deal(w3_rows, I32, "w3_code", "slot_h1")
             if q == 3:
                 w3_scale = deal(w3_scale_rows, U8, "w3_scale", "slot_h3")
 

@@ -46,7 +46,6 @@ def tile_picked_zrandla_relu_po_kernel(
 
         x_scale_table = keep.tile([P, T], U8, name="x_scale_table", tag="slot_a", align_bytes=64)
         w2_scale_rows = keep.tile([P, N], U8, name="w2_scale_rows", align_bytes=64)
-        w3_scale_rows = keep.tile([P, N], U8, name="w3_scale_rows", align_bytes=64)
         nc.vector.memset(x_scale_table[:].bitcast(I32), 0)
 
         w1_rows = keep.tile([P, PACK, H], F32, name="w1_rows", tag="slot_w1", align_bytes=64)
@@ -59,8 +58,7 @@ def tile_picked_zrandla_relu_po_kernel(
         for tile, source in zip(near, (pos1, pos2, pos3)):
             nc.sync.dma_start(tile[:], source)
         nc.gpsimd.memset(w2_scale_rows[:].bitcast(I32), 0)
-        load_scale_rows([nc.gpsimd] * 4, w2_scale_rows, w2_scales)
-        nc.gpsimd.memset(w3_scale_rows[:].bitcast(I32), 0)
+        load_scale_rows([nc.gpsimd, nc.gpsimd, nc.scalar, nc.scalar], w2_scale_rows, w2_scales)
 
         identity = keep.tile([P, P], F32, name="identity", align_bytes=64)
         make_identity(nc, identity[:])
@@ -84,6 +82,8 @@ def tile_picked_zrandla_relu_po_kernel(
             )
         w3_rows = keep.tile([P, N], I32, name="w3_rows", tag="slot_w1", align_bytes=64)
         nc.sync.dma_start(out=w3_rows[:], in_=words_of(w3_words))
+        w3_scale_rows = keep.tile([P, N], U8, name="w3_scale_rows", tag="slot_a", align_bytes=64)
+        nc.gpsimd.memset(w3_scale_rows[:].bitcast(I32), 0)
         load_scale_rows([nc.sync] * 4, w3_scale_rows, w3_scales)
 
         half = S // 2

@@ -22,9 +22,9 @@ QUAD = 32
 LANES = 16
 
 
-def load_scale_rows(queues, tile, scales):
+def load_scale_rows(queues, tile, scales, first=0):
     for q, queue in enumerate(queues):
-        row = QUAD * q
+        row = QUAD * q + first
         queue.dma_start(out=tile[row : row + PACK, :].bitcast(I32), in_=scales[0, PACK * q : PACK * (q + 1), :].bitcast(I32))
 
 
@@ -45,53 +45,69 @@ def tile_picked_zrandla_relu_po_kernel(
         near = [lists.tile([P, V // LANES], U16, name=f"near{d}") for d in range(3)]
 
         x_scale_table = keep.tile([P, T], U8, name="x_scale_table", tag="slot_a", align_bytes=64)
-        w2_scale_rows = keep.tile([P, N], U8, name="w2_scale_rows", align_bytes=64)
+        w_scale_rows = keep.tile([P, N], U8, name="w_scale_rows", align_bytes=64)
         nc.vector.memset(x_scale_table[:].bitcast(I32), 0)
 
-        w1_rows = keep.tile([P, PACK, H], F32, name="w1_rows", tag="slot_w1", align_bytes=64)
+        nc.gpsimd.memset(w_scale_rows[:].bitcast(I32), 0)
+        w1_rows = keep.tile([P, PACK, H], F32, name="w1_rows", align_bytes=64)
         x_table = keep.tile([P, T], I32, name="x_table", tag="slot_x", align_bytes=64)
-        x_scale_rows = keep.tile([P, T], U8, name="x_scale_rows", tag="slot_b", align_bytes=64)
+        x_scale_rows = keep.tile([P, T], U8, name="x_scale_rows", align_bytes=64)
+        w2_rows = keep.tile([P, N], I32, name="w2_rows", align_bytes=64)
+        w3_rows = keep.tile([P, N], I32, name="w3_rows", align_bytes=64)
         nc.sync.dma_start(picks[:], offs)
         load_scale_rows([nc.scalar, nc.scalar, nc.sync, nc.sync], x_scale_rows, x_scales)
         nc.sync.dma_start(out=w1_rows[:], in_=w1.rearrange("(p j) c -> p j c", j=PACK))
         nc.sync.dma_start(out=x_table[:], in_=words_of(x_words))
+        nc.sync.dma_start(out=w2_rows[:], in_=words_of(w2_words))
+        load_scale_rows([nc.sync] * 4, w_scale_rows, w2_scales)
+        load_scale_rows([nc.gpsimd] * 4, w_scale_rows, w3_scales, PACK)
+        nc.sync.dma_start(out=w3_rows[:], in_=words_of(w3_words))
         for tile, source in zip(near, (pos1, pos2, pos3)):
             nc.sync.dma_start(tile[:], source)
-        nc.gpsimd.memset(w2_scale_rows[:].bitcast(I32), 0)
-        load_scale_rows([nc.gpsimd, nc.gpsimd, nc.scalar, nc.scalar], w2_scale_rows, w2_scales)
 
         identity = keep.tile([P, P], F32, name="identity", align_bytes=64)
         make_identity(nc, identity[:])
         for q in range(P // QUAD):
             rows = slice(QUAD * q, QUAD * q + PACK)
             nc.vector.tensor_copy(out=x_scale_table[rows, :].bitcast(I32), in_=x_scale_rows[rows, :].bitcast(I32))
-        x_scale = keep.tile([P, S], U8, name="x_scale", align_bytes=64)
-        nc.vector.tensor_copy(x_scale[:], x_scale_table[:].indirect(picks[:]))
-        w2_rows = keep.tile([P, N], I32, name="w2_rows", tag="slot_b", align_bytes=64)
-        nc.sync.dma_start(out=w2_rows[:], in_=words_of(w2_words))
+        half = S // 2
+        pick_halves = [picks[:, a * half // LANES : (a + 1) * half // LANES] for a in range(2)]
+
+        def fetch_scales(a, tag):
+            picked = keep.tile([P, half], U8, name=f"x_scale{a}", tag=tag, align_bytes=64)
+            nc.vector.tensor_copy(picked[:], x_scale_table[:].indirect(pick_halves[a]))
+            return picked
+
+        x_scale = [fetch_scales(0, "x_scale0")]
 
         w1_code = keep.tile([P, H], U32, name="w1_code", align_bytes=64)
         w1_scale = keep.tile([P, H], U8, name="w1_scale", align_bytes=64)
         w1_src = w1_rows[:].rearrange("p j (m t) -> p m j t", t=PACK)
-        for a, (copy, tag) in enumerate(((nc.scalar.copy, "slot_c"), (nc.vector.tensor_copy, "slot_a"))):
+        for a, (copy, tag) in enumerate(((nc.scalar.copy, "slot_c"), (nc.vector.tensor_copy, "slot_d"))):
             w1_bf = keep.tile([P, 2, P, PACK], BF16, name=f"w1_bf{a}", tag=tag, align_bytes=64)
             copy(out=w1_bf[:].rearrange("p t m j -> p m j t"), in_=w1_src[:, :, :, 2 * a : 2 * a + 2])
             cols = slice(2 * a * P, 2 * (a + 1) * P)
             nc.vector.quantize_mx(
                 out=w1_code[:, cols].bitcast(FP8X4), scales=w1_scale[:, cols], in_=w1_bf[:].rearrange("p t m j -> p (t m j)")
             )
-        w3_rows = keep.tile([P, N], I32, name="w3_rows", tag="slot_w1", align_bytes=64)
-        nc.sync.dma_start(out=w3_rows[:], in_=words_of(w3_words))
-        w3_scale_rows = keep.tile([P, N], U8, name="w3_scale_rows", tag="slot_a", align_bytes=64)
-        nc.gpsimd.memset(w3_scale_rows[:].bitcast(I32), 0)
-        load_scale_rows([nc.sync] * 4, w3_scale_rows, w3_scales)
-
-        half = S // 2
+        x_scale.append(fetch_scales(1, "slot_d"))
+        for bank in range(4, 7):
+            warm = psum.tile([P, 2, half], F32, name=f"warm{bank}", tag=f"bank{bank}")
+            for a in range(2):
+                nc.tensor.matmul_mx(
+                    out=warm[:, a, :],
+                    lhsT=w1_code[:, half : half + P].bitcast(FP8X4),
+                    lhsT_scale=w1_scale[:, half : half + P],
+                    rhs=w1_code[:, half:H].bitcast(FP8X4),
+                    rhs_scale=w1_scale[:, half:H],
+                    start=True,
+                    stop=True,
+                )
         x_code = keep.tile([P, S], U32, name="x_code", tag="slot_c", align_bytes=64)
         for a in range(2):
             nc.vector.tensor_copy(
                 x_code[:, a * half : (a + 1) * half],
-                x_table[:].bitcast(U32).indirect(picks[:, a * half // LANES : (a + 1) * half // LANES]),
+                x_table[:].bitcast(U32).indirect(pick_halves[a]),
             )
 
         def deal(rows, dtype, name, tag):
@@ -113,19 +129,22 @@ def tile_picked_zrandla_relu_po_kernel(
                     lhsT=w1_code[:, w_cols].bitcast(FP8X4),
                     lhsT_scale=w1_scale[:, w_cols],
                     rhs=x_code[:, cols].bitcast(FP8X4),
-                    rhs_scale=x_scale[:, cols],
+                    rhs_scale=x_scale[q // 2][:, (q % 2) * P : (q % 2 + 1) * P],
                     start=True,
                     stop=True,
                 )
             h_bf = keep.tile([P, P, PACK], BF16, name=f"h_bf{q}", tag=f"slot_h{q}", align_bytes=64)
-            nc.scalar.activation(out=h_bf[:], in_=h_sum[:].rearrange("p t n -> p n t"), func=ACT.Relu)
+            if q == 1:
+                nc.vector.tensor_scalar_max(out=h_bf[:], in0=h_sum[:].rearrange("p t n -> p n t"), scalar1=0.0)
+            else:
+                nc.scalar.activation(out=h_bf[:], in_=h_sum[:].rearrange("p t n -> p n t"), func=ACT.Relu)
             nc.vector.quantize_mx(out=h_code[:, cols].bitcast(FP8X4), scales=h_scale[:, cols], in_=h_bf[:].rearrange("p n t -> p (n t)"))
             if q == 0:
-                w2_scale = deal(w2_scale_rows, U8, "w2_scale", "slot_h0")
-            if q == 1:
-                w3_code = deal(w3_rows, I32, "w3_code", "slot_h1")
+                w_scale = deal(w_scale_rows, U8, "w_scale", "slot_h0")
             if q == 3:
-                w3_scale = deal(w3_scale_rows, U8, "w3_scale", "slot_h3")
+                w3_code = deal(w3_rows, I32, "w3_code", "slot_h3")
+        w2_scale = w_scale[:]
+        w3_scale = w_scale[PACK:P, :]
 
         score = []
         feature = []
@@ -199,24 +218,18 @@ def tile_picked_zrandla_relu_po_kernel(
             ey_near = near_tiles(f"ey_near{t}", first_tag)
             for d in range(3):
                 nc.vector.tensor_tensor(ey_near[d][:], feature[t][:].indirect(near[d][:]), e_near[d][:], ALU.mult)
-            return turned_sum(ey_near, f"num{t}", f"bank{2 + t % 2}")
+            return turned_sum(ey_near, f"num{t}", f"bank{(2, 3, 1)[t]}")
 
         def finish(t, num, inv):
             turned = keep.tile([P, halves, P], F32, name=f"turned{t}", align_bytes=64)
             nc.vector.tensor_tensor(turned[:], num[:], inv[:], ALU.mult)
-            back = psum.tile([P, halves, P], F32, name=f"back{t}", tag=f"bank{(1, 0, 4)[t]}")
+            back = psum.tile([P, halves, P], F32, name=f"back{t}", tag=f"bank{(0, 4, 5)[t]}")
             for a in range(halves):
                 nc.tensor.transpose(back[:, a, :], turned[:, a, :], identity[:])
             nc.scalar.copy(out=result[:, t, :], in_=back[:].rearrange("p a v -> p (a v)"))
             nc.sync.dma_start(out=out_rows[:, t, :], in_=result[:, t, :])
             if t == 1:
                 nc.scalar.copy(out=result_bf[:, :, 0:2], in_=result[:, 0:2, :].rearrange("p t v -> p v t"))
-
-        e0, inv0 = fetch_scores(0)
-        num0 = fetch_features(0, e0)
-        e1, inv1 = fetch_scores(1)
-        num1 = fetch_features(1, e1)
-        e2, inv2 = fetch_scores(2)
 
         last = PACK - 1
         weighted = keep.tile([P, S], F32, name="weighted", align_bytes=64)
@@ -229,33 +242,39 @@ def tile_picked_zrandla_relu_po_kernel(
                 nc.vector.tensor_tensor(total[:], window[:].indirect(near[d][:]), before[:], ALU.add)
             return total
 
-        den = gather_sum(score[last], 0, None, "den_a", "den_a")
+        e0, inv0 = fetch_scores(0)
+        num0 = fetch_features(0, e0)
+        e1, inv1 = fetch_scores(1)
+        num1 = fetch_features(1, e1)
+        e2, inv2 = fetch_scores(2)
+        num2 = fetch_features(2, e2)
+        den = gather_sum(score[last], 0, None, "den_a", "e_near2_0")
         nc.vector.tensor_tensor(weighted[:], y_sum[:], score[last][:], ALU.mult)
-        den = gather_sum(score[last], 1, den, "den_b", "den_b")
+        den = gather_sum(score[last], 1, den, "den_b", "e_near2_1")
         finish(0, num0, inv0)
-        den = gather_sum(score[last], 2, den, "den_c", "inv0")
+        num_a = gather_sum(weighted, 0, None, "num_a", "inv0")
+        finish(1, num1, inv1)
+        den = gather_sum(score[last], 2, den, "den_c", "inv1")
         root = keep.tile([P, V], F32, name="root3", align_bytes=64)
         inv = keep.tile([P, V], F32, name="inv3", align_bytes=64)
         nc.scalar.activation(out=root[:], in_=den[:], func=ACT.Abs_reciprocal_sqrt)
         nc.scalar.activation(out=inv[:], in_=root[:], func=ACT.Square)
-        num2 = fetch_features(2, e2)
-        finish(1, num1, inv1)
-        num = gather_sum(weighted, 0, None, "num_a", "inv1")
         finish(2, num2, inv2)
-        num = gather_sum(weighted, 1, num, "num_b", "inv2")
 
         out_code = keep.tile([P, V], U32, name="out_code", align_bytes=64)
         out_scale = keep.tile([P, V], U8, name="out_scale", align_bytes=64)
-        total = keep.tile([P, V], F32, name="num_c", align_bytes=64)
+        num_b = keep.tile([P, V], F32, name="num_b", tag="inv2", align_bytes=64)
+        num_c = keep.tile([P, V], F32, name="num_c", align_bytes=64)
         parts = [slice(a * P, (a + 1) * P) for a in range(halves)]
-        for a, cols in enumerate(parts):
-            offsets = near[2][:, a * P // LANES : (a + 1) * P // LANES]
-            nc.vector.tensor_tensor(total[:, cols], weighted[:].indirect(offsets), num[:, cols], ALU.add)
+        for d, before, total in ((1, num_a, num_b), (2, num_b, num_c)):
+            for a, cols in enumerate(parts):
+                offsets = near[d][:, a * P // LANES : (a + 1) * P // LANES]
+                nc.vector.tensor_tensor(total[:, cols], weighted[:].indirect(offsets), before[:, cols], ALU.add)
         for cols in parts:
-            nc.vector.tensor_tensor(result[:, last, cols], total[:, cols], inv[:, cols], ALU.mult)
+            nc.vector.tensor_tensor(result[:, last, cols], num_c[:, cols], inv[:, cols], ALU.mult)
         nc.sync.dma_start(out=out_rows[:, last, :], in_=result[:, last, :])
-        for cols in parts:
-            nc.vector.tensor_copy(out=result_bf[:, cols, 2:4], in_=result[:, 2:4, cols].rearrange("p t v -> p v t"))
+        for copy, cols in zip((nc.scalar.copy, nc.vector.tensor_copy), parts):
+            copy(out=result_bf[:, cols, 2:4], in_=result[:, 2:4, cols].rearrange("p t v -> p v t"))
         for cols in parts:
             nc.vector.quantize_mx(
                 out=out_code[:, cols].bitcast(FP8X4), scales=out_scale[:, cols], in_=result_bf[:, cols, :].rearrange("p v t -> p (v t)")

@@ -39,6 +39,8 @@ def tile_picked_zrandla_relu_po_kernel(
     with ExitStack() as ctx:
         lists = ctx.enter_context(tc.tile_pool(name="lists", bufs=1))
         keep = ctx.enter_context(tc.tile_pool(name="keep", bufs=1))
+        held = ctx.enter_context(tc.tile_pool(name="held", bufs=1))
+        early = ctx.enter_context(tc.tile_pool(name="early", bufs=1))
         psum = ctx.enter_context(tc.psum_pool(name="psum", bufs=1))
 
         picks = lists.tile([P, S // LANES], U16, name="picks")
@@ -50,10 +52,10 @@ def tile_picked_zrandla_relu_po_kernel(
 
         nc.gpsimd.memset(w_scale_rows[:].bitcast(I32), 0)
         w1_rows = keep.tile([P, PACK, H], F32, name="w1_rows", align_bytes=64)
-        x_table = keep.tile([P, T], I32, name="x_table", tag="slot_x", align_bytes=64)
+        x_table = early.tile([P, T], I32, name="x_table", offset=0, align_bytes=64)
         x_scale_rows = keep.tile([P, T], U8, name="x_scale_rows", align_bytes=64)
         w2_rows = keep.tile([P, N], I32, name="w2_rows", align_bytes=64)
-        w3_rows = keep.tile([P, N], I32, name="w3_rows", align_bytes=64)
+        w3_rows = keep.tile([P, N], I32, name="w3_rows", tag="e_near0", align_bytes=64)
         nc.sync.dma_start(picks[:], offs)
         load_scale_rows([nc.scalar, nc.scalar, nc.sync, nc.sync], x_scale_rows, x_scales)
         nc.sync.dma_start(out=w1_rows[:], in_=w1.rearrange("(p j) c -> p j c", j=PACK))
@@ -73,12 +75,8 @@ def tile_picked_zrandla_relu_po_kernel(
         half = S // 2
         pick_halves = [picks[:, a * half // LANES : (a + 1) * half // LANES] for a in range(2)]
 
-        def fetch_scales(a, tag):
-            picked = keep.tile([P, half], U8, name=f"x_scale{a}", tag=tag, align_bytes=64)
-            nc.vector.tensor_copy(picked[:], x_scale_table[:].indirect(pick_halves[a]))
-            return picked
-
-        x_scale = [fetch_scales(0, "x_scale0")]
+        x_scale = keep.tile([P, S], U8, name="x_scale", align_bytes=64)
+        nc.vector.tensor_copy(x_scale[:], x_scale_table[:].indirect(picks[:]))
 
         w1_code = keep.tile([P, H], U32, name="w1_code", align_bytes=64)
         w1_scale = keep.tile([P, H], U8, name="w1_scale", align_bytes=64)
@@ -90,7 +88,6 @@ def tile_picked_zrandla_relu_po_kernel(
             nc.vector.quantize_mx(
                 out=w1_code[:, cols].bitcast(FP8X4), scales=w1_scale[:, cols], in_=w1_bf[:].rearrange("p t m j -> p (t m j)")
             )
-        x_scale.append(fetch_scales(1, "slot_d"))
         for bank in range(4, 7):
             warm = psum.tile([P, 2, half], F32, name=f"warm{bank}", tag=f"bank{bank}")
             for a in range(2):
@@ -105,17 +102,14 @@ def tile_picked_zrandla_relu_po_kernel(
                 )
         x_code = keep.tile([P, S], U32, name="x_code", tag="slot_c", align_bytes=64)
         for a in range(2):
-            nc.vector.tensor_copy(
-                x_code[:, a * half : (a + 1) * half],
-                x_table[:].bitcast(U32).indirect(pick_halves[a]),
-            )
+            nc.vector.tensor_copy(x_code[:, a * half : (a + 1) * half], x_table[:].bitcast(U32).indirect(pick_halves[a]))
 
-        def deal(rows, dtype, name, tag):
-            dealt = keep.tile([P, N], dtype, name=name, tag=tag, align_bytes=64)
+        def deal(rows, dealt):
             nc.vector.tensor_copy(out=dealt[:].rearrange("p (t m) -> p m t", t=PACK), in_=rows[:].rearrange("p (m t) -> p m t", t=PACK))
             return dealt
 
-        w2_code = deal(w2_rows, I32, "w2_code", "slot_x")
+        w2_code = deal(w2_rows, early.tile([P, N], I32, name="w2_code", offset=0, align_bytes=64))
+        w_scale = deal(w_scale_rows, early.tile([P, N], U8, name="w_scale", offset=4 * N, align_bytes=64))
 
         h_code = keep.tile([P, S], U32, name="h_code", align_bytes=64)
         h_scale = keep.tile([P, S], U8, name="h_scale", align_bytes=64)
@@ -129,7 +123,7 @@ def tile_picked_zrandla_relu_po_kernel(
                     lhsT=w1_code[:, w_cols].bitcast(FP8X4),
                     lhsT_scale=w1_scale[:, w_cols],
                     rhs=x_code[:, cols].bitcast(FP8X4),
-                    rhs_scale=x_scale[q // 2][:, (q % 2) * P : (q % 2 + 1) * P],
+                    rhs_scale=x_scale[:, cols],
                     start=True,
                     stop=True,
                 )
@@ -139,10 +133,8 @@ def tile_picked_zrandla_relu_po_kernel(
             else:
                 nc.scalar.activation(out=h_bf[:], in_=h_sum[:].rearrange("p t n -> p n t"), func=ACT.Relu)
             nc.vector.quantize_mx(out=h_code[:, cols].bitcast(FP8X4), scales=h_scale[:, cols], in_=h_bf[:].rearrange("p n t -> p (n t)"))
-            if q == 0:
-                w_scale = deal(w_scale_rows, U8, "w_scale", "slot_h0")
             if q == 3:
-                w3_code = deal(w3_rows, I32, "w3_code", "slot_h3")
+                w3_code = deal(w3_rows, keep.tile([P, N], I32, name="w3_code", tag="slot_h3", align_bytes=64))
         w2_scale = w_scale[:]
         w3_scale = w_scale[PACK:P, :]
 
@@ -164,18 +156,16 @@ def tile_picked_zrandla_relu_po_kernel(
 
             e = keep.tile([P, S], F32, name=f"score{t}", align_bytes=64)
             if t == 0:
-                s_head = psum.tile([P, S], F32, name="s_head", tag="bank7")
-                product(s_head[:, 0:256], w2_code, w2_scale, slice(0, 256))
-                product(s_head[:, 256:384], w2_code, w2_scale, slice(256, 384))
-                nc.scalar.activation(out=e[:, 0:384], in_=s_head[:, 0:384], func=ACT.Exp)
-                s_sum = psum.tile([P, S], F32, name=f"s_sum{t}", tag=f"bank{t}")
-                product(s_sum[:, 0:128], w2_code, w2_scale, slice(384, 512))
-                nc.scalar.activation(out=e[:, 384:512], in_=s_sum[:, 0:128], func=ACT.Exp)
+                for q in range(4):
+                    cols = slice(q * P, (q + 1) * P)
+                    s_part = psum.tile([P, P], F32, name=f"s_part{q}", tag=f"bank{PACK + q}")
+                    product(s_part[:], w2_code, w2_scale, cols)
+                    nc.scalar.activation(out=e[:, cols], in_=s_part[:], func=ACT.Exp)
             else:
-                s_sum = psum.tile([P, S], F32, name=f"s_sum{t}", tag=f"bank{t}")
+                s_sum = psum.tile([P, S], F32, name=f"s_sum{t}", tag=f"bank{(7, 0, 7)[t - 1]}")
                 product(s_sum[:], w2_code, w2_scale, slice(0, S))
                 nc.scalar.activation(out=e[:], in_=s_sum[:], func=ACT.Exp)
-            y_sum = psum.tile([P, S], F32, name=f"y_sum{t}", tag=f"bank{PACK + t}")
+            y_sum = psum.tile([P, S], F32, name=f"y_sum{t}", tag=f"bank{t}")
             product(y_sum[:], w3_code, w3_scale, slice(0, S))
             score.append(e)
             if t < PACK - 1:
@@ -194,31 +184,26 @@ def tile_picked_zrandla_relu_po_kernel(
             for a in range(halves):
                 for d in range(3):
                     nc.tensor.matmul(
-                        total[:, a, :], lhsT=terms[d][:, a * P : (a + 1) * P], rhs=identity[:],
+                        total[:, a, :], lhsT=terms[:, d, a * P : (a + 1) * P], rhs=identity[:],
                         is_transpose=True, start=(d == 0), stop=(d == 2),
                     )
             return total
 
-        def near_tiles(name, first_tag):
-            tags = [first_tag or f"{name}_0", f"{name}_1", f"{name}_2"]
-            return [keep.tile([P, V], F32, name=f"{name}_{d}", tag=tags[d], align_bytes=64) for d in range(3)]
-
-        def fetch_scores(t, first_tag=None):
-            e_near = near_tiles(f"e_near{t}", first_tag)
+        def fetch_scores(t, root):
+            e_near = keep.tile([P, 3, V], F32, name=f"e_near{t}", tag=f"e_near{t}", align_bytes=64)
             for d in range(3):
-                nc.vector.tensor_copy(e_near[d][:], score[t][:].indirect(near[d][:]))
+                nc.vector.tensor_copy(e_near[:, d, :], score[t][:].indirect(near[d][:]))
             den = turned_sum(e_near, f"den{t}", f"bank{5 + t % 2}")
-            root = keep.tile([P, halves, P], F32, name=f"root{t}", align_bytes=64)
-            inv = keep.tile([P, halves, P], F32, name=f"inv{t}", tag=f"inv{t}", align_bytes=64)
-            nc.scalar.activation(out=root[:], in_=den[:], func=ACT.Abs_reciprocal_sqrt)
-            nc.scalar.activation(out=inv[:], in_=root[:], func=ACT.Square)
+            inv = keep.tile([P, halves, P], F32, name=f"inv{t}", align_bytes=64)
+            root = root[:, 0:V].rearrange("p (a v) -> p a v", a=halves)
+            nc.scalar.activation(out=root, in_=den[:], func=ACT.Abs_reciprocal_sqrt)
+            nc.scalar.activation(out=inv[:], in_=root, func=ACT.Square)
             return e_near, inv
 
-        def fetch_features(t, e_near, first_tag=None):
-            ey_near = near_tiles(f"ey_near{t}", first_tag)
+        def fetch_features(t, e_near, ey_near):
             for d in range(3):
-                nc.vector.tensor_tensor(ey_near[d][:], feature[t][:].indirect(near[d][:]), e_near[d][:], ALU.mult)
-            return turned_sum(ey_near, f"num{t}", f"bank{(2, 3, 1)[t]}")
+                nc.vector.tensor_tensor(ey_near[:, d, :], feature[t][:].indirect(near[d][:]), e_near[:, d, :], ALU.mult)
+            return turned_sum(ey_near, f"num{t}", f"bank{(4, 1, 2)[t]}")
 
         def finish(t, num, inv):
             turned = keep.tile([P, halves, P], F32, name=f"turned{t}", align_bytes=64)
@@ -232,38 +217,37 @@ def tile_picked_zrandla_relu_po_kernel(
                 nc.scalar.copy(out=result_bf[:, :, 0:2], in_=result[:, 0:2, :].rearrange("p t v -> p v t"))
 
         last = PACK - 1
-        weighted = keep.tile([P, S], F32, name="weighted", align_bytes=64)
-
-        def gather_sum(window, d, before, name, tag):
-            total = keep.tile([P, V], F32, name=name, tag=tag, align_bytes=64)
-            if before is None:
-                nc.vector.tensor_copy(total[:], window[:].indirect(near[d][:]))
-            else:
-                nc.vector.tensor_tensor(total[:], window[:].indirect(near[d][:]), before[:], ALU.add)
-            return total
-
-        e0, inv0 = fetch_scores(0)
-        num0 = fetch_features(0, e0)
-        e1, inv1 = fetch_scores(1)
-        num1 = fetch_features(1, e1)
-        e2, inv2 = fetch_scores(2)
-        num2 = fetch_features(2, e2)
-        den = gather_sum(score[last], 0, None, "den_a", "e_near2_0")
-        nc.vector.tensor_tensor(weighted[:], y_sum[:], score[last][:], ALU.mult)
-        den = gather_sum(score[last], 1, den, "den_b", "e_near2_1")
+        words = 4 * V
+        root0 = held.tile([P, V], F32, name="root0", offset=6 * words)
+        e0, inv0 = fetch_scores(0, root0)
+        num0 = fetch_features(0, e0, keep.tile([P, 3, V], F32, name="ey_near0", align_bytes=64))
+        root1 = held.tile([P, 8 * V], F32, name="root1", offset=0)
+        e1, inv1 = fetch_scores(1, root1)
+        num1 = fetch_features(1, e1, keep.tile([P, 3, V], F32, name="ey_near1", align_bytes=64))
+        root2 = held.tile([P, V], F32, name="root2", offset=6 * words)
+        e2, inv2 = fetch_scores(2, root2)
         finish(0, num0, inv0)
-        num_a = gather_sum(weighted, 0, None, "num_a", "inv0")
         finish(1, num1, inv1)
-        den = gather_sum(score[last], 2, den, "den_c", "inv1")
-        root = keep.tile([P, V], F32, name="root3", align_bytes=64)
+        num2 = fetch_features(2, e2, held.tile([P, 3, V], F32, name="ey_near2", offset=0))
+        den_a = held.tile([P, V], F32, name="den_a", offset=3 * words)
+        weighted = held.tile([P, S], F32, name="weighted", offset=4 * words)
+        den_b = keep.tile([P, V], F32, name="den_b", align_bytes=64)
+        den_c = keep.tile([P, V], F32, name="den_c", align_bytes=64)
+        num_a = keep.tile([P, V], F32, name="num_a", align_bytes=64)
+        nc.vector.tensor_copy(den_a[:], score[last][:].indirect(near[0][:]))
+        nc.vector.tensor_tensor(weighted[:], y_sum[:], score[last][:], ALU.mult)
+        nc.vector.tensor_tensor(den_b[:], score[last][:].indirect(near[1][:]), den_a[:], ALU.add)
+        nc.vector.tensor_copy(num_a[:], weighted[:].indirect(near[0][:]))
+        nc.vector.tensor_tensor(den_c[:], score[last][:].indirect(near[2][:]), den_b[:], ALU.add)
+        root = held.tile([P, V], F32, name="root3", offset=6 * words)
         inv = keep.tile([P, V], F32, name="inv3", align_bytes=64)
-        nc.scalar.activation(out=root[:], in_=den[:], func=ACT.Abs_reciprocal_sqrt)
+        nc.scalar.activation(out=root[:], in_=den_c[:], func=ACT.Abs_reciprocal_sqrt)
         nc.scalar.activation(out=inv[:], in_=root[:], func=ACT.Square)
         finish(2, num2, inv2)
 
         out_code = keep.tile([P, V], U32, name="out_code", align_bytes=64)
         out_scale = keep.tile([P, V], U8, name="out_scale", align_bytes=64)
-        num_b = keep.tile([P, V], F32, name="num_b", tag="inv2", align_bytes=64)
+        num_b = held.tile([P, V], F32, name="num_b", offset=0)
         num_c = keep.tile([P, V], F32, name="num_c", align_bytes=64)
         parts = [slice(a * P, (a + 1) * P) for a in range(halves)]
         for d, before, total in ((1, num_a, num_b), (2, num_b, num_c)):

@@ -168,10 +168,9 @@ def tile_picked_zrandla_relu_po_kernel(
             y_sum = psum.tile([P, S], F32, name=f"y_sum{t}", tag=f"bank{t}")
             product(y_sum[:], w3_code, w3_scale, slice(0, S))
             score.append(e)
-            if t < PACK - 1:
-                y = keep.tile([P, S], F32, name=f"feature{t}", align_bytes=64)
-                nc.scalar.copy(out=y[:], in_=y_sum[:])
-                feature.append(y)
+            y = keep.tile([P, S], F32, name=f"feature{t}", tag=f"feature{t}", align_bytes=64)
+            nc.scalar.copy(out=y[:], in_=y_sum[:])
+            feature.append(y)
 
         result = keep.tile([P, PACK, V], F32, name="result", align_bytes=64)
         result_bf = keep.tile([P, V, PACK], BF16, name="result_bf", align_bytes=64)
@@ -205,9 +204,9 @@ def tile_picked_zrandla_relu_po_kernel(
                 nc.vector.tensor_tensor(ey_near[:, d, :], feature[t][:].indirect(near[d][:]), e_near[:, d, :], ALU.mult)
             return turned_sum(ey_near, f"num{t}", f"bank{(4, 1, 2)[t]}")
 
-        def finish(t, num, inv):
-            turned = keep.tile([P, halves, P], F32, name=f"turned{t}", align_bytes=64)
-            nc.vector.tensor_tensor(turned[:], num[:], inv[:], ALU.mult)
+        def finish(t, engine, num, inv, tag):
+            turned = keep.tile([P, halves, P], F32, name=f"turned{t}", tag=tag, align_bytes=64)
+            engine.tensor_tensor(turned[:], num[:], inv[:], ALU.mult)
             back = psum.tile([P, halves, P], F32, name=f"back{t}", tag=f"bank{(0, 4, 5)[t]}")
             for a in range(halves):
                 nc.tensor.transpose(back[:, a, :], turned[:, a, :], identity[:])
@@ -218,32 +217,34 @@ def tile_picked_zrandla_relu_po_kernel(
 
         last = PACK - 1
         words = 4 * V
-        root0 = held.tile([P, V], F32, name="root0", offset=6 * words)
+        root0 = held.tile([P, 3 * V], F32, name="root0", offset=6 * words)
         e0, inv0 = fetch_scores(0, root0)
         num0 = fetch_features(0, e0, keep.tile([P, 3, V], F32, name="ey_near0", align_bytes=64))
+        num0_sb = held.tile([P, halves, P], F32, name="num0_sb", offset=8 * words)
+        nc.scalar.copy(out=num0_sb[:], in_=num0[:])
         root1 = held.tile([P, 8 * V], F32, name="root1", offset=0)
         e1, inv1 = fetch_scores(1, root1)
         num1 = fetch_features(1, e1, keep.tile([P, 3, V], F32, name="ey_near1", align_bytes=64))
+        weighted = keep.tile([P, S], F32, name="weighted", tag="feature1", align_bytes=64)
+        nc.gpsimd.tensor_tensor(weighted[:], feature[last][:], score[last][:], ALU.mult)
+        finish(0, nc.gpsimd, num0_sb, inv0, "e_near1")
         root2 = held.tile([P, V], F32, name="root2", offset=6 * words)
         e2, inv2 = fetch_scores(2, root2)
-        finish(0, num0, inv0)
-        finish(1, num1, inv1)
+        finish(1, nc.vector, num1, inv1, "turned1")
         num2 = fetch_features(2, e2, held.tile([P, 3, V], F32, name="ey_near2", offset=0))
         den_a = held.tile([P, V], F32, name="den_a", offset=3 * words)
-        weighted = held.tile([P, S], F32, name="weighted", offset=4 * words)
         den_b = keep.tile([P, V], F32, name="den_b", align_bytes=64)
-        den_c = keep.tile([P, V], F32, name="den_c", align_bytes=64)
-        num_a = keep.tile([P, V], F32, name="num_a", align_bytes=64)
+        den_c = held.tile([P, V], F32, name="den_c", offset=words)
+        num_a = held.tile([P, V], F32, name="num_a", offset=4 * words)
         nc.vector.tensor_copy(den_a[:], score[last][:].indirect(near[0][:]))
-        nc.vector.tensor_tensor(weighted[:], y_sum[:], score[last][:], ALU.mult)
-        nc.vector.tensor_tensor(den_b[:], score[last][:].indirect(near[1][:]), den_a[:], ALU.add)
         nc.vector.tensor_copy(num_a[:], weighted[:].indirect(near[0][:]))
+        nc.vector.tensor_tensor(den_b[:], score[last][:].indirect(near[1][:]), den_a[:], ALU.add)
+        finish(2, nc.vector, num2, inv2, "turned2")
         nc.vector.tensor_tensor(den_c[:], score[last][:].indirect(near[2][:]), den_b[:], ALU.add)
         root = held.tile([P, V], F32, name="root3", offset=6 * words)
         inv = keep.tile([P, V], F32, name="inv3", align_bytes=64)
         nc.scalar.activation(out=root[:], in_=den_c[:], func=ACT.Abs_reciprocal_sqrt)
         nc.scalar.activation(out=inv[:], in_=root[:], func=ACT.Square)
-        finish(2, num2, inv2)
 
         out_code = keep.tile([P, V], U32, name="out_code", align_bytes=64)
         out_scale = keep.tile([P, V], U8, name="out_scale", align_bytes=64)

@@ -138,39 +138,41 @@ def tile_picked_zrandla_relu_po_kernel(
         w2_scale = w_scale[:]
         w3_scale = w_scale[PACK:P, :]
 
-        score = []
-        feature = []
-        for t in range(PACK):
+        def product(total, code, scale, t, cols):
             w_cols = slice(t * P, (t + 1) * P)
+            nc.tensor.matmul_mx(
+                out=total,
+                lhsT=code[:, w_cols].bitcast(FP8X4),
+                lhsT_scale=scale[:, w_cols],
+                rhs=h_code[:, cols].bitcast(FP8X4),
+                rhs_scale=h_scale[:, cols],
+                start=True,
+                stop=True,
+            )
 
-            def product(total, code, scale, cols):
-                nc.tensor.matmul_mx(
-                    out=total,
-                    lhsT=code[:, w_cols].bitcast(FP8X4),
-                    lhsT_scale=scale[:, w_cols],
-                    rhs=h_code[:, cols].bitcast(FP8X4),
-                    rhs_scale=h_scale[:, cols],
-                    start=True,
-                    stop=True,
-                )
+        score = [keep.tile([P, S], F32, name=f"score{t}", align_bytes=64) for t in range(PACK)]
+        feature = [keep.tile([P, S], F32, name=f"feature{t}", tag=f"feature{t}", align_bytes=64) for t in range(PACK)]
 
-            e = keep.tile([P, S], F32, name=f"score{t}", align_bytes=64)
-            if t == 0:
-                for q in range(4):
-                    cols = slice(q * P, (q + 1) * P)
-                    s_part = psum.tile([P, P], F32, name=f"s_part{q}", tag=f"bank{PACK + q}")
-                    product(s_part[:], w2_code, w2_scale, cols)
-                    nc.scalar.activation(out=e[:, cols], in_=s_part[:], func=ACT.Exp)
-            else:
-                s_sum = psum.tile([P, S], F32, name=f"s_sum{t}", tag=f"bank{(7, 0, 7)[t - 1]}")
-                product(s_sum[:], w2_code, w2_scale, slice(0, S))
-                nc.scalar.activation(out=e[:], in_=s_sum[:], func=ACT.Exp)
+        def make_scores(t, bank):
+            s_sum = psum.tile([P, S], F32, name=f"s_sum{t}", tag=bank)
+            product(s_sum[:], w2_code, w2_scale, t, slice(0, S))
+            nc.scalar.activation(out=score[t][:], in_=s_sum[:], func=ACT.Exp)
+
+        def make_features(t):
             y_sum = psum.tile([P, S], F32, name=f"y_sum{t}", tag=f"bank{t}")
-            product(y_sum[:], w3_code, w3_scale, slice(0, S))
-            score.append(e)
-            y = keep.tile([P, S], F32, name=f"feature{t}", tag=f"feature{t}", align_bytes=64)
-            nc.scalar.copy(out=y[:], in_=y_sum[:])
-            feature.append(y)
+            product(y_sum[:], w3_code, w3_scale, t, slice(0, S))
+            nc.scalar.copy(out=feature[t][:], in_=y_sum[:])
+
+        for q in range(4):
+            cols = slice(q * P, (q + 1) * P)
+            s_part = psum.tile([P, P], F32, name=f"s_part{q}", tag=f"bank{PACK + q}")
+            product(s_part[:], w2_code, w2_scale, 0, cols)
+            nc.scalar.activation(out=score[0][:, cols], in_=s_part[:], func=ACT.Exp)
+        make_features(0)
+        make_scores(1, "bank7")
+        make_features(1)
+        make_scores(2, "bank0")
+        make_scores(3, "bank7")
 
         result = keep.tile([P, PACK, V], F32, name="result", align_bytes=64)
         result_bf = keep.tile([P, V, PACK], BF16, name="result_bf", align_bytes=64)
@@ -183,7 +185,7 @@ def tile_picked_zrandla_relu_po_kernel(
             for a in range(halves):
                 for d in range(3):
                     nc.tensor.matmul(
-                        total[:, a, :], lhsT=terms[:, d, a * P : (a + 1) * P], rhs=identity[:],
+                        total[:, a, :], lhsT=terms[d][:, a * P : (a + 1) * P], rhs=identity[:],
                         is_transpose=True, start=(d == 0), stop=(d == 2),
                     )
             return total
@@ -192,17 +194,20 @@ def tile_picked_zrandla_relu_po_kernel(
             e_near = keep.tile([P, 3, V], F32, name=f"e_near{t}", tag=f"e_near{t}", align_bytes=64)
             for d in range(3):
                 nc.vector.tensor_copy(e_near[:, d, :], score[t][:].indirect(near[d][:]))
-            den = turned_sum(e_near, f"den{t}", f"bank{5 + t % 2}")
+            den = turned_sum(thirds(e_near), f"den{t}", f"bank{(7, 6, 5)[t]}")
             inv = keep.tile([P, halves, P], F32, name=f"inv{t}", align_bytes=64)
             root = root[:, 0:V].rearrange("p (a v) -> p a v", a=halves)
             nc.scalar.activation(out=root, in_=den[:], func=ACT.Abs_reciprocal_sqrt)
             nc.scalar.activation(out=inv[:], in_=root, func=ACT.Square)
             return e_near, inv
 
-        def fetch_features(t, e_near, ey_near):
+        def fetch_features(t, e_near, terms):
             for d in range(3):
-                nc.vector.tensor_tensor(ey_near[:, d, :], feature[t][:].indirect(near[d][:]), e_near[:, d, :], ALU.mult)
-            return turned_sum(ey_near, f"num{t}", f"bank{(4, 1, 2)[t]}")
+                nc.vector.tensor_tensor(terms[d], feature[t][:].indirect(near[d][:]), e_near[:, d, :], ALU.mult)
+            return turned_sum(terms, f"num{t}", f"bank{(4, 1, 2)[t]}")
+
+        def thirds(tile):
+            return [tile[:, d, :] for d in range(3)]
 
         def finish(t, engine, num, inv, tag):
             turned = keep.tile([P, halves, P], F32, name=f"turned{t}", tag=tag, align_bytes=64)
@@ -219,19 +224,23 @@ def tile_picked_zrandla_relu_po_kernel(
         words = 4 * V
         root0 = held.tile([P, 3 * V], F32, name="root0", offset=6 * words)
         e0, inv0 = fetch_scores(0, root0)
-        num0 = fetch_features(0, e0, keep.tile([P, 3, V], F32, name="ey_near0", align_bytes=64))
+        make_features(3)
+        num0 = fetch_features(0, e0, thirds(keep.tile([P, 3, V], F32, name="ey_near0", align_bytes=64)))
         num0_sb = held.tile([P, halves, P], F32, name="num0_sb", offset=8 * words)
         nc.scalar.copy(out=num0_sb[:], in_=num0[:])
+        make_features(2)
         root1 = held.tile([P, 8 * V], F32, name="root1", offset=0)
         e1, inv1 = fetch_scores(1, root1)
-        num1 = fetch_features(1, e1, keep.tile([P, 3, V], F32, name="ey_near1", align_bytes=64))
+        num1 = fetch_features(1, e1, thirds(keep.tile([P, 3, V], F32, name="ey_near1", align_bytes=64)))
         weighted = keep.tile([P, S], F32, name="weighted", tag="feature1", align_bytes=64)
         nc.gpsimd.tensor_tensor(weighted[:], feature[last][:], score[last][:], ALU.mult)
         finish(0, nc.gpsimd, num0_sb, inv0, "e_near1")
         root2 = held.tile([P, V], F32, name="root2", offset=6 * words)
         e2, inv2 = fetch_scores(2, root2)
         finish(1, nc.vector, num1, inv1, "turned1")
-        num2 = fetch_features(2, e2, held.tile([P, 3, V], F32, name="ey_near2", offset=0))
+        ey_first = keep.tile([P, 2, V], F32, name="ey_near2", align_bytes=64)
+        ey_last = held.tile([P, 2, V], F32, name="ey_last", offset=0)
+        num2 = fetch_features(2, e2, [ey_first[:, 0, :], ey_first[:, 1, :], ey_last[:, 0, :]])
         den_a = held.tile([P, V], F32, name="den_a", offset=3 * words)
         den_b = keep.tile([P, V], F32, name="den_b", align_bytes=64)
         den_c = held.tile([P, V], F32, name="den_c", offset=words)

@@ -20,9 +20,11 @@ P = 128
 PACK = 4
 QUAD = 32
 LANES = 16
+NEIGHBOURS = 3
+ROW = 4 * V
 
 
-def load_scale_rows(queues, tile, scales, first=0):
+def load_scale_rows(queues, tile, scales, first):
     for q, queue in enumerate(queues):
         row = QUAD * q + first
         queue.dma_start(out=tile[row : row + PACK, :].bitcast(I32), in_=scales[0, PACK * q : PACK * (q + 1), :].bitcast(I32))
@@ -39,82 +41,87 @@ def tile_picked_zrandla_relu_po_kernel(
     with ExitStack() as ctx:
         lists = ctx.enter_context(tc.tile_pool(name="lists", bufs=1))
         keep = ctx.enter_context(tc.tile_pool(name="keep", bufs=1))
-        held = ctx.enter_context(tc.tile_pool(name="held", bufs=1))
-        early = ctx.enter_context(tc.tile_pool(name="early", bufs=1))
+        shared = ctx.enter_context(tc.tile_pool(name="shared", bufs=1))
+        table = ctx.enter_context(tc.tile_pool(name="table", bufs=1))
         psum = ctx.enter_context(tc.psum_pool(name="psum", bufs=1))
 
         picks = lists.tile([P, S // LANES], U16, name="picks")
-        near = [lists.tile([P, V // LANES], U16, name=f"near{d}") for d in range(3)]
+        near = [lists.tile([P, V // LANES], U16, name=f"near{d}") for d in range(NEIGHBOURS)]
 
-        x_scale_table = keep.tile([P, T], U8, name="x_scale_table", tag="slot_a", align_bytes=64)
+        x_scale_table = keep.tile([P, T], U8, name="x_scale_table", align_bytes=64)
         w_scale_rows = keep.tile([P, N], U8, name="w_scale_rows", align_bytes=64)
         nc.vector.memset(x_scale_table[:].bitcast(I32), 0)
-
         nc.gpsimd.memset(w_scale_rows[:].bitcast(I32), 0)
+
         w1_rows = keep.tile([P, PACK, H], F32, name="w1_rows", align_bytes=64)
-        x_table = early.tile([P, T], I32, name="x_table", offset=0, align_bytes=64)
+        x_table = table.tile([P, T], I32, name="x_table", offset=0, align_bytes=64)
         x_scale_rows = keep.tile([P, T], U8, name="x_scale_rows", align_bytes=64)
         w2_rows = keep.tile([P, N], I32, name="w2_rows", align_bytes=64)
         w3_rows = keep.tile([P, N], I32, name="w3_rows", tag="e_near0", align_bytes=64)
         nc.sync.dma_start(picks[:], offs)
-        load_scale_rows([nc.scalar, nc.scalar, nc.sync, nc.sync], x_scale_rows, x_scales)
+        load_scale_rows([nc.scalar, nc.scalar, nc.sync, nc.sync], x_scale_rows, x_scales, 0)
         nc.sync.dma_start(out=w1_rows[:], in_=w1.rearrange("(p j) c -> p j c", j=PACK))
         nc.sync.dma_start(out=x_table[:], in_=words_of(x_words))
         nc.sync.dma_start(out=w2_rows[:], in_=words_of(w2_words))
-        load_scale_rows([nc.sync] * 4, w_scale_rows, w2_scales)
-        load_scale_rows([nc.gpsimd] * 4, w_scale_rows, w3_scales, PACK)
+        load_scale_rows([nc.sync] * PACK, w_scale_rows, w2_scales, 0)
+        load_scale_rows([nc.gpsimd] * PACK, w_scale_rows, w3_scales, PACK)
         nc.sync.dma_start(out=w3_rows[:], in_=words_of(w3_words))
         for tile, source in zip(near, (pos1, pos2, pos3)):
             nc.sync.dma_start(tile[:], source)
 
         identity = keep.tile([P, P], F32, name="identity", align_bytes=64)
         make_identity(nc, identity[:])
+
         for q in range(P // QUAD):
             rows = slice(QUAD * q, QUAD * q + PACK)
             nc.vector.tensor_copy(out=x_scale_table[rows, :].bitcast(I32), in_=x_scale_rows[rows, :].bitcast(I32))
-        half = S // 2
-        pick_halves = [picks[:, a * half // LANES : (a + 1) * half // LANES] for a in range(2)]
-
         x_scale = keep.tile([P, S], U8, name="x_scale", align_bytes=64)
         nc.vector.tensor_copy(x_scale[:], x_scale_table[:].indirect(picks[:]))
 
         w1_code = keep.tile([P, H], U32, name="w1_code", align_bytes=64)
         w1_scale = keep.tile([P, H], U8, name="w1_scale", align_bytes=64)
         w1_src = w1_rows[:].rearrange("p j (m t) -> p m j t", t=PACK)
-        for a, (copy, tag) in enumerate(((nc.scalar.copy, "slot_c"), (nc.vector.tensor_copy, "slot_d"))):
-            w1_bf = keep.tile([P, 2, P, PACK], BF16, name=f"w1_bf{a}", tag=tag, align_bytes=64)
-            copy(out=w1_bf[:].rearrange("p t m j -> p m j t"), in_=w1_src[:, :, :, 2 * a : 2 * a + 2])
-            cols = slice(2 * a * P, 2 * (a + 1) * P)
+        for pair, copy in enumerate((nc.scalar.copy, nc.vector.tensor_copy)):
+            w1_bf = keep.tile([P, 2, P, PACK], BF16, name=f"w1_bf{pair}", tag=f"w1_bf{pair}", align_bytes=64)
+            copy(out=w1_bf[:].rearrange("p t m j -> p m j t"), in_=w1_src[:, :, :, 2 * pair : 2 * pair + 2])
+            cols = slice(2 * pair * P, 2 * (pair + 1) * P)
             nc.vector.quantize_mx(
                 out=w1_code[:, cols].bitcast(FP8X4), scales=w1_scale[:, cols], in_=w1_bf[:].rearrange("p t m j -> p (t m j)")
             )
+
         for bank in range(4, 7):
-            warm = psum.tile([P, 2, half], F32, name=f"warm{bank}", tag=f"bank{bank}")
+            warm = psum.tile([P, 2, 2 * P], F32, name=f"warm{bank}", tag=f"bank{bank}")
             for a in range(2):
                 nc.tensor.matmul_mx(
                     out=warm[:, a, :],
-                    lhsT=w1_code[:, half : half + P].bitcast(FP8X4),
-                    lhsT_scale=w1_scale[:, half : half + P],
-                    rhs=w1_code[:, half:H].bitcast(FP8X4),
-                    rhs_scale=w1_scale[:, half:H],
+                    lhsT=w1_code[:, 2 * P : 3 * P].bitcast(FP8X4),
+                    lhsT_scale=w1_scale[:, 2 * P : 3 * P],
+                    rhs=w1_code[:, 2 * P : H].bitcast(FP8X4),
+                    rhs_scale=w1_scale[:, 2 * P : H],
                     start=True,
                     stop=True,
                 )
-        x_code = keep.tile([P, S], U32, name="x_code", tag="slot_c", align_bytes=64)
+
+        x_code = keep.tile([P, S], U32, name="x_code", tag="w1_bf0", align_bytes=64)
+        half = S // 2
         for a in range(2):
-            nc.vector.tensor_copy(x_code[:, a * half : (a + 1) * half], x_table[:].bitcast(U32).indirect(pick_halves[a]))
+            offsets = picks[:, a * half // LANES : (a + 1) * half // LANES]
+            nc.vector.tensor_copy(x_code[:, a * half : (a + 1) * half], x_table[:].bitcast(U32).indirect(offsets))
 
         def deal(rows, dealt):
             nc.vector.tensor_copy(out=dealt[:].rearrange("p (t m) -> p m t", t=PACK), in_=rows[:].rearrange("p (m t) -> p m t", t=PACK))
             return dealt
 
-        w2_code = deal(w2_rows, early.tile([P, N], I32, name="w2_code", offset=0, align_bytes=64))
-        w_scale = deal(w_scale_rows, early.tile([P, N], U8, name="w_scale", offset=4 * N, align_bytes=64))
+        w2_code = deal(w2_rows, table.tile([P, N], I32, name="w2_code", offset=0, align_bytes=64))
+        w_scale = deal(w_scale_rows, table.tile([P, N], U8, name="w_scale", offset=4 * N, align_bytes=64))
+        w2_scale = w_scale[:]
+        w3_scale = w_scale[PACK:P, :]
 
+        vector_quarter = 1
         h_code = keep.tile([P, S], U32, name="h_code", align_bytes=64)
         h_scale = keep.tile([P, S], U8, name="h_scale", align_bytes=64)
-        for q in range(4):
-            cols = slice(q * P, (q + 1) * P)
+        quarters = [slice(q * P, (q + 1) * P) for q in range(S // P)]
+        for q, cols in enumerate(quarters):
             h_sum = psum.tile([P, PACK, P], F32, name=f"h_sum{q}", tag=f"bank{q}")
             for t in range(PACK):
                 w_cols = slice(t * P, (t + 1) * P)
@@ -127,16 +134,13 @@ def tile_picked_zrandla_relu_po_kernel(
                     start=True,
                     stop=True,
                 )
-            h_bf = keep.tile([P, P, PACK], BF16, name=f"h_bf{q}", tag=f"slot_h{q}", align_bytes=64)
-            if q == 1:
+            h_bf = keep.tile([P, P, PACK], BF16, name=f"h_bf{q}", tag=f"h_bf{q}", align_bytes=64)
+            if q == vector_quarter:
                 nc.vector.tensor_scalar_max(out=h_bf[:], in0=h_sum[:].rearrange("p t n -> p n t"), scalar1=0.0)
             else:
                 nc.scalar.activation(out=h_bf[:], in_=h_sum[:].rearrange("p t n -> p n t"), func=ACT.Relu)
             nc.vector.quantize_mx(out=h_code[:, cols].bitcast(FP8X4), scales=h_scale[:, cols], in_=h_bf[:].rearrange("p n t -> p (n t)"))
-            if q == 3:
-                w3_code = deal(w3_rows, keep.tile([P, N], I32, name="w3_code", tag="slot_h3", align_bytes=64))
-        w2_scale = w_scale[:]
-        w3_scale = w_scale[PACK:P, :]
+        w3_code = deal(w3_rows, keep.tile([P, N], I32, name="w3_code", tag="h_bf3", align_bytes=64))
 
         def product(total, code, scale, t, cols):
             w_cols = slice(t * P, (t + 1) * P)
@@ -163,8 +167,7 @@ def tile_picked_zrandla_relu_po_kernel(
             product(y_sum[:], w3_code, w3_scale, t, slice(0, S))
             nc.scalar.copy(out=feature[t][:], in_=y_sum[:])
 
-        for q in range(4):
-            cols = slice(q * P, (q + 1) * P)
+        for q, cols in enumerate(quarters):
             s_part = psum.tile([P, P], F32, name=f"s_part{q}", tag=f"bank{PACK + q}")
             product(s_part[:], w2_code, w2_scale, 0, cols)
             nc.scalar.activation(out=score[0][:, cols], in_=s_part[:], func=ACT.Exp)
@@ -177,99 +180,99 @@ def tile_picked_zrandla_relu_po_kernel(
         result = keep.tile([P, PACK, V], F32, name="result", align_bytes=64)
         result_bf = keep.tile([P, V, PACK], BF16, name="result_bf", align_bytes=64)
         out_rows = out_0.rearrange("(p t) v -> p t v", t=PACK)
-
-        halves = V // P
+        groups = [slice(a * P, (a + 1) * P) for a in range(V // P)]
 
         def turned_sum(terms, name, bank):
-            total = psum.tile([P, halves, P], F32, name=name, tag=bank)
-            for a in range(halves):
-                for d in range(3):
+            total = psum.tile([P, len(groups), P], F32, name=name, tag=bank)
+            for a, cols in enumerate(groups):
+                for d in range(NEIGHBOURS):
                     nc.tensor.matmul(
-                        total[:, a, :], lhsT=terms[d][:, a * P : (a + 1) * P], rhs=identity[:],
-                        is_transpose=True, start=(d == 0), stop=(d == 2),
+                        total[:, a, :], lhsT=terms[d][:, cols], rhs=identity[:],
+                        is_transpose=True, start=(d == 0), stop=(d == NEIGHBOURS - 1),
                     )
             return total
 
-        def fetch_scores(t, root):
-            e_near = keep.tile([P, 3, V], F32, name=f"e_near{t}", tag=f"e_near{t}", align_bytes=64)
-            for d in range(3):
+        def by_neighbour(tile):
+            return [tile[:, d, :] for d in range(NEIGHBOURS)]
+
+        def invert(inv, root, den):
+            nc.scalar.activation(out=root, in_=den, func=ACT.Abs_reciprocal_sqrt)
+            nc.scalar.activation(out=inv, in_=root, func=ACT.Square)
+
+        def fetch_scores(t, bank, root_tile):
+            e_near = keep.tile([P, NEIGHBOURS, V], F32, name=f"e_near{t}", tag=f"e_near{t}", align_bytes=64)
+            for d in range(NEIGHBOURS):
                 nc.vector.tensor_copy(e_near[:, d, :], score[t][:].indirect(near[d][:]))
-            den = turned_sum(thirds(e_near), f"den{t}", f"bank{(7, 6, 5)[t]}")
-            inv = keep.tile([P, halves, P], F32, name=f"inv{t}", align_bytes=64)
-            root = root[:, 0:V].rearrange("p (a v) -> p a v", a=halves)
-            nc.scalar.activation(out=root, in_=den[:], func=ACT.Abs_reciprocal_sqrt)
-            nc.scalar.activation(out=inv[:], in_=root, func=ACT.Square)
+            den = turned_sum(by_neighbour(e_near), f"den{t}", bank)
+            inv = keep.tile([P, len(groups), P], F32, name=f"inv{t}", align_bytes=64)
+            invert(inv[:], root_tile[:, 0:V].rearrange("p (a v) -> p a v", a=len(groups)), den[:])
             return e_near, inv
 
-        def fetch_features(t, e_near, terms):
-            for d in range(3):
+        def fetch_features(t, bank, e_near, terms):
+            for d in range(NEIGHBOURS):
                 nc.vector.tensor_tensor(terms[d], feature[t][:].indirect(near[d][:]), e_near[:, d, :], ALU.mult)
-            return turned_sum(terms, f"num{t}", f"bank{(4, 1, 2)[t]}")
+            return turned_sum(terms, f"num{t}", bank)
 
-        def thirds(tile):
-            return [tile[:, d, :] for d in range(3)]
-
-        def finish(t, engine, num, inv, tag):
-            turned = keep.tile([P, halves, P], F32, name=f"turned{t}", tag=tag, align_bytes=64)
+        def finish(t, bank, engine, num, inv, tag):
+            turned = keep.tile([P, len(groups), P], F32, name=f"turned{t}", tag=tag, align_bytes=64)
             engine.tensor_tensor(turned[:], num[:], inv[:], ALU.mult)
-            back = psum.tile([P, halves, P], F32, name=f"back{t}", tag=f"bank{(0, 4, 5)[t]}")
-            for a in range(halves):
+            back = psum.tile([P, len(groups), P], F32, name=f"back{t}", tag=bank)
+            for a in range(len(groups)):
                 nc.tensor.transpose(back[:, a, :], turned[:, a, :], identity[:])
             nc.scalar.copy(out=result[:, t, :], in_=back[:].rearrange("p a v -> p (a v)"))
             nc.sync.dma_start(out=out_rows[:, t, :], in_=result[:, t, :])
-            if t == 1:
-                nc.scalar.copy(out=result_bf[:, :, 0:2], in_=result[:, 0:2, :].rearrange("p t v -> p v t"))
 
         last = PACK - 1
-        words = 4 * V
-        root0 = held.tile([P, 3 * V], F32, name="root0", offset=6 * words)
-        e0, inv0 = fetch_scores(0, root0)
+        root0 = shared.tile([P, 3 * V], F32, name="root0", offset=6 * ROW)
+        e0, inv0 = fetch_scores(0, "bank7", root0)
         make_features(3)
-        num0 = fetch_features(0, e0, thirds(keep.tile([P, 3, V], F32, name="ey_near0", align_bytes=64)))
-        num0_sb = held.tile([P, halves, P], F32, name="num0_sb", offset=8 * words)
-        nc.scalar.copy(out=num0_sb[:], in_=num0[:])
+        num0 = fetch_features(0, "bank4", e0, by_neighbour(keep.tile([P, NEIGHBOURS, V], F32, name="ey_near0", align_bytes=64)))
+        num0_sbuf = shared.tile([P, len(groups), P], F32, name="num0_sbuf", offset=8 * ROW)
+        nc.scalar.copy(out=num0_sbuf[:], in_=num0[:])
         make_features(2)
-        root1 = held.tile([P, 8 * V], F32, name="root1", offset=0)
-        e1, inv1 = fetch_scores(1, root1)
-        num1 = fetch_features(1, e1, thirds(keep.tile([P, 3, V], F32, name="ey_near1", align_bytes=64)))
+        root1 = shared.tile([P, 8 * V], F32, name="root1", offset=0)
+        e1, inv1 = fetch_scores(1, "bank6", root1)
+        num1 = fetch_features(1, "bank1", e1, by_neighbour(keep.tile([P, NEIGHBOURS, V], F32, name="ey_near1", align_bytes=64)))
+
         weighted = keep.tile([P, S], F32, name="weighted", tag="feature1", align_bytes=64)
         nc.gpsimd.tensor_tensor(weighted[:], feature[last][:], score[last][:], ALU.mult)
-        finish(0, nc.gpsimd, num0_sb, inv0, "e_near1")
-        root2 = held.tile([P, V], F32, name="root2", offset=6 * words)
-        e2, inv2 = fetch_scores(2, root2)
-        finish(1, nc.vector, num1, inv1, "turned1")
-        ey_first = keep.tile([P, 2, V], F32, name="ey_near2", align_bytes=64)
-        ey_last = held.tile([P, 2, V], F32, name="ey_last", offset=0)
-        num2 = fetch_features(2, e2, [ey_first[:, 0, :], ey_first[:, 1, :], ey_last[:, 0, :]])
-        den_a = held.tile([P, V], F32, name="den_a", offset=3 * words)
+        finish(0, "bank0", nc.gpsimd, num0_sbuf, inv0, "e_near1")
+
+        root2 = shared.tile([P, V], F32, name="root2", offset=6 * ROW)
+        e2, inv2 = fetch_scores(2, "bank5", root2)
+        finish(1, "bank4", nc.vector, num1, inv1, "turned1")
+        nc.scalar.copy(out=result_bf[:, :, 0:2], in_=result[:, 0:2, :].rearrange("p t v -> p v t"))
+        ey_first = keep.tile([P, 2, V], F32, name="ey_first", align_bytes=64)
+        ey_last = shared.tile([P, 2, V], F32, name="ey_last", offset=0)
+        num2 = fetch_features(2, "bank2", e2, [ey_first[:, 0, :], ey_first[:, 1, :], ey_last[:, 0, :]])
+
+        den_a = shared.tile([P, V], F32, name="den_a", offset=3 * ROW)
         den_b = keep.tile([P, V], F32, name="den_b", align_bytes=64)
-        den_c = held.tile([P, V], F32, name="den_c", offset=words)
-        num_a = held.tile([P, V], F32, name="num_a", offset=4 * words)
+        den_c = shared.tile([P, V], F32, name="den_c", offset=ROW)
+        num_a = shared.tile([P, V], F32, name="num_a", offset=4 * ROW)
         nc.vector.tensor_copy(den_a[:], score[last][:].indirect(near[0][:]))
         nc.vector.tensor_copy(num_a[:], weighted[:].indirect(near[0][:]))
         nc.vector.tensor_tensor(den_b[:], score[last][:].indirect(near[1][:]), den_a[:], ALU.add)
-        finish(2, nc.vector, num2, inv2, "turned2")
+        finish(2, "bank5", nc.vector, num2, inv2, "turned2")
         nc.vector.tensor_tensor(den_c[:], score[last][:].indirect(near[2][:]), den_b[:], ALU.add)
-        root = held.tile([P, V], F32, name="root3", offset=6 * words)
-        inv = keep.tile([P, V], F32, name="inv3", align_bytes=64)
-        nc.scalar.activation(out=root[:], in_=den_c[:], func=ACT.Abs_reciprocal_sqrt)
-        nc.scalar.activation(out=inv[:], in_=root[:], func=ACT.Square)
+        root3 = shared.tile([P, V], F32, name="root3", offset=6 * ROW)
+        inv3 = keep.tile([P, V], F32, name="inv3", align_bytes=64)
+        invert(inv3[:], root3[:], den_c[:])
 
         out_code = keep.tile([P, V], U32, name="out_code", align_bytes=64)
         out_scale = keep.tile([P, V], U8, name="out_scale", align_bytes=64)
-        num_b = held.tile([P, V], F32, name="num_b", offset=0)
+        num_b = shared.tile([P, V], F32, name="num_b", offset=0)
         num_c = keep.tile([P, V], F32, name="num_c", align_bytes=64)
-        parts = [slice(a * P, (a + 1) * P) for a in range(halves)]
         for d, before, total in ((1, num_a, num_b), (2, num_b, num_c)):
-            for a, cols in enumerate(parts):
+            for a, cols in enumerate(groups):
                 offsets = near[d][:, a * P // LANES : (a + 1) * P // LANES]
                 nc.vector.tensor_tensor(total[:, cols], weighted[:].indirect(offsets), before[:, cols], ALU.add)
-        for cols in parts:
-            nc.vector.tensor_tensor(result[:, last, cols], num_c[:, cols], inv[:, cols], ALU.mult)
+        for cols in groups:
+            nc.vector.tensor_tensor(result[:, last, cols], num_c[:, cols], inv3[:, cols], ALU.mult)
         nc.sync.dma_start(out=out_rows[:, last, :], in_=result[:, last, :])
-        for copy, cols in zip((nc.scalar.copy, nc.vector.tensor_copy), parts):
-            copy(out=result_bf[:, cols, 2:4], in_=result[:, 2:4, cols].rearrange("p t v -> p v t"))
-        for cols in parts:
+        for cols in groups:
+            nc.vector.tensor_copy(out=result_bf[:, cols, 2:4], in_=result[:, 2:4, cols].rearrange("p t v -> p v t"))
+        for cols in groups:
             nc.vector.quantize_mx(
                 out=out_code[:, cols].bitcast(FP8X4), scales=out_scale[:, cols], in_=result_bf[:, cols, :].rearrange("p v t -> p (v t)")
             )

@@ -89,19 +89,6 @@ def tile_picked_zrandla_relu_po_kernel(
                 out=w1_code[:, cols].bitcast(FP8X4), scales=w1_scale[:, cols], in_=w1_bf[:].rearrange("p t m j -> p (t m j)")
             )
 
-        for bank in range(4, 7):
-            warm = psum.tile([P, 2, 2 * P], F32, name=f"warm{bank}", tag=f"bank{bank}")
-            for a in range(2):
-                nc.tensor.matmul_mx(
-                    out=warm[:, a, :],
-                    lhsT=w1_code[:, 2 * P : 3 * P].bitcast(FP8X4),
-                    lhsT_scale=w1_scale[:, 2 * P : 3 * P],
-                    rhs=w1_code[:, 2 * P : H].bitcast(FP8X4),
-                    rhs_scale=w1_scale[:, 2 * P : H],
-                    start=True,
-                    stop=True,
-                )
-
         x_code = keep.tile([P, S], U32, name="x_code", tag="w1_bf0", align_bytes=64)
         half = S // 2
         for a in range(2):

@@ -41,7 +41,6 @@ def tile_picked_zrandla_relu_po_kernel(
     with ExitStack() as ctx:
         lists = ctx.enter_context(tc.tile_pool(name="lists", bufs=1))
         keep = ctx.enter_context(tc.tile_pool(name="keep", bufs=1))
-        shared = ctx.enter_context(tc.tile_pool(name="shared", bufs=1))
         table = ctx.enter_context(tc.tile_pool(name="table", bufs=1))
         psum = ctx.enter_context(tc.psum_pool(name="psum", bufs=1))
 
@@ -105,8 +104,8 @@ def tile_picked_zrandla_relu_po_kernel(
         w3_scale = w_scale[PACK:P, :]
 
         vector_quarter = 1
-        h_code = keep.tile([P, S], U32, name="h_code", align_bytes=64)
-        h_scale = keep.tile([P, S], U8, name="h_scale", align_bytes=64)
+        h_code = keep.tile([P, S], U32, name="h_code", tag="h_code", align_bytes=64)
+        h_scale = keep.tile([P, S], U8, name="h_scale", tag="h_scale", align_bytes=64)
         quarters = [slice(q * P, (q + 1) * P) for q in range(S // P)]
         for q, cols in enumerate(quarters):
             h_sum = psum.tile([P, PACK, P], F32, name=f"h_sum{q}", tag=f"bank{q}")
@@ -127,7 +126,7 @@ def tile_picked_zrandla_relu_po_kernel(
             else:
                 nc.scalar.activation(out=h_bf[:], in_=h_sum[:].rearrange("p t n -> p n t"), func=ACT.Relu)
             nc.vector.quantize_mx(out=h_code[:, cols].bitcast(FP8X4), scales=h_scale[:, cols], in_=h_bf[:].rearrange("p n t -> p (n t)"))
-        w3_code = deal(w3_rows, keep.tile([P, N], I32, name="w3_code", tag="h_bf3", align_bytes=64))
+        w3_code = deal(w3_rows, keep.tile([P, N], I32, name="w3_code", tag="h_bf2", align_bytes=64))
 
         def product(total, code, scale, t, cols):
             w_cols = slice(t * P, (t + 1) * P)
@@ -149,111 +148,98 @@ def tile_picked_zrandla_relu_po_kernel(
             product(s_sum[:], w2_code, w2_scale, t, slice(0, S))
             nc.scalar.activation(out=score[t][:], in_=s_sum[:], func=ACT.Exp)
 
-        def make_features(t):
-            y_sum = psum.tile([P, S], F32, name=f"y_sum{t}", tag=f"bank{t}")
+        weighted = [keep.tile([P, S], F32, name=f"weighted{t}", align_bytes=64) for t in range(PACK)]
+
+        def make_features(t, bank):
+            y_sum = psum.tile([P, S], F32, name=f"y_sum{t}", tag=bank)
             product(y_sum[:], w3_code, w3_scale, t, slice(0, S))
             nc.scalar.copy(out=feature[t][:], in_=y_sum[:])
+            nc.gpsimd.tensor_tensor(weighted[t][:], feature[t][:], score[t][:], ALU.mult)
 
         for q, cols in enumerate(quarters):
             s_part = psum.tile([P, P], F32, name=f"s_part{q}", tag=f"bank{PACK + q}")
             product(s_part[:], w2_code, w2_scale, 0, cols)
             nc.scalar.activation(out=score[0][:, cols], in_=s_part[:], func=ACT.Exp)
-        make_features(0)
-        make_scores(1, "bank7")
-        make_features(1)
-        make_scores(2, "bank0")
-        make_scores(3, "bank7")
+        make_features(0, "bank0")
+        make_scores(1, "bank1")
+        make_features(1, "bank2")
+        make_scores(2, "bank4")
+        make_features(2, "bank5")
+        make_scores(3, "bank6")
+        make_features(3, "bank7")
 
         result = keep.tile([P, PACK, V], F32, name="result", align_bytes=64)
         result_bf = keep.tile([P, V, PACK], BF16, name="result_bf", align_bytes=64)
         out_rows = out_0.rearrange("(p t) v -> p t v", t=PACK)
         groups = [slice(a * P, (a + 1) * P) for a in range(V // P)]
 
+        def add_turned(total, term, d):
+            nc.tensor.matmul(total, lhsT=term, rhs=identity[:], is_transpose=True, start=(d == 0), stop=(d == NEIGHBOURS - 1))
+
         def turned_sum(terms, name, bank):
             total = psum.tile([P, len(groups), P], F32, name=name, tag=bank)
             for a, cols in enumerate(groups):
                 for d in range(NEIGHBOURS):
-                    nc.tensor.matmul(
-                        total[:, a, :], lhsT=terms[d][:, cols], rhs=identity[:],
-                        is_transpose=True, start=(d == 0), stop=(d == NEIGHBOURS - 1),
-                    )
+                    add_turned(total[:, a, :], terms[:, d, cols], d)
             return total
 
-        def by_neighbour(tile):
-            return [tile[:, d, :] for d in range(NEIGHBOURS)]
-
-        def invert(inv, root, den):
-            nc.scalar.activation(out=root, in_=den, func=ACT.Abs_reciprocal_sqrt)
-            nc.scalar.activation(out=inv, in_=root, func=ACT.Square)
-
-        def fetch_scores(t, bank, root_tile):
-            e_near = keep.tile([P, NEIGHBOURS, V], F32, name=f"e_near{t}", tag=f"e_near{t}", align_bytes=64)
-            for d in range(NEIGHBOURS):
-                nc.vector.tensor_copy(e_near[:, d, :], score[t][:].indirect(near[d][:]))
-            den = turned_sum(by_neighbour(e_near), f"den{t}", bank)
-            inv = keep.tile([P, len(groups), P], F32, name=f"inv{t}", align_bytes=64)
-            invert(inv[:], root_tile[:, 0:V].rearrange("p (a v) -> p a v", a=len(groups)), den[:])
-            return e_near, inv
-
-        def fetch_features(t, bank, e_near, terms):
-            for d in range(NEIGHBOURS):
-                nc.vector.tensor_tensor(terms[d], feature[t][:].indirect(near[d][:]), e_near[:, d, :], ALU.mult)
-            return turned_sum(terms, f"num{t}", bank)
-
-        def finish(t, bank, engine, num, inv, tag):
-            turned = keep.tile([P, len(groups), P], F32, name=f"turned{t}", tag=tag, align_bytes=64)
-            engine.tensor_tensor(turned[:], num[:], inv[:], ALU.mult)
-            back = psum.tile([P, len(groups), P], F32, name=f"back{t}", tag=bank)
+        def turn_back(turned, name, bank):
+            back = psum.tile([P, len(groups), P], F32, name=name, tag=bank)
             for a in range(len(groups)):
                 nc.tensor.transpose(back[:, a, :], turned[:, a, :], identity[:])
-            nc.scalar.copy(out=result[:, t, :], in_=back[:].rearrange("p a v -> p (a v)"))
-            nc.sync.dma_start(out=out_rows[:, t, :], in_=result[:, t, :])
+            return back[:].rearrange("p a v -> p (a v)")
+
+        e_near = []
+        for t in range(PACK):
+            e_near.append(keep.tile([P, NEIGHBOURS, V], F32, name=f"e_near{t}", tag=f"e_near{t}", align_bytes=64))
+            for d in range(NEIGHBOURS):
+                nc.vector.tensor_copy(e_near[t][:, d, :], score[t][:].indirect(near[d][:]))
+
+        inv = [keep.tile([P, V], F32, name=f"inv{t}", align_bytes=64) for t in range(PACK)]
+        for t in range(PACK):
+            den = turned_sum(e_near[t], f"den{t}", ("bank3", "bank2", "bank4", "bank1")[t])
+            root = keep.tile([P, len(groups), P], F32, name=f"root{t}", tag=("h_code", "h_scale", "h_bf2", "root3")[t], align_bytes=64)
+            nc.scalar.activation(out=root[:], in_=den[:], func=ACT.Abs_reciprocal_sqrt)
+            nc.scalar.activation(out=inv[t][:], in_=turn_back(root, f"root_back{t}", ("bank0", "bank1", "bank5", "bank6")[t]), func=ACT.Square)
 
         last = PACK - 1
-        root0 = shared.tile([P, 3 * V], F32, name="root0", offset=6 * ROW)
-        e0, inv0 = fetch_scores(0, "bank7", root0)
-        make_features(3)
-        num0 = fetch_features(0, "bank4", e0, by_neighbour(keep.tile([P, NEIGHBOURS, V], F32, name="ey_near0", align_bytes=64)))
-        num0_sbuf = shared.tile([P, len(groups), P], F32, name="num0_sbuf", offset=8 * ROW)
-        nc.scalar.copy(out=num0_sbuf[:], in_=num0[:])
-        make_features(2)
-        root1 = shared.tile([P, 8 * V], F32, name="root1", offset=0)
-        e1, inv1 = fetch_scores(1, "bank6", root1)
-        num1 = fetch_features(1, "bank1", e1, by_neighbour(keep.tile([P, NEIGHBOURS, V], F32, name="ey_near1", align_bytes=64)))
+        for t in range(last):
+            terms = keep.tile([P, NEIGHBOURS, V], F32, name=f"terms{t}", tag=f"terms{t}", align_bytes=64)
+            for d in range(NEIGHBOURS):
+                nc.vector.tensor_tensor(terms[:, d, :], weighted[t][:].indirect(near[d][:]), inv[t][:], ALU.mult)
+            if t < last - 1:
+                total = turned_sum(terms, f"total{t}", ("bank7", "bank3")[t])
+                turned = keep.tile([P, len(groups), P], F32, name=f"turned{t}", align_bytes=64)
+                nc.scalar.copy(out=turned[:], in_=total[:])
+                nc.scalar.copy(out=result[:, t, :], in_=turn_back(turned, f"back{t}", ("bank0", "bank2")[t]))
+            else:
+                parts = [psum.tile([P, P], F32, name=f"part{a}", tag=f"bank{4 + a}") for a in range(len(groups))]
+                for d in range(NEIGHBOURS):
+                    for a, cols in enumerate(groups):
+                        add_turned(parts[a][:], terms[:, d, cols], d)
+                for a, cols in enumerate(groups):
+                    turned = keep.tile([P, P], F32, name=f"turned_part{a}", align_bytes=64)
+                    nc.scalar.copy(out=turned[:], in_=parts[a][:])
+                    back = psum.tile([P, P], F32, name=f"back_part{a}", tag=f"bank{6 + a}")
+                    nc.tensor.transpose(back[:], turned[:], identity[:])
+                    nc.scalar.copy(out=result[:, t, cols], in_=back[:])
+            nc.sync.dma_start(out=out_rows[:, t, :], in_=result[:, t, :])
+            if t == 1:
+                nc.scalar.copy(out=result_bf[:, :, 0:2], in_=result[:, 0:2, :].rearrange("p t v -> p v t"))
 
-        weighted = keep.tile([P, S], F32, name="weighted", tag="feature1", align_bytes=64)
-        nc.gpsimd.tensor_tensor(weighted[:], feature[last][:], score[last][:], ALU.mult)
-        finish(0, "bank0", nc.gpsimd, num0_sbuf, inv0, "e_near1")
-
-        root2 = shared.tile([P, V], F32, name="root2", offset=6 * ROW)
-        e2, inv2 = fetch_scores(2, "bank5", root2)
-        finish(1, "bank4", nc.vector, num1, inv1, "turned1")
-        nc.scalar.copy(out=result_bf[:, :, 0:2], in_=result[:, 0:2, :].rearrange("p t v -> p v t"))
-        ey_first = keep.tile([P, 2, V], F32, name="ey_first", align_bytes=64)
-        ey_last = shared.tile([P, 2, V], F32, name="ey_last", offset=0)
-        num2 = fetch_features(2, "bank2", e2, [ey_first[:, 0, :], ey_first[:, 1, :], ey_last[:, 0, :]])
-
-        den_a = shared.tile([P, V], F32, name="den_a", offset=3 * ROW)
-        den_b = keep.tile([P, V], F32, name="den_b", align_bytes=64)
-        den_c = shared.tile([P, V], F32, name="den_c", offset=ROW)
-        num_a = shared.tile([P, V], F32, name="num_a", offset=4 * ROW)
-        nc.vector.tensor_copy(den_a[:], score[last][:].indirect(near[0][:]))
-        nc.vector.tensor_copy(num_a[:], weighted[:].indirect(near[0][:]))
-        nc.vector.tensor_tensor(den_b[:], score[last][:].indirect(near[1][:]), den_a[:], ALU.add)
-        finish(2, "bank5", nc.vector, num2, inv2, "turned2")
-        nc.vector.tensor_tensor(den_c[:], score[last][:].indirect(near[2][:]), den_b[:], ALU.add)
-        root3 = shared.tile([P, V], F32, name="root3", offset=6 * ROW)
-        inv3 = keep.tile([P, V], F32, name="inv3", align_bytes=64)
-        invert(inv3[:], root3[:], den_c[:])
+        num_a = keep.tile([P, V], F32, name="num_a", tag="terms1", align_bytes=64)
+        for a, cols in enumerate(groups):
+            nc.vector.tensor_copy(num_a[:, cols], weighted[last][:].indirect(near[0][:, a * P // LANES : (a + 1) * P // LANES]))
+        inv3 = inv[last]
 
         out_code = keep.tile([P, V], U32, name="out_code", align_bytes=64)
         out_scale = keep.tile([P, V], U8, name="out_scale", align_bytes=64)
-        num_b = shared.tile([P, V], F32, name="num_b", offset=0)
+        num_b = keep.tile([P, V], F32, name="num_b", align_bytes=64)
         num_c = keep.tile([P, V], F32, name="num_c", align_bytes=64)
         for d, before, total in ((1, num_a, num_b), (2, num_b, num_c)):
             for a, cols in enumerate(groups):
                 offsets = near[d][:, a * P // LANES : (a + 1) * P // LANES]
-                nc.vector.tensor_tensor(total[:, cols], weighted[:].indirect(offsets), before[:, cols], ALU.add)
+                nc.vector.tensor_tensor(total[:, cols], weighted[last][:].indirect(offsets), before[:, cols], ALU.add)
         for cols in groups:
             nc.vector.tensor_tensor(result[:, last, cols], num_c[:, cols], inv3[:, cols], ALU.mult)
         nc.sync.dma_start(out=out_rows[:, last, :], in_=result[:, last, :])

@@ -88,6 +88,18 @@ def tile_picked_zrandla_relu_po_kernel(
                 out=w1_code[:, cols].bitcast(FP8X4), scales=w1_scale[:, cols], in_=w1_bf[:].rearrange("p t m j -> p (t m j)")
             )
 
+        warm = psum.tile([P, 2 * P], F32, name="warm", tag="bank7")
+        for k in range(4):
+            nc.tensor.matmul_mx(
+                out=warm[:],
+                lhsT=w1_code[:, 2 * P : 3 * P].bitcast(FP8X4),
+                lhsT_scale=w1_scale[:, 2 * P : 3 * P],
+                rhs=w1_code[:, 2 * P : 4 * P].bitcast(FP8X4),
+                rhs_scale=w1_scale[:, 2 * P : 4 * P],
+                start=True,
+                stop=True,
+            )
+
         x_code = keep.tile([P, S], U32, name="x_code", tag="w1_bf0", align_bytes=64)
         half = S // 2
         for a in range(2):

@@ -110,8 +110,10 @@ def tile_picked_zrandla_relu_po_kernel(
             nc.vector.tensor_copy(out=dealt[:].rearrange("p (t m) -> p m t", t=PACK), in_=rows[:].rearrange("p (m t) -> p m t", t=PACK))
             return dealt
 
-        w2_code = deal(w2_rows, table.tile([P, N], I32, name="w2_code", offset=0, align_bytes=64))
-        w_scale = deal(w_scale_rows, table.tile([P, N], U8, name="w_scale", offset=4 * N, align_bytes=64))
+        w2_code = keep.tile([P, N], U32, name="w2_code", align_bytes=64)
+        nc.scalar.copy(out=w2_code[:].rearrange("p (t m) -> p m t", t=PACK), in_=w2_rows[:].bitcast(U32).rearrange("p (m t) -> p m t", t=PACK))
+        w_scale = table.tile([P, N], U8, name="w_scale", offset=0, align_bytes=64)
+        nc.vector.tensor_copy(out=w_scale[:].rearrange("p (t m) -> p t m", t=PACK), in_=w_scale_rows[:].rearrange("p (m t) -> p t m", t=PACK))
         w2_scale = w_scale[:]
         w3_scale = w_scale[PACK:P, :]
 
@@ -215,31 +217,42 @@ def tile_picked_zrandla_relu_po_kernel(
             nc.scalar.activation(out=inv[t][:], in_=turn_back(root, f"root_back{t}", ("bank0", "bank1", "bank5", "bank6")[t]), func=ACT.Square)
 
         last = PACK - 1
-        for t in range(last):
-            terms = keep.tile([P, NEIGHBOURS, V], F32, name=f"terms{t}", tag=f"terms{t}", align_bytes=64)
-            for d in range(NEIGHBOURS):
-                nc.vector.tensor_tensor(terms[:, d, :], weighted[t][:].indirect(near[d][:]), inv[t][:], ALU.mult)
-            if t < last - 1:
-                total = turned_sum(terms, f"total{t}", ("bank7", "bank3")[t])
-                turned = keep.tile([P, len(groups), P], F32, name=f"turned{t}", align_bytes=64)
-                nc.scalar.copy(out=turned[:], in_=total[:])
-                nc.scalar.copy(out=result[:, t, :], in_=turn_back(turned, f"back{t}", ("bank0", "bank2")[t]))
-            else:
-                parts = [psum.tile([P, P], F32, name=f"part{a}", tag=f"bank{4 + a}") for a in range(len(groups))]
-                for d in range(NEIGHBOURS):
-                    for a, cols in enumerate(groups):
-                        add_turned(parts[a][:], terms[:, d, cols], d)
-                for a, cols in enumerate(groups):
-                    turned = keep.tile([P, P], F32, name=f"turned_part{a}", align_bytes=64)
-                    nc.scalar.copy(out=turned[:], in_=parts[a][:])
-                    back = psum.tile([P, P], F32, name=f"back_part{a}", tag=f"bank{6 + a}")
-                    nc.tensor.transpose(back[:], turned[:], identity[:])
-                    nc.scalar.copy(out=result[:, t, cols], in_=back[:])
-            nc.sync.dma_start(out=out_rows[:, t, :], in_=result[:, t, :])
-            if t == 1:
-                nc.scalar.copy(out=result_bf[:, :, 0:2], in_=result[:, 0:2, :].rearrange("p t v -> p v t"))
+        sums = [keep.tile([P, V], F32, name=f"sum{d}", tag=("sum0", "h_bf2", "sum2")[d], align_bytes=64) for d in range(NEIGHBOURS)]
+        nc.vector.tensor_copy(sums[0][:], weighted[2][:].indirect(near[0][:]))
 
-        num_a = keep.tile([P, V], F32, name="num_a", tag="terms1", align_bytes=64)
+        terms = keep.tile([P, NEIGHBOURS, V], F32, name="terms0", tag="terms0", align_bytes=64)
+        for d in range(NEIGHBOURS):
+            nc.vector.tensor_tensor(terms[:, d, :], weighted[0][:].indirect(near[d][:]), inv[0][:], ALU.mult)
+        total = turned_sum(terms, "total0", "bank7")
+        turned = keep.tile([P, len(groups), P], F32, name="turned0", align_bytes=64)
+        nc.scalar.copy(out=turned[:], in_=total[:])
+        nc.scalar.copy(out=result[:, 0, :], in_=turn_back(turned, "back0", "bank0"))
+        nc.sync.dma_start(out=out_rows[:, 0, :], in_=result[:, 0, :])
+
+        terms = keep.tile([P, NEIGHBOURS, V], F32, name="terms1", align_bytes=64)
+        for d in range(NEIGHBOURS):
+            nc.vector.tensor_tensor(terms[:, d, :], weighted[1][:].indirect(near[d][:]), inv[1][:], ALU.mult)
+            if d > 0:
+                nc.vector.tensor_tensor(sums[d][:], weighted[2][:].indirect(near[d][:]), sums[d - 1][:], ALU.add)
+        nc.gpsimd.tensor_tensor(result[:, 2, :], sums[2][:], inv[2][:], ALU.mult)
+        nc.sync.dma_start(out=out_rows[:, 2, :], in_=result[:, 2, :])
+        parts = [psum.tile([P, P], F32, name=f"part{a}", tag=f"bank{4 + a}") for a in range(len(groups))]
+        for d in range(NEIGHBOURS):
+            for a, cols in enumerate(groups):
+                add_turned(parts[a][:], terms[:, d, cols], d)
+        backs = []
+        for a, cols in enumerate(groups):
+            turned = keep.tile([P, P], F32, name=f"turned_part{a}", align_bytes=64)
+            nc.scalar.copy(out=turned[:], in_=parts[a][:])
+            backs.append(psum.tile([P, P], F32, name=f"back_part{a}", tag=f"bank{2 + a}"))
+            nc.tensor.transpose(backs[a][:], turned[:], identity[:])
+        for a, cols in enumerate(groups):
+            nc.scalar.copy(out=result[:, 1, cols], in_=backs[a][:])
+        for a, cols in enumerate(groups):
+            nc.scalar.copy(out=result_bf[:, cols, 0:2], in_=result[:, 0:2, cols].rearrange("p t v -> p v t"))
+        nc.sync.dma_start(out=out_rows[:, 1, :], in_=result[:, 1, :])
+
+        num_a = keep.tile([P, V], F32, name="num_a", tag="terms0", align_bytes=64)
         for a, cols in enumerate(groups):
             nc.vector.tensor_copy(num_a[:, cols], weighted[last][:].indirect(near[0][:, a * P // LANES : (a + 1) * P // LANES]))
         inv3 = inv[last]

@@ -21,7 +21,6 @@ PACK = 4
 QUAD = 32
 LANES = 16
 NEIGHBOURS = 3
-ROW = 4 * V
 
 
 def load_scale_rows(queues, tile, scales, first):
@@ -88,32 +87,21 @@ def tile_picked_zrandla_relu_po_kernel(
                 out=w1_code[:, cols].bitcast(FP8X4), scales=w1_scale[:, cols], in_=w1_bf[:].rearrange("p t m j -> p (t m j)")
             )
 
-        warm = psum.tile([P, 2 * P], F32, name="warm", tag="bank7")
-        for k in range(4):
-            nc.tensor.matmul_mx(
-                out=warm[:],
-                lhsT=w1_code[:, 2 * P : 3 * P].bitcast(FP8X4),
-                lhsT_scale=w1_scale[:, 2 * P : 3 * P],
-                rhs=w1_code[:, 2 * P : 4 * P].bitcast(FP8X4),
-                rhs_scale=w1_scale[:, 2 * P : 4 * P],
-                start=True,
-                stop=True,
-            )
-
         x_code = keep.tile([P, S], U32, name="x_code", tag="w1_bf0", align_bytes=64)
         half = S // 2
         for a in range(2):
             offsets = picks[:, a * half // LANES : (a + 1) * half // LANES]
             nc.vector.tensor_copy(x_code[:, a * half : (a + 1) * half], x_table[:].bitcast(U32).indirect(offsets))
 
-        def deal(rows, dealt):
-            nc.vector.tensor_copy(out=dealt[:].rearrange("p (t m) -> p m t", t=PACK), in_=rows[:].rearrange("p (m t) -> p m t", t=PACK))
-            return dealt
+        def deal_words(copy, rows, dealt):
+            copy(out=dealt.rearrange("p (t m) -> p m t", t=PACK), in_=rows.rearrange("p (m t) -> p m t", t=PACK))
 
         w2_code = keep.tile([P, N], U32, name="w2_code", align_bytes=64)
-        nc.scalar.copy(out=w2_code[:].rearrange("p (t m) -> p m t", t=PACK), in_=w2_rows[:].bitcast(U32).rearrange("p (m t) -> p m t", t=PACK))
+        deal_words(nc.scalar.copy, w2_rows[:].bitcast(U32), w2_code[:])
         w_scale = table.tile([P, N], U8, name="w_scale", offset=0, align_bytes=64)
-        nc.vector.tensor_copy(out=w_scale[:].rearrange("p (t m) -> p t m", t=PACK), in_=w_scale_rows[:].rearrange("p (m t) -> p t m", t=PACK))
+        nc.vector.tensor_copy(
+            out=w_scale[:].rearrange("p (t m) -> p t m", t=PACK), in_=w_scale_rows[:].rearrange("p (m t) -> p t m", t=PACK)
+        )
         w2_scale = w_scale[:]
         w3_scale = w_scale[PACK:P, :]
 
@@ -140,7 +128,8 @@ def tile_picked_zrandla_relu_po_kernel(
             else:
                 nc.scalar.activation(out=h_bf[:], in_=h_sum[:].rearrange("p t n -> p n t"), func=ACT.Relu)
             nc.vector.quantize_mx(out=h_code[:, cols].bitcast(FP8X4), scales=h_scale[:, cols], in_=h_bf[:].rearrange("p n t -> p (n t)"))
-        w3_code = deal(w3_rows, keep.tile([P, N], I32, name="w3_code", tag="h_bf2", align_bytes=64))
+        w3_code = keep.tile([P, N], I32, name="w3_code", tag="h_bf2", align_bytes=64)
+        deal_words(nc.vector.tensor_copy, w3_rows[:], w3_code[:])
 
         def product(total, code, scale, t, cols):
             w_cols = slice(t * P, (t + 1) * P)
@@ -155,14 +144,13 @@ def tile_picked_zrandla_relu_po_kernel(
             )
 
         score = [keep.tile([P, S], F32, name=f"score{t}", align_bytes=64) for t in range(PACK)]
-        feature = [keep.tile([P, S], F32, name=f"feature{t}", tag=f"feature{t}", align_bytes=64) for t in range(PACK)]
+        feature = [keep.tile([P, S], F32, name=f"feature{t}", align_bytes=64) for t in range(PACK)]
+        weighted = [keep.tile([P, S], F32, name=f"weighted{t}", align_bytes=64) for t in range(PACK)]
 
         def make_scores(t, bank):
             s_sum = psum.tile([P, S], F32, name=f"s_sum{t}", tag=bank)
             product(s_sum[:], w2_code, w2_scale, t, slice(0, S))
             nc.scalar.activation(out=score[t][:], in_=s_sum[:], func=ACT.Exp)
-
-        weighted = [keep.tile([P, S], F32, name=f"weighted{t}", align_bytes=64) for t in range(PACK)]
 
         def make_features(t, bank):
             y_sum = psum.tile([P, S], F32, name=f"y_sum{t}", tag=bank)
@@ -187,21 +175,10 @@ def tile_picked_zrandla_relu_po_kernel(
         out_rows = out_0.rearrange("(p t) v -> p t v", t=PACK)
         groups = [slice(a * P, (a + 1) * P) for a in range(V // P)]
 
-        def add_turned(total, term, d):
-            nc.tensor.matmul(total, lhsT=term, rhs=identity[:], is_transpose=True, start=(d == 0), stop=(d == NEIGHBOURS - 1))
-
-        def turned_sum(terms, name, bank):
-            total = psum.tile([P, len(groups), P], F32, name=name, tag=bank)
-            for a, cols in enumerate(groups):
-                for d in range(NEIGHBOURS):
-                    add_turned(total[:, a, :], terms[:, d, cols], d)
-            return total
-
-        def turn_back(turned, name, bank):
-            back = psum.tile([P, len(groups), P], F32, name=name, tag=bank)
-            for a in range(len(groups)):
-                nc.tensor.transpose(back[:, a, :], turned[:, a, :], identity[:])
-            return back[:].rearrange("p a v -> p (a v)")
+        def add_turned(total, terms, d, cols):
+            nc.tensor.matmul(
+                total, lhsT=terms[:, d, cols], rhs=identity[:], is_transpose=True, start=(d == 0), stop=(d == NEIGHBOURS - 1)
+            )
 
         e_near = []
         for t in range(PACK):
@@ -209,67 +186,76 @@ def tile_picked_zrandla_relu_po_kernel(
             for d in range(NEIGHBOURS):
                 nc.vector.tensor_copy(e_near[t][:, d, :], score[t][:].indirect(near[d][:]))
 
+        den_banks = ("bank3", "bank2", "bank4", "bank1")
+        root_tags = ("h_code", "h_scale", "h_bf2", "root3")
+        root_banks = ("bank0", "bank1", "bank5", "bank6")
         inv = [keep.tile([P, V], F32, name=f"inv{t}", align_bytes=64) for t in range(PACK)]
         for t in range(PACK):
-            den = turned_sum(e_near[t], f"den{t}", ("bank3", "bank2", "bank4", "bank1")[t])
-            root = keep.tile([P, len(groups), P], F32, name=f"root{t}", tag=("h_code", "h_scale", "h_bf2", "root3")[t], align_bytes=64)
+            den = psum.tile([P, len(groups), P], F32, name=f"den{t}", tag=den_banks[t])
+            for a, cols in enumerate(groups):
+                for d in range(NEIGHBOURS):
+                    add_turned(den[:, a, :], e_near[t], d, cols)
+            root = keep.tile([P, len(groups), P], F32, name=f"root{t}", tag=root_tags[t], align_bytes=64)
             nc.scalar.activation(out=root[:], in_=den[:], func=ACT.Abs_reciprocal_sqrt)
-            nc.scalar.activation(out=inv[t][:], in_=turn_back(root, f"root_back{t}", ("bank0", "bank1", "bank5", "bank6")[t]), func=ACT.Square)
+            root_back = psum.tile([P, len(groups), P], F32, name=f"root_back{t}", tag=root_banks[t])
+            for a in range(len(groups)):
+                nc.tensor.transpose(root_back[:, a, :], root[:, a, :], identity[:])
+            nc.scalar.activation(out=inv[t][:], in_=root_back[:].rearrange("p a v -> p (a v)"), func=ACT.Square)
 
-        last = PACK - 1
-        sums = [keep.tile([P, V], F32, name=f"sum{d}", tag=("sum0", "h_bf2", "sum2")[d], align_bytes=64) for d in range(NEIGHBOURS)]
-        nc.vector.tensor_copy(sums[0][:], weighted[2][:].indirect(near[0][:]))
+        def add_and_turn_back(t, terms, sum_banks, back_banks):
+            totals = [psum.tile([P, P], F32, name=f"total{t}{a}", tag=bank) for a, bank in enumerate(sum_banks)]
+            for d in range(NEIGHBOURS):
+                for a, cols in enumerate(groups):
+                    add_turned(totals[a][:], terms, d, cols)
+            backs = []
+            for a in range(len(groups)):
+                turned = keep.tile([P, P], F32, name=f"turned{t}{a}", align_bytes=64)
+                nc.scalar.copy(out=turned[:], in_=totals[a][:])
+                backs.append(psum.tile([P, P], F32, name=f"back{t}{a}", tag=back_banks[a]))
+                nc.tensor.transpose(backs[a][:], turned[:], identity[:])
+            for a, cols in enumerate(groups):
+                nc.scalar.copy(out=result[:, t, cols], in_=backs[a][:])
 
-        terms = keep.tile([P, NEIGHBOURS, V], F32, name="terms0", tag="terms0", align_bytes=64)
+        num2 = [
+            keep.tile([P, V], F32, name=f"num2_{d}", tag=tag, align_bytes=64) for d, tag in enumerate(("num2_0", "h_bf2", "num2_2"))
+        ]
+        nc.vector.tensor_copy(num2[0][:], weighted[2][:].indirect(near[0][:]))
+
+        terms0 = keep.tile([P, NEIGHBOURS, V], F32, name="terms0", tag="terms0", align_bytes=64)
         for d in range(NEIGHBOURS):
-            nc.vector.tensor_tensor(terms[:, d, :], weighted[0][:].indirect(near[d][:]), inv[0][:], ALU.mult)
-        total = turned_sum(terms, "total0", "bank7")
-        turned = keep.tile([P, len(groups), P], F32, name="turned0", align_bytes=64)
-        nc.scalar.copy(out=turned[:], in_=total[:])
-        nc.scalar.copy(out=result[:, 0, :], in_=turn_back(turned, "back0", "bank0"))
-        nc.sync.dma_start(out=out_rows[:, 0, :], in_=result[:, 0, :])
+            nc.vector.tensor_tensor(terms0[:, d, :], weighted[0][:].indirect(near[d][:]), inv[0][:], ALU.mult)
+        add_and_turn_back(0, terms0, ("bank7", "bank5"), ("bank0", "bank4"))
 
-        terms = keep.tile([P, NEIGHBOURS, V], F32, name="terms1", align_bytes=64)
+        terms1 = keep.tile([P, NEIGHBOURS, V], F32, name="terms1", align_bytes=64)
         for d in range(NEIGHBOURS):
-            nc.vector.tensor_tensor(terms[:, d, :], weighted[1][:].indirect(near[d][:]), inv[1][:], ALU.mult)
+            nc.vector.tensor_tensor(terms1[:, d, :], weighted[1][:].indirect(near[d][:]), inv[1][:], ALU.mult)
             if d > 0:
-                nc.vector.tensor_tensor(sums[d][:], weighted[2][:].indirect(near[d][:]), sums[d - 1][:], ALU.add)
-        nc.gpsimd.tensor_tensor(result[:, 2, :], sums[2][:], inv[2][:], ALU.mult)
+                nc.vector.tensor_tensor(num2[d][:], weighted[2][:].indirect(near[d][:]), num2[d - 1][:], ALU.add)
+        nc.gpsimd.tensor_tensor(result[:, 2, :], num2[2][:], inv[2][:], ALU.mult)
         nc.sync.dma_start(out=out_rows[:, 2, :], in_=result[:, 2, :])
-        parts = [psum.tile([P, P], F32, name=f"part{a}", tag=f"bank{4 + a}") for a in range(len(groups))]
-        for d in range(NEIGHBOURS):
-            for a, cols in enumerate(groups):
-                add_turned(parts[a][:], terms[:, d, cols], d)
-        backs = []
-        for a, cols in enumerate(groups):
-            turned = keep.tile([P, P], F32, name=f"turned_part{a}", align_bytes=64)
-            nc.scalar.copy(out=turned[:], in_=parts[a][:])
-            backs.append(psum.tile([P, P], F32, name=f"back_part{a}", tag=f"bank{2 + a}"))
-            nc.tensor.transpose(backs[a][:], turned[:], identity[:])
-        for a, cols in enumerate(groups):
-            nc.scalar.copy(out=result[:, 1, cols], in_=backs[a][:])
-        for a, cols in enumerate(groups):
-            nc.scalar.copy(out=result_bf[:, cols, 0:2], in_=result[:, 0:2, cols].rearrange("p t v -> p v t"))
-        nc.sync.dma_start(out=out_rows[:, 1, :], in_=result[:, 1, :])
-
-        num_a = keep.tile([P, V], F32, name="num_a", tag="terms0", align_bytes=64)
-        for a, cols in enumerate(groups):
-            nc.vector.tensor_copy(num_a[:, cols], weighted[last][:].indirect(near[0][:, a * P // LANES : (a + 1) * P // LANES]))
-        inv3 = inv[last]
-
-        out_code = keep.tile([P, V], U32, name="out_code", align_bytes=64)
-        out_scale = keep.tile([P, V], U8, name="out_scale", align_bytes=64)
-        num_b = keep.tile([P, V], F32, name="num_b", align_bytes=64)
-        num_c = keep.tile([P, V], F32, name="num_c", align_bytes=64)
-        for d, before, total in ((1, num_a, num_b), (2, num_b, num_c)):
-            for a, cols in enumerate(groups):
-                offsets = near[d][:, a * P // LANES : (a + 1) * P // LANES]
-                nc.vector.tensor_tensor(total[:, cols], weighted[last][:].indirect(offsets), before[:, cols], ALU.add)
+        add_and_turn_back(1, terms1, ("bank5", "bank0"), ("bank2", "bank3"))
         for cols in groups:
-            nc.vector.tensor_tensor(result[:, last, cols], num_c[:, cols], inv3[:, cols], ALU.mult)
-        nc.sync.dma_start(out=out_rows[:, last, :], in_=result[:, last, :])
+            nc.scalar.copy(out=result_bf[:, cols, 0:2], in_=result[:, 0:2, cols].rearrange("p t v -> p v t"))
+        nc.scalar.dma_start(out=out_rows[:, 0:2, :], in_=result[:, 0:2, :])
+
+        def group_offsets(d, a):
+            return near[d][:, a * P // LANES : (a + 1) * P // LANES]
+
+        num3 = [
+            keep.tile([P, V], F32, name=f"num3_{d}", tag=tag, align_bytes=64) for d, tag in enumerate(("terms0", "num3_1", "num3_2"))
+        ]
+        for a, cols in enumerate(groups):
+            nc.vector.tensor_copy(num3[0][:, cols], weighted[3][:].indirect(group_offsets(0, a)))
+        for d in range(1, NEIGHBOURS):
+            for a, cols in enumerate(groups):
+                nc.vector.tensor_tensor(num3[d][:, cols], weighted[3][:].indirect(group_offsets(d, a)), num3[d - 1][:, cols], ALU.add)
+        for cols in groups:
+            nc.vector.tensor_tensor(result[:, 3, cols], num3[2][:, cols], inv[3][:, cols], ALU.mult)
+        nc.sync.dma_start(out=out_rows[:, 3, :], in_=result[:, 3, :])
         for cols in groups:
             nc.vector.tensor_copy(out=result_bf[:, cols, 2:4], in_=result[:, 2:4, cols].rearrange("p t v -> p v t"))
+        out_code = keep.tile([P, V], U32, name="out_code", align_bytes=64)
+        out_scale = keep.tile([P, V], U8, name="out_scale", align_bytes=64)
         for cols in groups:
             nc.vector.quantize_mx(
                 out=out_code[:, cols].bitcast(FP8X4), scales=out_scale[:, cols], in_=result_bf[:, cols, :].rearrange("p v t -> p (v t)")

@@ -21,6 +21,9 @@ PACK = 4
 QUAD = 32
 LANES = 16
 NEIGHBOURS = 3
+PAIR = 2
+ROW = 4 * V
+HELD = 2 * ROW
 
 
 def load_scale_rows(queues, tile, scales, first):
@@ -144,7 +147,8 @@ def tile_picked_zrandla_relu_po_kernel(
             )
 
         score = [keep.tile([P, S], F32, name=f"score{t}", align_bytes=64) for t in range(PACK)]
-        feature = [keep.tile([P, S], F32, name=f"feature{t}", align_bytes=64) for t in range(PACK)]
+        feature = [keep.tile([P, S], F32, name=f"feature{t}", align_bytes=64) for t in range(PACK - 1)]
+        feature.append(table.tile([P, S], F32, name="feature3", offset=HELD, align_bytes=64))
         weighted = [keep.tile([P, S], F32, name=f"weighted{t}", align_bytes=64) for t in range(PACK)]
 
         def make_scores(t, bank):
@@ -171,7 +175,6 @@ def tile_picked_zrandla_relu_po_kernel(
         make_features(3, "bank7")
 
         result = keep.tile([P, PACK, V], F32, name="result", align_bytes=64)
-        result_bf = keep.tile([P, V, PACK], BF16, name="result_bf", align_bytes=64)
         out_rows = out_0.rearrange("(p t) v -> p t v", t=PACK)
         groups = [slice(a * P, (a + 1) * P) for a in range(V // P)]
 
@@ -186,74 +189,60 @@ def tile_picked_zrandla_relu_po_kernel(
             for d in range(NEIGHBOURS):
                 nc.vector.tensor_copy(e_near[t][:, d, :], score[t][:].indirect(near[d][:]))
 
-        den_banks = ("bank3", "bank2", "bank4", "bank1")
-        root_tags = ("h_code", "h_scale", "h_bf2", "root3")
-        root_banks = ("bank0", "bank1", "bank5", "bank6")
-        inv = [keep.tile([P, V], F32, name=f"inv{t}", align_bytes=64) for t in range(PACK)]
-        for t in range(PACK):
-            den = psum.tile([P, len(groups), P], F32, name=f"den{t}", tag=den_banks[t])
-            for a, cols in enumerate(groups):
-                for d in range(NEIGHBOURS):
-                    add_turned(den[:, a, :], e_near[t], d, cols)
-            root = keep.tile([P, len(groups), P], F32, name=f"root{t}", tag=root_tags[t], align_bytes=64)
-            nc.scalar.activation(out=root[:], in_=den[:], func=ACT.Abs_reciprocal_sqrt)
-            root_back = psum.tile([P, len(groups), P], F32, name=f"root_back{t}", tag=root_banks[t])
-            for a in range(len(groups)):
-                nc.tensor.transpose(root_back[:, a, :], root[:, a, :], identity[:])
-            nc.scalar.activation(out=inv[t][:], in_=root_back[:].rearrange("p a v -> p (a v)"), func=ACT.Square)
-
-        def add_and_turn_back(t, terms, sum_banks, back_banks):
-            totals = [psum.tile([P, P], F32, name=f"total{t}{a}", tag=bank) for a, bank in enumerate(sum_banks)]
-            for d in range(NEIGHBOURS):
+        inv = []
+        for pair, (den_bank, root_tag, back_bank) in enumerate((("bank6", "h_code", "bank0"), ("bank6", "root1", "bank2"))):
+            den = psum.tile([P, PAIR, len(groups), P], F32, name=f"den{pair}", tag=den_bank)
+            for i in range(PAIR):
                 for a, cols in enumerate(groups):
-                    add_turned(totals[a][:], terms, d, cols)
-            backs = []
-            for a in range(len(groups)):
-                turned = keep.tile([P, P], F32, name=f"turned{t}{a}", align_bytes=64)
-                nc.scalar.copy(out=turned[:], in_=totals[a][:])
-                backs.append(psum.tile([P, P], F32, name=f"back{t}{a}", tag=back_banks[a]))
-                nc.tensor.transpose(backs[a][:], turned[:], identity[:])
-            for a, cols in enumerate(groups):
-                nc.scalar.copy(out=result[:, t, cols], in_=backs[a][:])
+                    for d in range(NEIGHBOURS):
+                        add_turned(den[:, i, a, :], e_near[PAIR * pair + i], d, cols)
+            root = keep.tile([P, PAIR, len(groups), P], F32, name=f"root{pair}", tag=root_tag, align_bytes=64)
+            nc.scalar.activation(
+                out=root[:].rearrange("p i a v -> p (i a v)"), in_=den[:].rearrange("p i a v -> p (i a v)"), func=ACT.Abs_reciprocal_sqrt
+            )
+            root_back = psum.tile([P, PAIR, len(groups), P], F32, name=f"root_back{pair}", tag=back_bank)
+            for i in range(PAIR):
+                for a in range(len(groups)):
+                    nc.tensor.transpose(root_back[:, i, a, :], root[:, i, a, :], identity[:])
+            inv.append(keep.tile([P, PAIR, V], F32, name=f"inv{pair}", align_bytes=64))
+            nc.scalar.activation(
+                out=inv[pair][:].rearrange("p i v -> p (i v)"), in_=root_back[:].rearrange("p i a v -> p (i a v)"), func=ACT.Square
+            )
 
-        num2 = [
-            keep.tile([P, V], F32, name=f"num2_{d}", tag=tag, align_bytes=64) for d, tag in enumerate(("num2_0", "h_bf2", "num2_2"))
-        ]
-        nc.vector.tensor_copy(num2[0][:], weighted[2][:].indirect(near[0][:]))
+        def add_neighbours(pair, sums):
+            for d in range(NEIGHBOURS):
+                for i in range(PAIR):
+                    fetched = weighted[PAIR * pair + i][:].indirect(near[d][:])
+                    if d == 0:
+                        nc.vector.tensor_copy(sums[0][i], fetched)
+                    else:
+                        nc.vector.tensor_tensor(sums[d][i], fetched, sums[d - 1][i], ALU.add)
 
-        terms0 = keep.tile([P, NEIGHBOURS, V], F32, name="terms0", tag="terms0", align_bytes=64)
-        for d in range(NEIGHBOURS):
-            nc.vector.tensor_tensor(terms0[:, d, :], weighted[0][:].indirect(near[d][:]), inv[0][:], ALU.mult)
-        add_and_turn_back(0, terms0, ("bank7", "bank5"), ("bank0", "bank4"))
+        def free_sums(name):
+            tile = keep.tile([P, PAIR, V], F32, name=name, align_bytes=64)
+            return tile, [tile[:, i, :] for i in range(PAIR)]
 
-        terms1 = keep.tile([P, NEIGHBOURS, V], F32, name="terms1", align_bytes=64)
-        for d in range(NEIGHBOURS):
-            nc.vector.tensor_tensor(terms1[:, d, :], weighted[1][:].indirect(near[d][:]), inv[1][:], ALU.mult)
-            if d > 0:
-                nc.vector.tensor_tensor(num2[d][:], weighted[2][:].indirect(near[d][:]), num2[d - 1][:], ALU.add)
-        nc.gpsimd.tensor_tensor(result[:, 2, :], num2[2][:], inv[2][:], ALU.mult)
+        def held_sums(name):
+            return [table.tile([P, V], F32, name=f"{name}{i}", offset=HELD + i * ROW, align_bytes=64)[:] for i in range(PAIR)]
+
+        num_low, last_low = free_sums("num_low")
+        add_neighbours(0, [free_sums("first_low")[1], held_sums("second_low"), last_low])
+        nc.gpsimd.tensor_tensor(result[:, 0:PAIR, :], num_low[:], inv[0][:], ALU.mult)
+        nc.sync.dma_start(out=out_rows[:, 0:PAIR, :], in_=result[:, 0:PAIR, :])
+        result_bf = keep.tile([P, V, PACK], BF16, name="result_bf", tag="root1", align_bytes=64)
+        for cols in groups:
+            nc.scalar.copy(out=result_bf[:, cols, 0:PAIR], in_=result[:, 0:PAIR, cols].rearrange("p t v -> p v t"))
+
+        num_high, last_high = free_sums("num_high")
+        add_neighbours(1, [held_sums("first_high"), free_sums("second_high")[1], last_high])
+        nc.vector.tensor_tensor(result[:, 2, :], num_high[:, 0, :], inv[1][:, 0, :], ALU.mult)
         nc.sync.dma_start(out=out_rows[:, 2, :], in_=result[:, 2, :])
-        add_and_turn_back(1, terms1, ("bank5", "bank0"), ("bank2", "bank3"))
-        for cols in groups:
-            nc.scalar.copy(out=result_bf[:, cols, 0:2], in_=result[:, 0:2, cols].rearrange("p t v -> p v t"))
-        nc.scalar.dma_start(out=out_rows[:, 0:2, :], in_=result[:, 0:2, :])
 
-        def group_offsets(d, a):
-            return near[d][:, a * P // LANES : (a + 1) * P // LANES]
-
-        num3 = [
-            keep.tile([P, V], F32, name=f"num3_{d}", tag=tag, align_bytes=64) for d, tag in enumerate(("terms0", "num3_1", "num3_2"))
-        ]
-        for a, cols in enumerate(groups):
-            nc.vector.tensor_copy(num3[0][:, cols], weighted[3][:].indirect(group_offsets(0, a)))
-        for d in range(1, NEIGHBOURS):
-            for a, cols in enumerate(groups):
-                nc.vector.tensor_tensor(num3[d][:, cols], weighted[3][:].indirect(group_offsets(d, a)), num3[d - 1][:, cols], ALU.add)
         for cols in groups:
-            nc.vector.tensor_tensor(result[:, 3, cols], num3[2][:, cols], inv[3][:, cols], ALU.mult)
+            nc.vector.tensor_tensor(result[:, 3, cols], num_high[:, 1, cols], inv[1][:, 1, cols], ALU.mult)
         nc.sync.dma_start(out=out_rows[:, 3, :], in_=result[:, 3, :])
         for cols in groups:
-            nc.vector.tensor_copy(out=result_bf[:, cols, 2:4], in_=result[:, 2:4, cols].rearrange("p t v -> p v t"))
+            nc.vector.tensor_copy(out=result_bf[:, cols, PAIR:PACK], in_=result[:, PAIR:PACK, cols].rearrange("p t v -> p v t"))
         out_code = keep.tile([P, V], U32, name="out_code", align_bytes=64)
         out_scale = keep.tile([P, V], U8, name="out_scale", align_bytes=64)
         for cols in groups:

@@ -147,32 +147,20 @@ def tile_picked_zrandla_relu_po_kernel(
             )
 
         score = [keep.tile([P, S], F32, name=f"score{t}", align_bytes=64) for t in range(PACK)]
-        feature = [keep.tile([P, S], F32, name=f"feature{t}", align_bytes=64) for t in range(PACK - 1)]
-        feature.append(table.tile([P, S], F32, name="feature3", offset=HELD, align_bytes=64))
         weighted = [keep.tile([P, S], F32, name=f"weighted{t}", align_bytes=64) for t in range(PACK)]
-
-        def make_scores(t, bank):
-            s_sum = psum.tile([P, S], F32, name=f"s_sum{t}", tag=bank)
-            product(s_sum[:], w2_code, w2_scale, t, slice(0, S))
-            nc.scalar.activation(out=score[t][:], in_=s_sum[:], func=ACT.Exp)
-
-        def make_features(t, bank):
-            y_sum = psum.tile([P, S], F32, name=f"y_sum{t}", tag=bank)
-            product(y_sum[:], w3_code, w3_scale, t, slice(0, S))
-            nc.scalar.copy(out=feature[t][:], in_=y_sum[:])
-            nc.gpsimd.tensor_tensor(weighted[t][:], feature[t][:], score[t][:], ALU.mult)
 
         for q, cols in enumerate(quarters):
             s_part = psum.tile([P, P], F32, name=f"s_part{q}", tag=f"bank{PACK + q}")
             product(s_part[:], w2_code, w2_scale, 0, cols)
             nc.scalar.activation(out=score[0][:, cols], in_=s_part[:], func=ACT.Exp)
-        make_features(0, "bank0")
-        make_scores(1, "bank1")
-        make_features(1, "bank2")
-        make_scores(2, "bank4")
-        make_features(2, "bank5")
-        make_scores(3, "bank6")
-        make_features(3, "bank7")
+        for t in range(1, PACK):
+            s_sum = psum.tile([P, S], F32, name=f"s_sum{t}", tag=f"bank{t - 1}")
+            product(s_sum[:], w2_code, w2_scale, t, slice(0, S))
+            nc.scalar.activation(out=score[t][:], in_=s_sum[:], func=ACT.Exp)
+        y_sum = []
+        for t in range(PACK):
+            y_sum.append(psum.tile([P, S], F32, name=f"y_sum{t}", tag=f"bank{PACK - 1 + t}"))
+            product(y_sum[t][:], w3_code, w3_scale, t, slice(0, S))
 
         result = keep.tile([P, PACK, V], F32, name="result", align_bytes=64)
         out_rows = out_0.rearrange("(p t) v -> p t v", t=PACK)
@@ -187,62 +175,58 @@ def tile_picked_zrandla_relu_po_kernel(
         for t in range(PACK):
             e_near.append(keep.tile([P, NEIGHBOURS, V], F32, name=f"e_near{t}", tag=f"e_near{t}", align_bytes=64))
             for d in range(NEIGHBOURS):
-                nc.vector.tensor_copy(e_near[t][:, d, :], score[t][:].indirect(near[d][:]))
+                fetched = score[t][:].indirect(near[d][:])
+                if t == 0:
+                    nc.vector.tensor_copy(e_near[t][:, d, :], fetched)
+                else:
+                    nc.scalar.activation(out=e_near[t][:, d, :], in_=fetched, func=ACT.Copy)
 
-        inv = []
-        for pair, (den_bank, root_tag, back_bank) in enumerate((("bank6", "h_code", "bank0"), ("bank6", "root1", "bank2"))):
+        roots = []
+        for pair, den_bank in enumerate(("bank2", "bank0")):
             den = psum.tile([P, PAIR, len(groups), P], F32, name=f"den{pair}", tag=den_bank)
             for i in range(PAIR):
                 for a, cols in enumerate(groups):
                     for d in range(NEIGHBOURS):
                         add_turned(den[:, i, a, :], e_near[PAIR * pair + i], d, cols)
-            root = keep.tile([P, PAIR, len(groups), P], F32, name=f"root{pair}", tag=root_tag, align_bytes=64)
+            root = keep.tile([P, PAIR, len(groups), P], F32, name=f"root{pair}", align_bytes=64)
             nc.scalar.activation(
                 out=root[:].rearrange("p i a v -> p (i a v)"), in_=den[:].rearrange("p i a v -> p (i a v)"), func=ACT.Abs_reciprocal_sqrt
             )
+            roots.append(root)
+        inv = []
+        for pair, back_bank in enumerate(("bank1", "bank7")):
             root_back = psum.tile([P, PAIR, len(groups), P], F32, name=f"root_back{pair}", tag=back_bank)
             for i in range(PAIR):
                 for a in range(len(groups)):
-                    nc.tensor.transpose(root_back[:, i, a, :], root[:, i, a, :], identity[:])
+                    nc.tensor.transpose(root_back[:, i, a, :], roots[pair][:, i, a, :], identity[:])
             inv.append(keep.tile([P, PAIR, V], F32, name=f"inv{pair}", align_bytes=64))
             nc.scalar.activation(
                 out=inv[pair][:].rearrange("p i v -> p (i v)"), in_=root_back[:].rearrange("p i a v -> p (i a v)"), func=ACT.Square
             )
 
-        def add_neighbours(pair, sums):
+        num = []
+        for pair in range(PACK // PAIR):
+            tiles = range(PAIR * pair, PAIR * (pair + 1))
+            for t in tiles:
+                nc.vector.tensor_tensor(weighted[t][:], y_sum[t][:], score[t][:], ALU.mult)
+            sums = [keep.tile([P, PAIR, V], F32, name=f"sums{pair}_{d}", align_bytes=64) for d in range(NEIGHBOURS)]
             for d in range(NEIGHBOURS):
-                for i in range(PAIR):
-                    fetched = weighted[PAIR * pair + i][:].indirect(near[d][:])
+                for i, t in enumerate(tiles):
+                    fetched = weighted[t][:].indirect(near[d][:])
                     if d == 0:
-                        nc.vector.tensor_copy(sums[0][i], fetched)
+                        nc.vector.tensor_copy(sums[0][:, i, :], fetched)
                     else:
-                        nc.vector.tensor_tensor(sums[d][i], fetched, sums[d - 1][i], ALU.add)
+                        nc.vector.tensor_tensor(sums[d][:, i, :], fetched, sums[d - 1][:, i, :], ALU.add)
+            num.append(sums[NEIGHBOURS - 1])
 
-        def free_sums(name):
-            tile = keep.tile([P, PAIR, V], F32, name=name, align_bytes=64)
-            return tile, [tile[:, i, :] for i in range(PAIR)]
-
-        def held_sums(name):
-            return [table.tile([P, V], F32, name=f"{name}{i}", offset=HELD + i * ROW, align_bytes=64)[:] for i in range(PAIR)]
-
-        num_low, last_low = free_sums("num_low")
-        add_neighbours(0, [free_sums("first_low")[1], held_sums("second_low"), last_low])
-        nc.gpsimd.tensor_tensor(result[:, 0:PAIR, :], num_low[:], inv[0][:], ALU.mult)
+        nc.vector.tensor_tensor(result[:, 0:PAIR, :], num[0][:], inv[0][:], ALU.mult)
         nc.sync.dma_start(out=out_rows[:, 0:PAIR, :], in_=result[:, 0:PAIR, :])
-        result_bf = keep.tile([P, V, PACK], BF16, name="result_bf", tag="root1", align_bytes=64)
         for cols in groups:
-            nc.scalar.copy(out=result_bf[:, cols, 0:PAIR], in_=result[:, 0:PAIR, cols].rearrange("p t v -> p v t"))
-
-        num_high, last_high = free_sums("num_high")
-        add_neighbours(1, [held_sums("first_high"), free_sums("second_high")[1], last_high])
-        nc.vector.tensor_tensor(result[:, 2, :], num_high[:, 0, :], inv[1][:, 0, :], ALU.mult)
-        nc.sync.dma_start(out=out_rows[:, 2, :], in_=result[:, 2, :])
-
+            nc.vector.tensor_tensor(result[:, PAIR:PACK, cols], num[1][:, :, cols], inv[1][:, :, cols], ALU.mult)
+        nc.sync.dma_start(out=out_rows[:, PAIR:PACK, :], in_=result[:, PAIR:PACK, :])
+        result_bf = keep.tile([P, V, PACK], BF16, name="result_bf", align_bytes=64)
         for cols in groups:
-            nc.vector.tensor_tensor(result[:, 3, cols], num_high[:, 1, cols], inv[1][:, 1, cols], ALU.mult)
-        nc.sync.dma_start(out=out_rows[:, 3, :], in_=result[:, 3, :])
-        for cols in groups:
-            nc.vector.tensor_copy(out=result_bf[:, cols, PAIR:PACK], in_=result[:, PAIR:PACK, cols].rearrange("p t v -> p v t"))
+            nc.vector.tensor_copy(out=result_bf[:, cols, :], in_=result[:, :, cols].rearrange("p t v -> p v t"))
         out_code = keep.tile([P, V], U32, name="out_code", align_bytes=64)
         out_scale = keep.tile([P, V], U8, name="out_scale", align_bytes=64)
         for cols in groups:

@@ -50,7 +50,7 @@ def tile_picked_zrandla_relu_po_kernel(
         near = [lists.tile([P, V // LANES], U16, name=f"near{d}") for d in range(NEIGHBOURS)]
 
         x_scale_table = keep.tile([P, T], U8, name="x_scale_table", align_bytes=64)
-        w_scale_rows = keep.tile([P, N], U8, name="w_scale_rows", align_bytes=64)
+        w_scale_rows = keep.tile([P, N], U8, name="w_scale_rows", tag="h_scale", align_bytes=64)
         nc.vector.memset(x_scale_table[:].bitcast(I32), 0)
         nc.gpsimd.memset(w_scale_rows[:].bitcast(I32), 0)
 
@@ -58,7 +58,7 @@ def tile_picked_zrandla_relu_po_kernel(
         x_table = table.tile([P, T], I32, name="x_table", offset=0, align_bytes=64)
         x_scale_rows = keep.tile([P, T], U8, name="x_scale_rows", align_bytes=64)
         w2_rows = keep.tile([P, N], I32, name="w2_rows", align_bytes=64)
-        w3_rows = keep.tile([P, N], I32, name="w3_rows", tag="e_near0", align_bytes=64)
+        w3_rows = keep.tile([P, N], I32, name="w3_rows", tag="h_code", align_bytes=64)
         nc.sync.dma_start(picks[:], offs)
         load_scale_rows([nc.scalar, nc.scalar, nc.sync, nc.sync], x_scale_rows, x_scales, 0)
         nc.sync.dma_start(out=w1_rows[:], in_=w1.rearrange("(p j) c -> p j c", j=PACK))
@@ -91,10 +91,9 @@ def tile_picked_zrandla_relu_po_kernel(
             )
 
         x_code = keep.tile([P, S], U32, name="x_code", tag="w1_bf0", align_bytes=64)
-        half = S // 2
-        for a in range(2):
-            offsets = picks[:, a * half // LANES : (a + 1) * half // LANES]
-            nc.vector.tensor_copy(x_code[:, a * half : (a + 1) * half], x_table[:].bitcast(U32).indirect(offsets))
+        for start, stop in ((0, P), (P, 2 * P), (2 * P, S)):
+            offsets = picks[:, start // LANES : stop // LANES]
+            nc.vector.tensor_copy(x_code[:, start:stop], x_table[:].bitcast(U32).indirect(offsets))
 
         def deal_words(copy, rows, dealt):
             copy(out=dealt.rearrange("p (t m) -> p m t", t=PACK), in_=rows.rearrange("p (m t) -> p m t", t=PACK))
@@ -108,7 +107,10 @@ def tile_picked_zrandla_relu_po_kernel(
         w2_scale = w_scale[:]
         w3_scale = w_scale[PACK:P, :]
 
-        vector_quarter = 1
+        w3_code = table.tile([P, N], I32, name="w3_code", offset=HELD, align_bytes=64)
+        deal_words(nc.vector.tensor_copy, w3_rows[:], w3_code[:])
+
+        vector_quarter = 3
         h_code = keep.tile([P, S], U32, name="h_code", tag="h_code", align_bytes=64)
         h_scale = keep.tile([P, S], U8, name="h_scale", tag="h_scale", align_bytes=64)
         quarters = [slice(q * P, (q + 1) * P) for q in range(S // P)]
@@ -125,15 +127,12 @@ def tile_picked_zrandla_relu_po_kernel(
                     start=True,
                     stop=True,
                 )
-            h_bf = keep.tile([P, P, PACK], BF16, name=f"h_bf{q}", tag=f"h_bf{q}", align_bytes=64)
+            h_bf = keep.tile([P, P, PACK], BF16, name=f"h_bf{q}", tag=f"h_bf{1 if q == vector_quarter else q}", align_bytes=64)
             if q == vector_quarter:
                 nc.vector.tensor_scalar_max(out=h_bf[:], in0=h_sum[:].rearrange("p t n -> p n t"), scalar1=0.0)
             else:
                 nc.scalar.activation(out=h_bf[:], in_=h_sum[:].rearrange("p t n -> p n t"), func=ACT.Relu)
             nc.vector.quantize_mx(out=h_code[:, cols].bitcast(FP8X4), scales=h_scale[:, cols], in_=h_bf[:].rearrange("p n t -> p (n t)"))
-        w3_code = keep.tile([P, N], I32, name="w3_code", tag="h_bf2", align_bytes=64)
-        deal_words(nc.vector.tensor_copy, w3_rows[:], w3_code[:])
-
         def product(total, code, scale, t, cols):
             w_cols = slice(t * P, (t + 1) * P)
             nc.tensor.matmul_mx(
@@ -149,18 +148,39 @@ def tile_picked_zrandla_relu_po_kernel(
         score = [keep.tile([P, S], F32, name=f"score{t}", align_bytes=64) for t in range(PACK)]
         weighted = [keep.tile([P, S], F32, name=f"weighted{t}", align_bytes=64) for t in range(PACK)]
 
-        for q, cols in enumerate(quarters):
-            s_part = psum.tile([P, P], F32, name=f"s_part{q}", tag=f"bank{PACK + q}")
-            product(s_part[:], w2_code, w2_scale, 0, cols)
-            nc.scalar.activation(out=score[0][:, cols], in_=s_part[:], func=ACT.Exp)
-        for t in range(1, PACK):
-            s_sum = psum.tile([P, S], F32, name=f"s_sum{t}", tag=f"bank{t - 1}")
-            product(s_sum[:], w2_code, w2_scale, t, slice(0, S))
-            nc.scalar.activation(out=score[t][:], in_=s_sum[:], func=ACT.Exp)
-        y_sum = []
+        halves = [slice(a * S // 2, (a + 1) * S // 2) for a in range(2)]
+        s_sum = [psum.tile([P, S], F32, name=f"s_sum{t}", tag=f"bank{PACK + t}") for t in range(PACK)]
+        early = range(PACK - 1)
+
+        def make_scores(total, t, cols):
+            product(total, w2_code, w2_scale, t, cols)
+            nc.scalar.activation(out=score[t][:, cols], in_=total, func=ACT.Exp)
+
+        make_scores(s_sum[0][:, halves[0]], 0, halves[0])
+        make_scores(s_sum[0][:, quarters[2]], 0, quarters[2])
+        s_last = psum.tile([P, P], F32, name="s_last", tag="bank3")
+        make_scores(s_last[:], 0, quarters[3])
+        for cols in halves:
+            for t in range(1, PACK):
+                make_scores(s_sum[t][:, cols], t, cols)
+
+        e_near = [keep.tile([P, NEIGHBOURS, V], F32, name=f"e_near{t}", tag=f"e_near{t}", align_bytes=64) for t in range(PACK)]
+        last = NEIGHBOURS - 1
+        for d in range(last):
+            nc.vector.tensor_copy(e_near[0][:, d, :], score[0][:].indirect(near[d][:]))
+        nc.vector.tensor_copy(e_near[0][:, last, 0:P], score[0][:].indirect(near[last][:, 0 : P // LANES]))
+
+        y_sum = [psum.tile([P, S], F32, name=f"y_sum{t}", tag=f"bank{t}") for t in range(PACK)]
+
+        def weigh(t, cols):
+            nc.vector.tensor_tensor(weighted[t][:, cols], y_sum[t][:, cols], score[t][:, cols], ALU.mult)
+
+        for t in early:
+            product(y_sum[t][:, halves[0]], w3_code, w3_scale, t, halves[0])
+            weigh(t, halves[0])
+        rest = [halves[1] if t in early else slice(0, S) for t in range(PACK)]
         for t in range(PACK):
-            y_sum.append(psum.tile([P, S], F32, name=f"y_sum{t}", tag=f"bank{PACK - 1 + t}"))
-            product(y_sum[t][:], w3_code, w3_scale, t, slice(0, S))
+            product(y_sum[t][:, rest[t]], w3_code, w3_scale, t, rest[t])
 
         result = keep.tile([P, PACK, V], F32, name="result", align_bytes=64)
         out_rows = out_0.rearrange("(p t) v -> p t v", t=PACK)
@@ -171,44 +191,11 @@ def tile_picked_zrandla_relu_po_kernel(
                 total, lhsT=terms[:, d, cols], rhs=identity[:], is_transpose=True, start=(d == 0), stop=(d == NEIGHBOURS - 1)
             )
 
-        e_near = []
-        for t in range(PACK):
-            e_near.append(keep.tile([P, NEIGHBOURS, V], F32, name=f"e_near{t}", tag=f"e_near{t}", align_bytes=64))
-            for d in range(NEIGHBOURS):
-                fetched = score[t][:].indirect(near[d][:])
-                if t == 0:
-                    nc.vector.tensor_copy(e_near[t][:, d, :], fetched)
-                else:
-                    nc.scalar.activation(out=e_near[t][:, d, :], in_=fetched, func=ACT.Copy)
-
-        roots = []
-        for pair, den_bank in enumerate(("bank2", "bank0")):
-            den = psum.tile([P, PAIR, len(groups), P], F32, name=f"den{pair}", tag=den_bank)
-            for i in range(PAIR):
-                for a, cols in enumerate(groups):
-                    for d in range(NEIGHBOURS):
-                        add_turned(den[:, i, a, :], e_near[PAIR * pair + i], d, cols)
-            root = keep.tile([P, PAIR, len(groups), P], F32, name=f"root{pair}", align_bytes=64)
-            nc.scalar.activation(
-                out=root[:].rearrange("p i a v -> p (i a v)"), in_=den[:].rearrange("p i a v -> p (i a v)"), func=ACT.Abs_reciprocal_sqrt
-            )
-            roots.append(root)
-        inv = []
-        for pair, back_bank in enumerate(("bank1", "bank7")):
-            root_back = psum.tile([P, PAIR, len(groups), P], F32, name=f"root_back{pair}", tag=back_bank)
-            for i in range(PAIR):
-                for a in range(len(groups)):
-                    nc.tensor.transpose(root_back[:, i, a, :], roots[pair][:, i, a, :], identity[:])
-            inv.append(keep.tile([P, PAIR, V], F32, name=f"inv{pair}", align_bytes=64))
-            nc.scalar.activation(
-                out=inv[pair][:].rearrange("p i v -> p (i v)"), in_=root_back[:].rearrange("p i a v -> p (i a v)"), func=ACT.Square
-            )
-
         num = []
         for pair in range(PACK // PAIR):
             tiles = range(PAIR * pair, PAIR * (pair + 1))
             for t in tiles:
-                nc.vector.tensor_tensor(weighted[t][:], y_sum[t][:], score[t][:], ALU.mult)
+                weigh(t, rest[t])
             sums = [keep.tile([P, PAIR, V], F32, name=f"sums{pair}_{d}", align_bytes=64) for d in range(NEIGHBOURS)]
             for d in range(NEIGHBOURS):
                 for i, t in enumerate(tiles):
@@ -219,14 +206,41 @@ def tile_picked_zrandla_relu_po_kernel(
                         nc.vector.tensor_tensor(sums[d][:, i, :], fetched, sums[d - 1][:, i, :], ALU.add)
             num.append(sums[NEIGHBOURS - 1])
 
+        nc.scalar.activation(out=e_near[0][:, last, P:V], in_=score[0][:].indirect(near[last][:, P // LANES : V // LANES]), func=ACT.Copy)
+        first = [(t, d) for t in range(1, PACK) for d in range(NEIGHBOURS) if t == 2 or d < last]
+        for t, d in first + [(1, last), (3, last)]:
+            nc.scalar.activation(out=e_near[t][:, d, :], in_=score[t][:].indirect(near[d][:]), func=ACT.Copy)
+
+        den = [psum.tile([P, PAIR, len(groups), P], F32, name=f"den{pair}", tag=bank) for pair, bank in enumerate(("bank7", "bank4"))]
+        roots = []
+        for t in range(PACK):
+            for a, cols in enumerate(groups):
+                for d in range(NEIGHBOURS):
+                    add_turned(den[t // PAIR][:, t % PAIR, a, :], e_near[t], d, cols)
+        for t in range(PACK):
+            roots.append(keep.tile([P, len(groups), P], F32, name=f"root{t}", align_bytes=64))
+            nc.scalar.activation(
+                out=roots[t][:].rearrange("p a v -> p (a v)"),
+                in_=den[t // PAIR][:, t % PAIR, :, :].rearrange("p a v -> p (a v)"),
+                func=ACT.Abs_reciprocal_sqrt,
+            )
+        inv = [keep.tile([P, PAIR, V], F32, name=f"inv{pair}", align_bytes=64) for pair in range(PACK // PAIR)]
+        for t, back_bank in enumerate(("bank5", "bank6", "bank0", "bank1")):
+            root_back = psum.tile([P, len(groups), P], F32, name=f"root_back{t}", tag=back_bank)
+            for a in range(len(groups)):
+                nc.tensor.transpose(root_back[:, a, :], roots[t][:, a, :], identity[:])
+            nc.scalar.activation(out=inv[t // PAIR][:, t % PAIR, :], in_=root_back[:].rearrange("p a v -> p (a v)"), func=ACT.Square)
+
         nc.vector.tensor_tensor(result[:, 0:PAIR, :], num[0][:], inv[0][:], ALU.mult)
         nc.sync.dma_start(out=out_rows[:, 0:PAIR, :], in_=result[:, 0:PAIR, :])
+        result_bf = keep.tile([P, V, PACK], BF16, name="result_bf", align_bytes=64)
+        for cols in groups:
+            nc.scalar.copy(out=result_bf[:, cols, 0:PAIR], in_=result[:, 0:PAIR, cols].rearrange("p t v -> p v t"))
         for cols in groups:
             nc.vector.tensor_tensor(result[:, PAIR:PACK, cols], num[1][:, :, cols], inv[1][:, :, cols], ALU.mult)
         nc.sync.dma_start(out=out_rows[:, PAIR:PACK, :], in_=result[:, PAIR:PACK, :])
-        result_bf = keep.tile([P, V, PACK], BF16, name="result_bf", align_bytes=64)
         for cols in groups:
-            nc.vector.tensor_copy(out=result_bf[:, cols, :], in_=result[:, :, cols].rearrange("p t v -> p v t"))
+            nc.vector.tensor_copy(out=result_bf[:, cols, PAIR:PACK], in_=result[:, PAIR:PACK, cols].rearrange("p t v -> p v t"))
         out_code = keep.tile([P, V], U32, name="out_code", align_bytes=64)
         out_scale = keep.tile([P, V], U8, name="out_scale", align_bytes=64)
         for cols in groups:

@@ -22,8 +22,7 @@ QUAD = 32
 LANES = 16
 NEIGHBOURS = 3
 PAIR = 2
-ROW = 4 * V
-HELD = 2 * ROW
+W3_OFFSET = 4 * N
 
 
 def load_scale_rows(queues, tile, scales, first):
@@ -34,6 +33,10 @@ def load_scale_rows(queues, tile, scales, first):
 
 def words_of(packed):
     return packed[0].rearrange("p c r -> p (c r)").bitcast(I32)
+
+
+def entries(tile, start, stop):
+    return tile[:, start // LANES : stop // LANES]
 
 
 def tile_picked_zrandla_relu_po_kernel(
@@ -83,17 +86,16 @@ def tile_picked_zrandla_relu_po_kernel(
         w1_scale = keep.tile([P, H], U8, name="w1_scale", align_bytes=64)
         w1_src = w1_rows[:].rearrange("p j (m t) -> p m j t", t=PACK)
         for pair, copy in enumerate((nc.scalar.copy, nc.vector.tensor_copy)):
-            w1_bf = keep.tile([P, 2, P, PACK], BF16, name=f"w1_bf{pair}", tag=f"w1_bf{pair}", align_bytes=64)
-            copy(out=w1_bf[:].rearrange("p t m j -> p m j t"), in_=w1_src[:, :, :, 2 * pair : 2 * pair + 2])
-            cols = slice(2 * pair * P, 2 * (pair + 1) * P)
+            w1_bf = keep.tile([P, PAIR, P, PACK], BF16, name=f"w1_bf{pair}", tag=f"w1_bf{pair}", align_bytes=64)
+            copy(out=w1_bf[:].rearrange("p t m j -> p m j t"), in_=w1_src[:, :, :, PAIR * pair : PAIR * (pair + 1)])
+            cols = slice(PAIR * pair * P, PAIR * (pair + 1) * P)
             nc.vector.quantize_mx(
                 out=w1_code[:, cols].bitcast(FP8X4), scales=w1_scale[:, cols], in_=w1_bf[:].rearrange("p t m j -> p (t m j)")
             )
 
         x_code = keep.tile([P, S], U32, name="x_code", tag="w1_bf0", align_bytes=64)
         for start, stop in ((0, P), (P, 2 * P), (2 * P, S)):
-            offsets = picks[:, start // LANES : stop // LANES]
-            nc.vector.tensor_copy(x_code[:, start:stop], x_table[:].bitcast(U32).indirect(offsets))
+            nc.vector.tensor_copy(x_code[:, start:stop], x_table[:].bitcast(U32).indirect(entries(picks, start, stop)))
 
         def deal_words(copy, rows, dealt):
             copy(out=dealt.rearrange("p (t m) -> p m t", t=PACK), in_=rows.rearrange("p (m t) -> p m t", t=PACK))
@@ -106,11 +108,9 @@ def tile_picked_zrandla_relu_po_kernel(
         )
         w2_scale = w_scale[:]
         w3_scale = w_scale[PACK:P, :]
-
-        w3_code = table.tile([P, N], I32, name="w3_code", offset=HELD, align_bytes=64)
+        w3_code = table.tile([P, N], I32, name="w3_code", offset=W3_OFFSET, align_bytes=64)
         deal_words(nc.vector.tensor_copy, w3_rows[:], w3_code[:])
 
-        vector_quarter = 3
         h_code = keep.tile([P, S], U32, name="h_code", tag="h_code", align_bytes=64)
         h_scale = keep.tile([P, S], U8, name="h_scale", tag="h_scale", align_bytes=64)
         quarters = [slice(q * P, (q + 1) * P) for q in range(S // P)]
@@ -127,12 +127,14 @@ def tile_picked_zrandla_relu_po_kernel(
                     start=True,
                     stop=True,
                 )
-            h_bf = keep.tile([P, P, PACK], BF16, name=f"h_bf{q}", tag=f"h_bf{1 if q == vector_quarter else q}", align_bytes=64)
-            if q == vector_quarter:
+            on_vector = q == len(quarters) - 1
+            h_bf = keep.tile([P, P, PACK], BF16, name=f"h_bf{q}", tag=f"h_bf{1 if on_vector else q}", align_bytes=64)
+            if on_vector:
                 nc.vector.tensor_scalar_max(out=h_bf[:], in0=h_sum[:].rearrange("p t n -> p n t"), scalar1=0.0)
             else:
                 nc.scalar.activation(out=h_bf[:], in_=h_sum[:].rearrange("p t n -> p n t"), func=ACT.Relu)
             nc.vector.quantize_mx(out=h_code[:, cols].bitcast(FP8X4), scales=h_scale[:, cols], in_=h_bf[:].rearrange("p n t -> p (n t)"))
+
         def product(total, code, scale, t, cols):
             w_cols = slice(t * P, (t + 1) * P)
             nc.tensor.matmul_mx(
@@ -147,10 +149,8 @@ def tile_picked_zrandla_relu_po_kernel(
 
         score = [keep.tile([P, S], F32, name=f"score{t}", align_bytes=64) for t in range(PACK)]
         weighted = [keep.tile([P, S], F32, name=f"weighted{t}", align_bytes=64) for t in range(PACK)]
-
         halves = [slice(a * S // 2, (a + 1) * S // 2) for a in range(2)]
         s_sum = [psum.tile([P, S], F32, name=f"s_sum{t}", tag=f"bank{PACK + t}") for t in range(PACK)]
-        early = range(PACK - 1)
 
         def make_scores(total, t, cols):
             product(total, w2_code, w2_scale, t, cols)
@@ -166,30 +166,27 @@ def tile_picked_zrandla_relu_po_kernel(
 
         e_near = [keep.tile([P, NEIGHBOURS, V], F32, name=f"e_near{t}", tag=f"e_near{t}", align_bytes=64) for t in range(PACK)]
         last = NEIGHBOURS - 1
+        split = V // 2
         for d in range(last):
             nc.vector.tensor_copy(e_near[0][:, d, :], score[0][:].indirect(near[d][:]))
-        nc.vector.tensor_copy(e_near[0][:, last, 0:P], score[0][:].indirect(near[last][:, 0 : P // LANES]))
+        nc.vector.tensor_copy(e_near[0][:, last, 0:split], score[0][:].indirect(entries(near[last], 0, split)))
 
         y_sum = [psum.tile([P, S], F32, name=f"y_sum{t}", tag=f"bank{t}") for t in range(PACK)]
 
         def weigh(t, cols):
             nc.vector.tensor_tensor(weighted[t][:, cols], y_sum[t][:, cols], score[t][:, cols], ALU.mult)
 
-        for t in early:
+        halved = range(PACK - 1)
+        for t in halved:
             product(y_sum[t][:, halves[0]], w3_code, w3_scale, t, halves[0])
             weigh(t, halves[0])
-        rest = [halves[1] if t in early else slice(0, S) for t in range(PACK)]
+        rest = [halves[1] if t in halved else slice(0, S) for t in range(PACK)]
         for t in range(PACK):
             product(y_sum[t][:, rest[t]], w3_code, w3_scale, t, rest[t])
 
         result = keep.tile([P, PACK, V], F32, name="result", align_bytes=64)
         out_rows = out_0.rearrange("(p t) v -> p t v", t=PACK)
         groups = [slice(a * P, (a + 1) * P) for a in range(V // P)]
-
-        def add_turned(total, terms, d, cols):
-            nc.tensor.matmul(
-                total, lhsT=terms[:, d, cols], rhs=identity[:], is_transpose=True, start=(d == 0), stop=(d == NEIGHBOURS - 1)
-            )
 
         num = []
         for pair in range(PACK // PAIR):
@@ -204,19 +201,28 @@ def tile_picked_zrandla_relu_po_kernel(
                         nc.vector.tensor_copy(sums[0][:, i, :], fetched)
                     else:
                         nc.vector.tensor_tensor(sums[d][:, i, :], fetched, sums[d - 1][:, i, :], ALU.add)
-            num.append(sums[NEIGHBOURS - 1])
+            num.append(sums[last])
 
-        nc.scalar.activation(out=e_near[0][:, last, P:V], in_=score[0][:].indirect(near[last][:, P // LANES : V // LANES]), func=ACT.Copy)
-        first = [(t, d) for t in range(1, PACK) for d in range(NEIGHBOURS) if t == 2 or d < last]
-        for t, d in first + [(1, last), (3, last)]:
+        nc.scalar.activation(out=e_near[0][:, last, split:V], in_=score[0][:].indirect(entries(near[last], split, V)), func=ACT.Copy)
+        closing = [(PAIR * pair + 1, last) for pair in range(PACK // PAIR)]
+        opening = [(t, d) for t in range(1, PACK) for d in range(NEIGHBOURS) if (t, d) not in closing]
+        for t, d in opening + closing:
             nc.scalar.activation(out=e_near[t][:, d, :], in_=score[t][:].indirect(near[d][:]), func=ACT.Copy)
 
         den = [psum.tile([P, PAIR, len(groups), P], F32, name=f"den{pair}", tag=bank) for pair, bank in enumerate(("bank7", "bank4"))]
-        roots = []
         for t in range(PACK):
             for a, cols in enumerate(groups):
                 for d in range(NEIGHBOURS):
-                    add_turned(den[t // PAIR][:, t % PAIR, a, :], e_near[t], d, cols)
+                    nc.tensor.matmul(
+                        den[t // PAIR][:, t % PAIR, a, :],
+                        lhsT=e_near[t][:, d, cols],
+                        rhs=identity[:],
+                        is_transpose=True,
+                        start=(d == 0),
+                        stop=(d == last),
+                    )
+
+        roots = []
         for t in range(PACK):
             roots.append(keep.tile([P, len(groups), P], F32, name=f"root{t}", align_bytes=64))
             nc.scalar.activation(
@@ -231,13 +237,16 @@ def tile_picked_zrandla_relu_po_kernel(
                 nc.tensor.transpose(root_back[:, a, :], roots[t][:, a, :], identity[:])
             nc.scalar.activation(out=inv[t // PAIR][:, t % PAIR, :], in_=root_back[:].rearrange("p a v -> p (a v)"), func=ACT.Square)
 
-        nc.vector.tensor_tensor(result[:, 0:PAIR, :], num[0][:], inv[0][:], ALU.mult)
+        for i in range(PAIR):
+            nc.vector.tensor_tensor(result[:, i, :], num[0][:, i, :], inv[0][:, i, :], ALU.mult)
         nc.sync.dma_start(out=out_rows[:, 0:PAIR, :], in_=result[:, 0:PAIR, :])
         result_bf = keep.tile([P, V, PACK], BF16, name="result_bf", align_bytes=64)
         for cols in groups:
             nc.scalar.copy(out=result_bf[:, cols, 0:PAIR], in_=result[:, 0:PAIR, cols].rearrange("p t v -> p v t"))
+
+        nc.vector.tensor_tensor(result[:, PAIR, :], num[1][:, 0, :], inv[1][:, 0, :], ALU.mult)
         for cols in groups:
-            nc.vector.tensor_tensor(result[:, PAIR:PACK, cols], num[1][:, :, cols], inv[1][:, :, cols], ALU.mult)
+            nc.vector.tensor_tensor(result[:, PAIR + 1, cols], num[1][:, 1, cols], inv[1][:, 1, cols], ALU.mult)
         nc.sync.dma_start(out=out_rows[:, PAIR:PACK, :], in_=result[:, PAIR:PACK, :])
         for cols in groups:
             nc.vector.tensor_copy(out=result_bf[:, cols, PAIR:PACK], in_=result[:, PAIR:PACK, cols].rearrange("p t v -> p v t"))

@@ -47,6 +47,7 @@ def tile_picked_zrandla_relu_po_kernel(
         lists = ctx.enter_context(tc.tile_pool(name="lists", bufs=1))
         keep = ctx.enter_context(tc.tile_pool(name="keep", bufs=1))
         table = ctx.enter_context(tc.tile_pool(name="table", bufs=1))
+        early = ctx.enter_context(tc.tile_pool(name="early", bufs=1))
         psum = ctx.enter_context(tc.psum_pool(name="psum", bufs=1))
 
         picks = lists.tile([P, S // LANES], U16, name="picks")
@@ -73,9 +74,6 @@ def tile_picked_zrandla_relu_po_kernel(
         for tile, source in zip(near, (pos1, pos2, pos3)):
             nc.sync.dma_start(tile[:], source)
 
-        identity = keep.tile([P, P], F32, name="identity", align_bytes=64)
-        make_identity(nc, identity[:])
-
         for q in range(P // QUAD):
             rows = slice(QUAD * q, QUAD * q + PACK)
             nc.vector.tensor_copy(out=x_scale_table[rows, :].bitcast(I32), in_=x_scale_rows[rows, :].bitcast(I32))
@@ -86,16 +84,19 @@ def tile_picked_zrandla_relu_po_kernel(
         w1_scale = keep.tile([P, H], U8, name="w1_scale", align_bytes=64)
         w1_src = w1_rows[:].rearrange("p j (m t) -> p m j t", t=PACK)
         for pair, copy in enumerate((nc.scalar.copy, nc.vector.tensor_copy)):
-            w1_bf = keep.tile([P, PAIR, P, PACK], BF16, name=f"w1_bf{pair}", tag=f"w1_bf{pair}", align_bytes=64)
+            w1_bf = early.tile([P, PAIR, P, PACK], BF16, name=f"w1_bf{pair}", offset=3 * H * PAIR * pair, align_bytes=64)
             copy(out=w1_bf[:].rearrange("p t m j -> p m j t"), in_=w1_src[:, :, :, PAIR * pair : PAIR * (pair + 1)])
             cols = slice(PAIR * pair * P, PAIR * (pair + 1) * P)
             nc.vector.quantize_mx(
                 out=w1_code[:, cols].bitcast(FP8X4), scales=w1_scale[:, cols], in_=w1_bf[:].rearrange("p t m j -> p (t m j)")
             )
 
-        x_code = keep.tile([P, S], U32, name="x_code", tag="w1_bf0", align_bytes=64)
+        x_code = early.tile([P, S], U32, name="x_code", offset=2 * H, align_bytes=64)
         for start, stop in ((0, P), (P, 2 * P), (2 * P, S)):
             nc.vector.tensor_copy(x_code[:, start:stop], x_table[:].bitcast(U32).indirect(entries(picks, start, stop)))
+
+        identity = early.tile([P, P], F32, name="identity", offset=0, align_bytes=64)
+        make_identity(nc, identity[:])
 
         def deal_words(copy, rows, dealt):
             copy(out=dealt.rearrange("p (t m) -> p m t", t=PACK), in_=rows.rearrange("p (m t) -> p m t", t=PACK))
@@ -210,17 +211,19 @@ def tile_picked_zrandla_relu_po_kernel(
             nc.scalar.activation(out=e_near[t][:, d, :], in_=score[t][:].indirect(near[d][:]), func=ACT.Copy)
 
         den = [psum.tile([P, PAIR, len(groups), P], F32, name=f"den{pair}", tag=bank) for pair, bank in enumerate(("bank7", "bank4"))]
-        for t in range(PACK):
-            for a, cols in enumerate(groups):
-                for d in range(NEIGHBOURS):
-                    nc.tensor.matmul(
-                        den[t // PAIR][:, t % PAIR, a, :],
-                        lhsT=e_near[t][:, d, cols],
-                        rhs=identity[:],
-                        is_transpose=True,
-                        start=(d == 0),
-                        stop=(d == last),
-                    )
+        steps = [(a, d) for a in range(len(groups)) for d in range(NEIGHBOURS)]
+        whole = [(t, a, d) for t in range(0, PACK, PAIR) for a, d in steps]
+        ahead = [(t, a, d) for t, closing_d in closing for a, d in steps[:closing_d]]
+        behind = [(t, a, d) for t, closing_d in closing for a, d in steps[closing_d:]]
+        for t, a, d in whole + ahead + behind:
+            nc.tensor.matmul(
+                den[t // PAIR][:, t % PAIR, a, :],
+                lhsT=e_near[t][:, d, groups[a]],
+                rhs=identity[:],
+                is_transpose=True,
+                start=(d == 0),
+                stop=(d == last),
+            )
 
         roots = []
         for t in range(PACK):

@@ -68,9 +68,9 @@ def tile_picked_zrandla_relu_po_kernel(
         nc.sync.dma_start(out=w1_rows[:], in_=w1.rearrange("(p j) c -> p j c", j=PACK))
         nc.sync.dma_start(out=x_table[:], in_=words_of(x_words))
         nc.sync.dma_start(out=w2_rows[:], in_=words_of(w2_words))
-        load_scale_rows([nc.sync] * PACK, w_scale_rows, w2_scales, 0)
-        load_scale_rows([nc.gpsimd] * PACK, w_scale_rows, w3_scales, PACK)
         nc.sync.dma_start(out=w3_rows[:], in_=words_of(w3_words))
+        load_scale_rows([nc.sync] * PACK, w_scale_rows, w2_scales, 0)
+        load_scale_rows([nc.gpsimd, nc.gpsimd, nc.gpsimd, nc.sync], w_scale_rows, w3_scales, PACK)
         for tile, source in zip(near, (pos1, pos2, pos3)):
             nc.sync.dma_start(tile[:], source)
 

@@ -85,11 +85,25 @@ def tile_picked_zrandla_relu_po_kernel(
         w1_src = w1_rows[:].rearrange("p j (m t) -> p m j t", t=PACK)
         for pair, copy in enumerate((nc.scalar.copy, nc.vector.tensor_copy)):
             w1_bf = early.tile([P, PAIR, P, PACK], BF16, name=f"w1_bf{pair}", offset=3 * H * PAIR * pair, align_bytes=64)
-            copy(out=w1_bf[:].rearrange("p t m j -> p m j t"), in_=w1_src[:, :, :, PAIR * pair : PAIR * (pair + 1)])
-            cols = slice(PAIR * pair * P, PAIR * (pair + 1) * P)
-            nc.vector.quantize_mx(
-                out=w1_code[:, cols].bitcast(FP8X4), scales=w1_scale[:, cols], in_=w1_bf[:].rearrange("p t m j -> p (t m j)")
-            )
+            tiles = slice(PAIR * pair, PAIR * (pair + 1))
+            if pair == 0:
+                copy(out=w1_bf[:].rearrange("p t m j -> p m j t"), in_=w1_src[:, :, :, tiles])
+                cols = slice(0, PAIR * P)
+                nc.vector.quantize_mx(
+                    out=w1_code[:, cols].bitcast(FP8X4), scales=w1_scale[:, cols], in_=w1_bf[:].rearrange("p t m j -> p (t m j)")
+                )
+            else:
+                parts = [slice(0, P // 2), slice(P // 2, P)]
+                for part in parts:
+                    copy(out=w1_bf[:, :, part, :].rearrange("p t m j -> p m j t"), in_=w1_src[:, part, :, tiles])
+                for part in parts:
+                    for i in range(PAIR):
+                        cols = slice((PAIR + i) * P + part.start, (PAIR + i) * P + part.stop)
+                        nc.vector.quantize_mx(
+                            out=w1_code[:, cols].bitcast(FP8X4),
+                            scales=w1_scale[:, cols],
+                            in_=w1_bf[:, i, part, :].rearrange("p m j -> p (m j)"),
+                        )
 
         x_code = early.tile([P, S], U32, name="x_code", offset=2 * H, align_bytes=64)
         for start, stop in ((0, P), (P, 2 * P), (2 * P, S)):

from contextlib import ExitStack

import concourse.mybir as mybir
from concourse.masks import make_identity

K, T, S, V, H, N = 512, 2048, 512, 256, 512, 512
FLOPS = 2 * S * (K * H + 2 * H * N)

F32 = mybir.dt.float32
BF16 = mybir.dt.bfloat16
I32 = mybir.dt.int32
U32 = mybir.dt.uint32
U16 = mybir.dt.uint16
U8 = mybir.dt.uint8
FP8X4 = mybir.dt.float8_e4m3fn_x4
ACT = mybir.ActivationFunctionType
ALU = mybir.AluOpType

P = 128
PACK = 4
QUAD = 32
LANES = 16
NEIGHBOURS = 3
PAIR = 2
W3_OFFSET = 4 * N


def load_scale_rows(queues, tile, scales, first):
    for q, queue in enumerate(queues):
        row = QUAD * q + first
        queue.dma_start(out=tile[row : row + PACK, :].bitcast(I32), in_=scales[0, PACK * q : PACK * (q + 1), :].bitcast(I32))


def words_of(packed):
    return packed[0].rearrange("p c r -> p (c r)").bitcast(I32)


def entries(tile, start, stop):
    return tile[:, start // LANES : stop // LANES]


def tile_picked_zrandla_relu_po_kernel(
    tc, x_words, x_scales, w1, w2_words, w2_scales, w3_words, w3_scales, offs, pos1, pos2, pos3, out_0, out_1, out_2
):
    nc = tc.nc
    with ExitStack() as ctx:
        lists = ctx.enter_context(tc.tile_pool(name="lists", bufs=1))
        keep = ctx.enter_context(tc.tile_pool(name="keep", bufs=1))
        table = ctx.enter_context(tc.tile_pool(name="table", bufs=1))
        early = ctx.enter_context(tc.tile_pool(name="early", bufs=1))
        psum = ctx.enter_context(tc.psum_pool(name="psum", bufs=1))

        picks = lists.tile([P, S // LANES], U16, name="picks")
        near = [lists.tile([P, V // LANES], U16, name=f"near{d}") for d in range(NEIGHBOURS)]

        x_scale_table = keep.tile([P, T], U8, name="x_scale_table", align_bytes=64)
        w_scale_rows = keep.tile([P, N], U8, name="w_scale_rows", tag="h_scale", align_bytes=64)
        nc.vector.memset(x_scale_table[:].bitcast(I32), 0)
        nc.gpsimd.memset(w_scale_rows[:].bitcast(I32), 0)

        w1_rows = keep.tile([P, PACK, H], F32, name="w1_rows", align_bytes=64)
        x_table = table.tile([P, T], I32, name="x_table", offset=0, align_bytes=64)
        x_scale_rows = keep.tile([P, T], U8, name="x_scale_rows", align_bytes=64)
        w2_rows = keep.tile([P, N], I32, name="w2_rows", align_bytes=64)
        w3_rows = keep.tile([P, N], I32, name="w3_rows", tag="h_code", align_bytes=64)
        nc.sync.dma_start(picks[:], offs)
        load_scale_rows([nc.scalar, nc.scalar, nc.sync, nc.sync], x_scale_rows, x_scales, 0)
        nc.sync.dma_start(out=w1_rows[:], in_=w1.rearrange("(p j) c -> p j c", j=PACK))
        nc.sync.dma_start(out=x_table[:], in_=words_of(x_words))
        nc.sync.dma_start(out=w2_rows[:], in_=words_of(w2_words))
        nc.sync.dma_start(out=w3_rows[:], in_=words_of(w3_words))
        load_scale_rows([nc.sync] * PACK, w_scale_rows, w2_scales, 0)
        load_scale_rows([nc.gpsimd, nc.gpsimd, nc.gpsimd, nc.sync], w_scale_rows, w3_scales, PACK)
        for tile, source in zip(near, (pos1, pos2, pos3)):
            nc.sync.dma_start(tile[:], source)

        for q in range(P // QUAD):
            rows = slice(QUAD * q, QUAD * q + PACK)
            nc.vector.tensor_copy(out=x_scale_table[rows, :].bitcast(I32), in_=x_scale_rows[rows, :].bitcast(I32))
        x_scale = keep.tile([P, S], U8, name="x_scale", align_bytes=64)
        nc.vector.tensor_copy(x_scale[:], x_scale_table[:].indirect(picks[:]))

        w1_code = keep.tile([P, H], U32, name="w1_code", align_bytes=64)
        w1_scale = keep.tile([P, H], U8, name="w1_scale", align_bytes=64)
        w1_src = w1_rows[:].rearrange("p j (m t) -> p m j t", t=PACK)
        for pair, copy in enumerate((nc.scalar.copy, nc.vector.tensor_copy)):
            w1_bf = early.tile([P, PAIR, P, PACK], BF16, name=f"w1_bf{pair}", offset=3 * H * PAIR * pair, align_bytes=64)
            tiles = slice(PAIR * pair, PAIR * (pair + 1))
            if pair == 0:
                copy(out=w1_bf[:].rearrange("p t m j -> p m j t"), in_=w1_src[:, :, :, tiles])
                cols = slice(0, PAIR * P)
                nc.vector.quantize_mx(
                    out=w1_code[:, cols].bitcast(FP8X4), scales=w1_scale[:, cols], in_=w1_bf[:].rearrange("p t m j -> p (t m j)")
                )
            else:
                parts = [slice(0, P // 2), slice(P // 2, P)]
                for part in parts:
                    copy(out=w1_bf[:, :, part, :].rearrange("p t m j -> p m j t"), in_=w1_src[:, part, :, tiles])
                for part in parts:
                    for i in range(PAIR):
                        cols = slice((PAIR + i) * P + part.start, (PAIR + i) * P + part.stop)
                        nc.vector.quantize_mx(
                            out=w1_code[:, cols].bitcast(FP8X4),
                            scales=w1_scale[:, cols],
                            in_=w1_bf[:, i, part, :].rearrange("p m j -> p (m j)"),
                        )

        x_code = early.tile([P, S], U32, name="x_code", offset=2 * H, align_bytes=64)
        for start, stop in ((0, P), (P, 2 * P), (2 * P, S)):
            nc.vector.tensor_copy(x_code[:, start:stop], x_table[:].bitcast(U32).indirect(entries(picks, start, stop)))

        identity = early.tile([P, P], F32, name="identity", offset=0, align_bytes=64)
        make_identity(nc, identity[:])

        def deal_words(copy, rows, dealt):
            copy(out=dealt.rearrange("p (t m) -> p m t", t=PACK), in_=rows.rearrange("p (m t) -> p m t", t=PACK))

        w2_code = keep.tile([P, N], U32, name="w2_code", align_bytes=64)
        deal_words(nc.scalar.copy, w2_rows[:].bitcast(U32), w2_code[:])
        w_scale = table.tile([P, N], U8, name="w_scale", offset=0, align_bytes=64)
        nc.vector.tensor_copy(
            out=w_scale[:].rearrange("p (t m) -> p t m", t=PACK), in_=w_scale_rows[:].rearrange("p (m t) -> p t m", t=PACK)
        )
        w2_scale = w_scale[:]
        w3_scale = w_scale[PACK:P, :]
        w3_code = table.tile([P, N], I32, name="w3_code", offset=W3_OFFSET, align_bytes=64)
        deal_words(nc.vector.tensor_copy, w3_rows[:], w3_code[:])

        h_code = keep.tile([P, S], U32, name="h_code", tag="h_code", align_bytes=64)
        h_scale = keep.tile([P, S], U8, name="h_scale", tag="h_scale", align_bytes=64)
        quarters = [slice(q * P, (q + 1) * P) for q in range(S // P)]
        for q, cols in enumerate(quarters):
            h_sum = psum.tile([P, PACK, P], F32, name=f"h_sum{q}", tag=f"bank{q}")
            for t in range(PACK):
                w_cols = slice(t * P, (t + 1) * P)
                nc.tensor.matmul_mx(
                    out=h_sum[:, t, :],
                    lhsT=w1_code[:, w_cols].bitcast(FP8X4),
                    lhsT_scale=w1_scale[:, w_cols],
                    rhs=x_code[:, cols].bitcast(FP8X4),
                    rhs_scale=x_scale[:, cols],
                    start=True,
                    stop=True,
                )
            on_vector = q == len(quarters) - 1
            h_bf = keep.tile([P, P, PACK], BF16, name=f"h_bf{q}", tag=f"h_bf{1 if on_vector else q}", align_bytes=64)
            if on_vector:
                nc.vector.tensor_scalar_max(out=h_bf[:], in0=h_sum[:].rearrange("p t n -> p n t"), scalar1=0.0)
            else:
                nc.scalar.activation(out=h_bf[:], in_=h_sum[:].rearrange("p t n -> p n t"), func=ACT.Relu)
            nc.vector.quantize_mx(out=h_code[:, cols].bitcast(FP8X4), scales=h_scale[:, cols], in_=h_bf[:].rearrange("p n t -> p (n t)"))

        def product(total, code, scale, t, cols):
            w_cols = slice(t * P, (t + 1) * P)
            nc.tensor.matmul_mx(
                out=total,
                lhsT=code[:, w_cols].bitcast(FP8X4),
                lhsT_scale=scale[:, w_cols],
                rhs=h_code[:, cols].bitcast(FP8X4),
                rhs_scale=h_scale[:, cols],
                start=True,
                stop=True,
            )

        score = [keep.tile([P, S], F32, name=f"score{t}", align_bytes=64) for t in range(PACK)]
        weighted = [keep.tile([P, S], F32, name=f"weighted{t}", align_bytes=64) for t in range(PACK)]
        halves = [slice(a * S // 2, (a + 1) * S // 2) for a in range(2)]
        s_sum = [psum.tile([P, S], F32, name=f"s_sum{t}", tag=f"bank{PACK + t}") for t in range(PACK)]

        def make_scores(total, t, cols):
            product(total, w2_code, w2_scale, t, cols)
            nc.scalar.activation(out=score[t][:, cols], in_=total, func=ACT.Exp)

        make_scores(s_sum[0][:, halves[0]], 0, halves[0])
        make_scores(s_sum[0][:, quarters[2]], 0, quarters[2])
        s_last = psum.tile([P, P], F32, name="s_last", tag="bank3")
        make_scores(s_last[:], 0, quarters[3])
        for cols in halves:
            for t in range(1, PACK):
                make_scores(s_sum[t][:, cols], t, cols)

        e_near = [keep.tile([P, NEIGHBOURS, V], F32, name=f"e_near{t}", tag=f"e_near{t}", align_bytes=64) for t in range(PACK)]
        last = NEIGHBOURS - 1
        split = V // 2
        for d in range(last):
            nc.vector.tensor_copy(e_near[0][:, d, :], score[0][:].indirect(near[d][:]))
        nc.vector.tensor_copy(e_near[0][:, last, 0:split], score[0][:].indirect(entries(near[last], 0, split)))

        y_sum = [psum.tile([P, S], F32, name=f"y_sum{t}", tag=f"bank{t}") for t in range(PACK)]

        def weigh(t, cols):
            nc.vector.tensor_tensor(weighted[t][:, cols], y_sum[t][:, cols], score[t][:, cols], ALU.mult)

        halved = range(PACK - 1)
        for t in halved:
            product(y_sum[t][:, halves[0]], w3_code, w3_scale, t, halves[0])
            weigh(t, halves[0])
        rest = [halves[1] if t in halved else slice(0, S) for t in range(PACK)]
        for t in range(PACK):
            product(y_sum[t][:, rest[t]], w3_code, w3_scale, t, rest[t])

        result = keep.tile([P, PACK, V], F32, name="result", align_bytes=64)
        out_rows = out_0.rearrange("(p t) v -> p t v", t=PACK)
        groups = [slice(a * P, (a + 1) * P) for a in range(V // P)]

        num = []
        for pair in range(PACK // PAIR):
            tiles = range(PAIR * pair, PAIR * (pair + 1))
            for t in tiles:
                weigh(t, rest[t])
            sums = [keep.tile([P, PAIR, V], F32, name=f"sums{pair}_{d}", align_bytes=64) for d in range(NEIGHBOURS)]
            for d in range(NEIGHBOURS):
                for i, t in enumerate(tiles):
                    fetched = weighted[t][:].indirect(near[d][:])
                    if d == 0:
                        nc.vector.tensor_copy(sums[0][:, i, :], fetched)
                    else:
                        nc.vector.tensor_tensor(sums[d][:, i, :], fetched, sums[d - 1][:, i, :], ALU.add)
            num.append(sums[last])

        nc.scalar.activation(out=e_near[0][:, last, split:V], in_=score[0][:].indirect(entries(near[last], split, V)), func=ACT.Copy)
        closing = [(PAIR * pair + 1, last) for pair in range(PACK // PAIR)]
        opening = [(t, d) for t in range(1, PACK) for d in range(NEIGHBOURS) if (t, d) not in closing]
        for t, d in opening + closing:
            nc.scalar.activation(out=e_near[t][:, d, :], in_=score[t][:].indirect(near[d][:]), func=ACT.Copy)

        den = [psum.tile([P, PAIR, len(groups), P], F32, name=f"den{pair}", tag=bank) for pair, bank in enumerate(("bank7", "bank4"))]
        steps = [(a, d) for a in range(len(groups)) for d in range(NEIGHBOURS)]
        whole = [(t, a, d) for t in range(0, PACK, PAIR) for a, d in steps]
        ahead = [(t, a, d) for t, closing_d in closing for a, d in steps[:closing_d]]
        behind = [(t, a, d) for t, closing_d in closing for a, d in steps[closing_d:]]
        for t, a, d in whole + ahead + behind:
            nc.tensor.matmul(
                den[t // PAIR][:, t % PAIR, a, :],
                lhsT=e_near[t][:, d, groups[a]],
                rhs=identity[:],
                is_transpose=True,
                start=(d == 0),
                stop=(d == last),
            )

        roots = []
        for t in range(PACK):
            roots.append(keep.tile([P, len(groups), P], F32, name=f"root{t}", align_bytes=64))
            nc.scalar.activation(
                out=roots[t][:].rearrange("p a v -> p (a v)"),
                in_=den[t // PAIR][:, t % PAIR, :, :].rearrange("p a v -> p (a v)"),
                func=ACT.Abs_reciprocal_sqrt,
            )
        inv = [keep.tile([P, PAIR, V], F32, name=f"inv{pair}", align_bytes=64) for pair in range(PACK // PAIR)]
        for t, back_bank in enumerate(("bank5", "bank6", "bank0", "bank1")):
            root_back = psum.tile([P, len(groups), P], F32, name=f"root_back{t}", tag=back_bank)
            for a in range(len(groups)):
                nc.tensor.transpose(root_back[:, a, :], roots[t][:, a, :], identity[:])
            nc.scalar.activation(out=inv[t // PAIR][:, t % PAIR, :], in_=root_back[:].rearrange("p a v -> p (a v)"), func=ACT.Square)

        for i in range(PAIR):
            nc.vector.tensor_tensor(result[:, i, :], num[0][:, i, :], inv[0][:, i, :], ALU.mult)
        nc.sync.dma_start(out=out_rows[:, 0:PAIR, :], in_=result[:, 0:PAIR, :])
        result_bf = keep.tile([P, V, PACK], BF16, name="result_bf", align_bytes=64)
        for cols in groups:
            nc.scalar.copy(out=result_bf[:, cols, 0:PAIR], in_=result[:, 0:PAIR, cols].rearrange("p t v -> p v t"))

        nc.vector.tensor_tensor(result[:, PAIR, :], num[1][:, 0, :], inv[1][:, 0, :], ALU.mult)
        for cols in groups:
            nc.vector.tensor_tensor(result[:, PAIR + 1, cols], num[1][:, 1, cols], inv[1][:, 1, cols], ALU.mult)
        nc.sync.dma_start(out=out_rows[:, PAIR:PACK, :], in_=result[:, PAIR:PACK, :])
        for cols in groups:
            nc.vector.tensor_copy(out=result_bf[:, cols, PAIR:PACK], in_=result[:, PAIR:PACK, cols].rearrange("p t v -> p v t"))
        out_code = keep.tile([P, V], U32, name="out_code", align_bytes=64)
        out_scale = keep.tile([P, V], U8, name="out_scale", align_bytes=64)
        for cols in groups:
            nc.vector.quantize_mx(
                out=out_code[:, cols].bitcast(FP8X4), scales=out_scale[:, cols], in_=result_bf[:, cols, :].rearrange("p v t -> p (v t)")
            )
        nc.sync.dma_start(out=words_of(out_1), in_=out_code[:].bitcast(I32))
        for q in range(P // QUAD):
            queue = nc.sync if q % 2 else nc.scalar
            queue.dma_start(
                out=out_2[0, PACK * q : PACK * (q + 1), :].bitcast(I32), in_=out_scale[QUAD * q : QUAD * q + PACK, :].bitcast(I32)
            )
